import numpy as np, ml_dtypes
CORES = [5,29,101,125,133,157,229,253]
N = 8
BF = ml_dtypes.bfloat16
def gentries(a):
    return np.ascontiguousarray(a.reshape(8, 16, -1).transpose(0, 2, 1)).reshape(8, -1)
def gtable(e):
    e = np.asarray(e); return np.ascontiguousarray(e.reshape(8, -1, 16).transpose(0, 2, 1)).reshape(128, -1).astype(np.int32)
M, D, B, RO, Q = 128, 1024, 256, 5, 7
NV = 16 * M
def parts(rng):
    v = rng.integers(0, 256, (N, 8, 16, NV)); a = rng.integers(0, NV, (N, 8, 16, D)); l = rng.integers(0, NV, (N, 8, 16, B))
    z = rng.integers(0, 256, (N, 8, 16, M)); c = rng.integers(0, B, (N, 8, M)); ka = rng.integers(0, 4096, (N, 8, 16))
    th = rng.integers(1150, 1450, (N, 8, 1)) + rng.integers(-150, 151, (N, 8, 16))
    return v, a, l, z, c, ka, th
def pack(v, a, l, z, c, ka, th):
    return {"vf": np.ascontiguousarray(v.reshape(N, 128, NV)).astype(np.float32).astype(BF), "ad": np.ascontiguousarray(a.reshape(N, 128, D)).astype(np.int32),
            "le": np.ascontiguousarray(l.reshape(N, 128, B)).astype(np.int32), "z0": np.ascontiguousarray(z.reshape(N, 128, M)).astype(np.float32).astype(BF),
            "cb": np.stack([gtable(x) for x in c]), "ka": ka.reshape(N, 128, 1).astype(np.int32), "th": th.reshape(N, 128, 1).astype(np.int32)}
def setup_inputs(rng):
    return pack(*parts(rng))
def setup_inputs_spread(rng):
    def uneven(n, *shape):
        v = np.minimum((n * rng.random((N, 8) + shape) ** 3).astype(np.int64), n - 1)
        up = (np.arange(8) % 2 == 1).reshape((1, 8) + (1,) * len(shape))
        return np.where(up, n - 1 - v, v)
    def sizes(n):
        return np.minimum((np.exp2(8.5 * rng.random((N, 8, 1, n))) * rng.random((N, 8, 16, n))).astype(np.int64), 255)
    th = np.minimum((4081 * rng.random((N, 8, 16)) ** 2.5).astype(np.int64), 4080)
    return pack(sizes(NV), uneven(NV, 16, D), uneven(NV, 16, B), sizes(M), uneven(B, M), uneven(4096, 16), th)
def setup_inputs_ends(rng):
    def halves(n):
        e = rng.random((N, 8, 16, n)) < 0.5; a = rng.random((N, 8, 1, n)) < 0.5
        return np.where(rng.random((N, 8, 1, n)) < 0.5, a, e).astype(np.int64)
    def coin(*shape):
        return (rng.random((N, 8) + shape) < 0.5).astype(np.int64)
    v = 255 * halves(NV); v[:, 1::2, :, 0] = 0; v[:, 1::2, :, NV - 1] = 255; v[:, 0, :, 0] = 255; v[:, 0, :, NV - 1] = 0
    top = np.zeros(16, np.int64); top[np.array([0, 1, 2, 6, 9])] = 255
    z = np.where(rng.random((N, 8, 1, M)) < 0.15, top[:, None], 255 * halves(M)); z[..., M - 1] = top; z[..., M - 2] = 255; z[..., 0] = 0
    c = (B - 1) * coin(M); c[..., M - 1] = B - 1; c[..., 0] = 0
    l = (NV - 1) * coin(16, B); l[:, :, 15, B - 1] = NV - 1; l[:, :, 0, 0] = 0
    a = (NV - 1) * coin(16, D); a[:, 7, 15] = 0
    ka = 4095 * coin(16); ka[:, 0, 0] = 0; ka[:, 7, 15] = 4095
    th = 4080 * (rng.random((N, 8, 16)) < rng.choice(np.array([0.1, 0.3, 0.6]), (N, 8, 1))).astype(np.int64); th[:, 0, 0] = 0; th[:, 7, 15] = 4080
    return pack(v, a, l, z, c, ka, th)
def setup_inputs_corners(rng):
    v, a, l, z, c, ka, th = parts(rng); h = NV // 2; late = int(rng.integers(0, 7)); last = int(rng.integers(0, 8))
    for r in range(N):
        kinds = rng.permutation(np.array([1, 2, 3, 4, 5, 7])).tolist(); kinds.insert(late, 0); kinds.insert(last, 6)
        for g, kind in enumerate(kinds):
            if kind < 5:
                n = (0, int(rng.choice(np.array([1, 15]))), Q - 1, Q, 16)[kind]
                if kind == 0 or (kind + r) % 2 == 0:
                    d = rng.integers(129, 250, 16); odd = r & 1 if kind == 0 else 1 if kind == 4 else int(rng.integers(0, 2))
                    d[0] -= (int(np.add.reduce(d)) - odd) & 3
                else:
                    d = rng.integers(3, 120, 16)
                p = rng.integers(0, 256 - d); e = int(np.add.reduce(d))
                v[r, g, :, :h] = p[:, None]; v[r, g, :, h:] = (p + d)[:, None]
                l[r, g] = np.where(rng.random((16, B)) < 0.5, rng.integers(0, h, (16, B)), rng.choice(np.array([0, h - 1]), (16, B)))
                a[r, g] = np.where(rng.random((16, D)) < 0.5, rng.integers(h, NV, (16, D)), rng.choice(np.array([h, NV - 1]), (16, D)))
                t = rng.choice(np.array([e - 1, e - 32, e - 33]), 16); o = rng.permutation(16); t[o[:n]] = e
                if kind == 0:
                    t[o[Q - 1:]] = e - 32 * (RO - 1) - rng.integers(0, 2, 17 - Q); c[r, g] = int(rng.integers(0, B))
                th[r, g] = t
            elif kind == 5:
                o = rng.permutation(B)[:M]; c[r, g] = o
                l[r, g][:, o] = 16 * np.arange(M)[None, :] + np.arange(16)[:, None]
                a[r, g] = rng.choice(np.array([0, NV - 1]), (16, D))
            elif kind == 6:
                j = np.arange(NV) & 15; v[r, g] = np.where((j > 0) & (j < 8), 0, np.maximum(v[r, g], 1))
                l[r, g] = 16 * rng.integers(0, M, (16, B)) + rng.integers(1, 8, (16, B))
                a[r, g] = 16 * rng.integers(0, M, (16, D)) + rng.integers(1, 8, (16, D)); a[r, g, 15] = 16 * rng.integers(0, M, D) + rng.integers(8, 16, D)
                x = rng.integers(0, 255, (16, M)); y = (32 - np.add.reduce(x[2:] * (14 * np.arange(2, 16) + 1)[:, None], axis=0)) & 4095
                over = (y > 4080).astype(np.int64); x[2] += over; y = y - 29 * over
                x[1] = np.minimum(y // 15, 255); x[0] = y - 15 * x[1]; z[r, g] = x
                b = (1103 * 32 >> 4) & (B - 1); c[r, g] = b; th[r, g] = 0
                ka[r, g, 15] = ((D - 1 - 37 * 32 - 613 * b) & (D - 1)) + D * int(rng.integers(0, 4096 // D))
            else:
                th[r, g] = 4080 * (r & 1)
    return pack(v, a, l, z, c, ka, th)
def setup_inputs_crowd(rng):
    v, a, l, z, c, ka, th = parts(rng); o = rng.permutation(8).tolist(); q = np.arange(N)
    x = rng.choice(np.array([0, M // 2, M - 1]), N)
    c[:, o[0]] = rng.integers(0, B, (N, 1))
    c[:, o[1]] = rng.integers(0, B, (N, 1)); c[q, o[1], x] = (c[q, o[1], x] + 1) % B
    for g in (o[2], o[3], o[7]):
        z[:, g] = rng.integers(0, 256, (16, 1)); c[:, g] = int(rng.integers(0, B))
    z[q, o[3], :, x] = rng.integers(0, 256, (N, 16))
    two = rng.integers(0, 256, (2, 16)); z[:, o[4]] = two[rng.integers(0, 2, (N, M))].transpose(0, 2, 1); c[:, o[4]] = rng.choice(rng.integers(0, B, 2), (N, M))
    z[:, o[5]] = rng.integers(0, 256, (16, 1))
    z[:, o[6]] = 0; ka[:, o[6]] = 0
    n = int(rng.integers(0, NV)); l[:, o[7]] = n; a[:, o[7]] = (n + int(rng.integers(1, NV))) % NV
    return pack(v, a, l, z, c, ka, th)
def check_inputs(d):
    bad = []
    for k, lo, hi in (("vf", 0, 255), ("ad", 0, NV - 1), ("le", 0, NV - 1), ("z0", 0, 255), ("cb", 0, B - 1), ("ka", 0, 4095), ("th", 0, 4080)):
        x = np.asarray(d[k]); x = x.astype(np.float32) if k in ("vf", "z0") else x
        if not (np.min(x) >= lo and np.max(x) <= hi): bad.append("range of " + k)
        elif k in ("vf", "z0") and np.any(x != np.floor(x)): bad.append("whole numbers in " + k)
    return bad
def hashed(z):
    return np.add.reduce(z * (14 * np.arange(16) + 1)[:, None], axis=2) & 4095
def values(v, x):
    return np.take_along_axis(v, x.reshape(N, 8, 1, 16 * M), 3).reshape(N, 8, 16, 16, M)
def first(x):
    return np.argmax(x[:, :, :, None] == x[:, :, None, :], axis=3) == np.arange(M)
def reference(vf, ad, le, z0, cb, ka, th):
    v = vf.astype(np.float32).astype(np.int32).reshape(N, 8, 16, NV); dirs = ad.astype(np.int64).reshape(N, 8, 16, D); blk = le.astype(np.int64).reshape(N, 8, 16, B)
    z = z0.astype(np.float32).astype(np.int64).reshape(N, 8, 16, M); c = np.stack([gentries(x) for x in cb]).astype(np.int64)
    kap = ka.astype(np.int64).reshape(N, 8, 16, 1); lim = th.astype(np.int64).reshape(N, 8, 16, 1)
    count = np.zeros((N, 8, M), np.int64); u = hashed(z)
    for m in range(1, RO + 1):
        names = np.take_along_axis(blk, c[:, :, None, :], 3)
        a = ((u[:, :, None, :] * kap >> 5) + (37 * u + 613 * c)[:, :, None, :]) & (D - 1)
        n = np.take_along_axis(dirs, a, 3)
        s = values(v, names); y = values(v, n)
        e = np.add.reduce(np.abs(s - y), axis=2)
        ok = e <= lim + 32 * count[:, :, None, :]
        names = np.where(ok, names, n)
        squash = np.add.reduce(ok.astype(np.int64), axis=2) < Q
        hi = np.where(squash[:, :, None, :], np.maximum.reduce(y, axis=3), np.maximum.reduce(np.where(ok[:, :, None], s, -1), axis=3))
        lo = np.where(squash[:, :, None, :], np.minimum.reduce(y, axis=3), np.minimum.reduce(np.where(ok[:, :, None], s, 256), axis=3))
        z = np.abs(z - ((hi.astype(np.int64) + lo) >> 1)); u = hashed(z)
        new = 16 * np.arange(M) + (u & 15)
        np.put_along_axis(v, new[:, :, None, :], z.astype(np.int32), 3)
        r, g, t = np.nonzero(first(c)); blk[r, g, :, c[r, g, t]] = names[r, g, :, t]
        if m == RO: break
        k = np.argmax(e, axis=2)
        col = np.take_along_axis(a, k[:, :, None, :], 2)[:, :, 0]
        r, g, t = np.nonzero(first(col)); dirs[r, g, k[r, g, t], col[r, g, t]] = new[r, g, t]
        count = count + squash; c = (1103 * u >> 4) & (B - 1)
        src = (np.arange(N)[:, None] - np.arange(M) // (M // N) - m) % N
        z = np.take_along_axis(z, src[:, None, None, :], 0); u = np.take_along_axis(u, src[:, None, :], 0)
        c = np.take_along_axis(c, src[:, None, :], 0); count = np.take_along_axis(count, src[:, None, :], 0)
    return {"yv": v.reshape(N, 128, NV).astype(np.float32).astype(BF), "yl": blk.reshape(N, 128, B).astype(np.float32), "yz": z.reshape(N, 128, M).astype(np.float32).astype(BF)}

@@ -1,0 +1,619 @@
+from concourse.bass import DstId, RemoteDMATransfer
+from concourse.mybir import AluOpType, ActivationFunctionType
+
+F32, BF, F16, I32, U16 = "float32", "bfloat16", "float16", "int32", "uint16"
+STEPS, NR, HALF, FLD = 5, 8, 64, 5
+BLK = 16 * FLD
+CS = 19616.0
+BIG = float(2 ** 25)
+MAGIC = 12582912.0
+TRI = 576
+
+_S = {
+    "W": (BF, 4096), "ADI": (I32, 1024), "LEI": (I32, 256), "AD": (F32, 1152), "LE": (F32, 384),
+    "G": (F16, 2048), "D": (BF, 2048), "DA": (BF, 2048), "FV": (BF, 2048), "MX": (BF, 2048), "MN": (BF, 2048),
+    "SELN": (BF, 2048), "SELE": (BF, 2048),
+    "ML": (F32, 5 * 8 * BLK), "MS": (F32, 4 * 8 * BLK),
+    "CBI": (I32, 8), "KAI": (I32, 8), "THI": (I32, 8), "CF": (F32, 8), "COL": (F32, 16), "COLI": (I32, 16),
+    "JM": (F32, 128), "JG": (F32, 128), "TMP": (F32, 8), "IOT": (I32, 8), "IOF": (F32, 16), "MK": (F32, 16),
+    "ID": (BF, 128), "BO": (BF, 128), "BOH": (F16, 128), "TR": (BF, 128), "WK": (BF, 128), "WU": (BF, 128),
+    "NEG": (BF, 128), "DK": (BF, 128), "MH": (BF, 128), "BM": (BF, 64), "M1": (BF, 128), "QC": (BF, 64),
+    "M32": (BF, 128), "CE": (BF, 128), "CE2": (BF, 128),
+    "BASE": (BF, 144), "KEEP": (BF, 512), "RST": (BF, 512), "CMP": (F32, 128), "T16": (F32, 128), "DUMP": (F32, 16),
+    "RD": (BF, 2 * TRI), "DD": (BF, 2 * TRI), "RR": (BF, 2 * TRI),
+    "LB": (U16, 8), "LC": (U16, 8), "LP": (U16, 8),
+    "C16": (U16, 16), "S16": (U16, 256), "A16": (U16, 256), "N16": (U16, 128), "F16": (U16, 128), "W16": (U16, 8),
+    "O16": (U16, 16),
+    "PI": (I32, 128), "AI": (I32, 256), "AB": (BF, 256), "ZB": (BF, 256), "NF": (F32, 128),
+    "OK": (BF, 128), "FL": (BF, 256), "X1": (F32, 128), "X2": (F32, 128), "ZR": (F32, 128), "Z16": (BF, 128),
+    "XS": (F32, 128), "Y": (I32, 144), "YU": (I32, 144), "YM": (I32, 144), "YC": (I32, 144), "YL": (I32, 144),
+    "WF": (F32, 144),
+    "KEY": (F32, 128), "KT": (F32, 128), "KS": (F32, 128), "IT": (F32, 128), "NI": (F32, 128),
+    "IA": (F16, 128), "AL": (F32, 128), "XD": (F32, 48), "YD": (F32, 16), "ZD": (F32, 16),
+    "SN": (F32, 128), "SO": (F32, 128), "T1": (F32, 128), "T2": (F32, 128),
+}
+PS = ["PN0", "PN1", "PE0", "PE1", "PF0", "PF1", "PU0", "PU1"]
+SCRATCH = {}
+for _n in _S:
+    SCRATCH[_n] = ("sbuf", [128, _S[_n][1]], _S[_n][0])
+for _n in PS:
+    SCRATCH[_n] = ("psum", [128, 512], F32)
+
+LOADS = ["z0", "cb", "ka", "le", "th", "ad", "vf"]
+STORES = ["yv0", "yv1", "yl", "yz"]
+SEMAPHORES = ["cv", "ca", "cp", "cg", "sent"] + ["ld_" + x for x in LOADS] + ["st_" + x for x in STORES] + \
+    ["arr%d_%d" % (m, h) for m in range(1, STEPS) for h in range(2)]
+CNT = {"v": "cv", "a": "ca", "p": "cp", "g": "cg"}
+
+ENG = "aaaaaaaavaavvavaaaaavaavvavaavaavaavaaaavaaavaavaavaaaaa"
+ORDER = "0102071k03051e000608040c0b0M090d0a1l0e0n180o0j0g0q0t1q0h0p1g0P0S0N0f1a1p0x0m1h0J0l0s0I1s150E1P1S140A1Q160D1R0y0w1V1T2F0K1W0R220F1X1U2G2H23241f0Q250Y2I0H262J0L1i270G2K2c120B2e2d0u0z0Z0v130C2S2Q2g1w2f2P2h0U172T0V2l0O112R1B2j1A0W1C0X1D100T1z2m1y1x2U1j1E2W192k1G1m2N2n1b2Y2L1n2i2X1F1H282o1N2Z2q1I2r2s3n2O2t1J2u1L2a302M2v2b1r292w2V0i2p2x1t1M2z311K3334350k3s362C371u383t391v3a2B2A1c3f2D2E3o3K3i323L3g3M3c3h3O463P3R3Q3j3X472y3Z3N3Y401Z3S1Y411o420r3e433b213d201d3p4o3u3k3T4p1O4q4K4r3v4s3l3w4t3x3y4v4u3U4B3z4D3A4C3B4E3m3C4F3D4G484H4I4w494x4a3E4b4c4y3F3V4d3G3r4e4g5r4f4J4h3H4i3I4j3J443q4k454l4z4m3W4n4A4P4M4Q4U4N4W4R4V4T4S4L4O4Y4X4Z50515u5w525B5x5D5v5A5y5H5z545F5E5G565I555J5L575C58535N5M5t5K5s59685O5b5c5d6d5a5e5f695P5g6a5h6b5i6c5l5o5j5Q5k5m5R5S5T5q5n5p6f6A6e6i6h6B6C5U6D6E6j6g5V5W6F606H6G5X616N5Y6P5Z6Q656O6R6S6k6T6W6l6X6m6I6Y6o626J6p667A676Z6r636t6q6s646n716K707e6V727f6u6U7g7h7i6v737j777l7k766w7r747m757t7s7u6L7v7w7n787x7y6x7o6y796z7a6M8h7z7b7p7c7d7q7D7F7C7G7B7E7M7L7H7K7J7I7N7O7Q7P7R7S7T7U7W7V8m8j8i8n8k7X8o8l8p8u8v7Y8x8w8y7Z8z8081828A8D8r8q8t8s8B8E838C93848598898699878a8F888b8e8G8g8H8I8J8K8c8L8M8Q8N9M8O8R9N8P8d8V8f9a9q9b9c9r8X9e9s8S8W9u9v9x9w9f9D9y9t9F9h9E9G9i9z9g9I9j9H9d8T9J8U94a4958Ya5a69Oaqa79Ba89P8Z9Ra9abaa9Qah9S9Aajaiak9Tal9Wam9k9Vao909l9X919U9m96an9nac9o9Y9pb79Zada09Ka1aea29Cafa392ag97ap9LatavasawazauaAaCaxaFayaGaEaDaBaraHbabcb9bdbhbjbebgbfb8bbblaIaKbkaMbnbobmaLbpbtaNaJaObqbrbubiaPbTbsaRbVaSaTbUaQaUaVbvaWbYaXbZaYbOb1c0aZbwc1bybWbzbPbAb4b3bBbCbGb2bDc2bEb0bQbxbFb5c4bLb6cCc5cgcDbRcEchbMcibIbNckclcncmbSctcFcjcvc7cucwc9cGc8cyc6cxbHbJc3czcIcHbKcacUcocbcpcccVcqcdcWcJdgcXcecrcYcMcfcKcLcZd1cNd0d7d2d9d8dad3dcdbbXddded4cBcOcAdUdfcPd5cQcscRcScTd6djdldqdkdidrdmdvdndodtdudwe3dxdsdpdhdXdZdWe0e4dYe6e1dyeae2e7e8dAe9ebdCdBecegdDdzdEedeeehe5dVdFeDefdGeFdHdIeEdJdKeidLdMdNeydOezejeAekeGeleBemdReCeneoepeqereHevdTdQdPesdSexeIeweJeteKeueLeMeTeNeOeUePeVeQeWf4eReXf5eYeZf0f1f2eSf6f3"
+DIGITS = "0123456789abcdefghijklmnopqrstuvwxyzABCDEFGHIJKLMNOPQRSTUVWXYZ"
+
+
+def ap(n, a, b, s=1):
+    return (n, a, b, s, None)
+
+
+def ind(win, off):
+    return (win[0], win[1], win[2], 1, off)
+
+
+def cnt(x):
+    if x[4] is not None:
+        return 16 * (x[4][2] - x[4][1])
+    return len(range(x[1], x[2], x[3]))
+
+
+def bits(x):
+    n = len(range(x[1], x[2], x[3]))
+    return (((1 << (n * x[3])) - 1) // ((1 << x[3]) - 1)) << x[1]
+
+
+def build_ops():
+    ops = []
+    cur = ["-"]
+    seen = {}
+    flex = [0]
+    A = AluOpType
+    AF = ActivationFunctionType
+
+    def add(e, kind, args, r, w, sem=None):
+        rr = []
+        for x in r:
+            if isinstance(x, tuple):
+                rr.append(x)
+                if x[4] is not None:
+                    rr.append(x[4])
+        for x in w:
+            if x[4] is not None:
+                rr.append(x[4])
+        tag = cur[0] + (w[0][0] if w else kind)
+        seen[tag] = seen.get(tag, 0) + 1
+        ops.append({"tag": tag + str(seen[tag]), "e": e, "k": kind, "a": args, "r": rr, "w": w, "sem": sem})
+
+    def copy(out, x):
+        add("v", "copy", (out, x), [x], [out])
+
+    def tt(out, x, y, op):
+        add("v", "tt", (out, x, y, op), [x, y], [out])
+
+    def ts(out, x, s1, op0, s2=None, op1=None):
+        add("v", "ts", (out, x, s1, s2, op0, op1), [x, s1, s2], [out])
+
+    def scan(out, d0, d1, op0, op1):
+        add("v", "scan", (out, d0, d1, 0.0, op0, op1), [d0, d1], [out])
+
+    def transp(out, x):
+        add("v", "tr", (out, x), [x], [out])
+
+    def memset(out, val):
+        add("v", "memset", (out, val), [], [out])
+
+    def act(out, x, func, bias=None, scale=None):
+        add("a", "act", (out, x, func, bias, scale), [x, bias, scale], [out])
+
+    def mm(groups, first=True, final=True):
+        lst, r, w = [], [], []
+        for out, terms in groups:
+            w.append(out)
+            for i, (l, x) in enumerate(terms):
+                lst.append((out, l, x, first and i == 0, final and i == len(terms) - 1))
+                r += [l, x]
+        add("p", "mm", lst, r, w)
+
+    def iota(out, pattern, base, cm):
+        add("g", "iota", (out, pattern, base, cm), [], [out])
+
+    def asel(out, x, op, fill):
+        add("g", "asel", (out, x, op, fill), [x], [out])
+
+    def gather(out, x):
+        e = ENG[flex[0]]
+        flex[0] += 1
+        if e == "v":
+            copy(out, x)
+        else:
+            act(out, x, AF.Copy)
+
+    def col(j):
+        return ap("COL", j, j + 1)
+
+    def full(n):
+        return ap(n, 0, 128)
+
+    def hs(n, h, o=0):
+        return ap(n, o + HALF * h, o + HALF * h + HALF)
+
+    def fld(buf, m, h, f):
+        a = m * 8 * BLK + h * 4 * BLK
+        return ap(buf, a + f, a + 4 * BLK, FLD)
+
+    def lst(buf, m, b0, b1):
+        return ap(buf, m * 8 * BLK + b0 * BLK + 4, m * 8 * BLK + b1 * BLK, BLK)
+
+    def blk(buf, m, b):
+        return ap(buf, m * 8 * BLK + b * BLK, m * 8 * BLK + b * BLK + BLK)
+
+    z1 = 128
+    for e, name, out in (("s", "z0", ap("ZB", z1, z1 + 128)), ("s", "cb", ap("CBI", 0, 8)), ("a", "ka", ap("KAI", 0, 1)),
+                         ("a", "le", ap("LEI", 0, 256)), ("s", "ad", ap("ADI", 0, 1024)), ("s", "vf", ap("W", 0, 2048)),
+                         ("a", "th", ap("THI", 0, 1))):
+        add(e, "load", (out, name), [], [out], "ld_" + name)
+
+    K, G16, KM15, K15, K16, WUC, KA1, K2, TH, KCS, K16X, MGN, MGP = [col(j) for j in range(13)]
+    iota(ap("COLI", 0, 1), [[0, 1]], 0, 1)
+    iota(full("JG"), [[16, 8], [0, 16]], 0, 0)
+    iota(full("JM"), [[0, 8], [1, 16]], 0, 0)
+    iota(ap("IOT", 0, 8), [[1, 8]], 0, 0)
+    ts(ap("COLI", 1, 2), ap("COLI", 0, 1), 15, A.bitwise_and)
+    ts(ap("COLI", 2, 3), ap("COLI", 0, 1), 112, A.bitwise_and)
+    copy(ap("COL", 0, 2), ap("COLI", 1, 3))
+    ts(full("BO"), full("JG"), G16, A.is_equal)
+    ts(full("M1"), full("JM"), K, A.is_equal)
+    ts(ap("MK", 0, 16), ap("JM", 0, 16), K, A.is_equal)
+    copy(ap("LC", 0, 8), ap("IOT", 0, 8))
+    ts(ap("LB", 0, 8), ap("IOT", 0, 8), 16.0, A.mult, 15.0, A.add)
+    for c, mul, plus in ((WUC, 14.0, 1.0), (KM15, 1.0, -15.0), (K15, -1.0, 4111.0), (K16, 1.0, 16.0)):
+        ts(c, K, mul, A.mult, plus, A.add)
+    act(K16X, K, AF.Copy, None, 16.0)
+    act(KCS, K, AF.Copy, None, CS)
+    act(full("WU"), full("BO"), AF.Copy, None, WUC)
+    act(full("WK"), full("BO"), AF.Copy, None, K)
+    act(full("BOH"), full("BO"), AF.Copy, None, CS)
+    ts(ap("BM", 0, 64), ap("JM", 0, 64), K, A.not_equal, BIG, A.mult)
+    asel(full("ID"), full("BO"), A.is_equal, 0.0)
+    asel(full("CE2"), full("BO"), A.is_gt, 0.0)
+    asel(full("TR"), full("CE2"), A.not_equal, -1.0)
+    for k in range(16):
+        act(ap("SELN", 128 * k, 128 * k + 128), full("ID"), AF.Copy, None, ap("MK", k, k + 1))
+    memset(ap("SELE", 0, 1024), 0.0)
+    iota(ap("SELE", 1024, 2048), [[0, 1024]], 0, 0)
+    for k in range(16):
+        act(ap("SELE", 129 * k, 128 * k + 128, 16), ap("BO", 0, 128, 16), AF.Copy)
+    ts(KA1, ap("KAI", 0, 1), 1184.0, A.add)
+    ts(ap("COLI", 3, 4), ap("KAI", 0, 1), 15, A.bitwise_and)
+    ts(K2, ap("COLI", 3, 4), 2048.0, A.mult)
+    copy(TH, ap("THI", 0, 1))
+    iota(MGP, [[0, 1]], int(MAGIC), 0)
+    iota(MGN, [[0, 1]], -int(MAGIC), 0)
+    act(full("NEG"), full("ID"), AF.Copy, None, -4096.0)
+    act(full("DK"), full("ID"), AF.Copy, None, K16)
+    act(full("MH"), full("ID"), AF.Copy, None, -0.5)
+    act(full("M32"), full("ID"), AF.Copy, None, -32.0)
+    memset(ap("QC", 0, 64), 0.25)
+    iota(ap("BASE", 0, 144), [[16, 144]], 2032, 0)
+    memset(ap("KEEP", 0, 512), 1.0)
+    memset(ap("KEEP", 0, 512, 16), 0.0)
+    iota(ap("RST", 0, 512), [[0, 512]], 0, 0)
+    memset(ap("RST", 0, 512, 16), 2 * BIG)
+    memset(ap("CMP", 0, 64), -0.5)
+    memset(ap("CMP", 64, 128), 6.5)
+    iota(ap("T16", 0, 128), [[16, 128]], 0, 0)
+    iota(ap("IOF", 0, 16), [[768, 2], [16, 8]], 256, 0)
+    act(ap("DUMP", 0, 16), ap("IOF", 0, 16), AF.Identity, KCS, CS)
+    ts(ap("COLI", 4, 5), ap("COLI", 0, 1), 7, A.bitwise_and)
+    ts(ap("COLI", 5, 6), ap("COLI", 0, 1), 3, A.bitwise_and)
+    ts(ap("TMP", 0, 2), ap("COLI", 4, 6), 1.5, A.add)
+    ts(ap("TMP", 2, 3), ap("COLI", 5, 6), 5.5, A.add)
+    act(ap("TMP", 4, 7), ap("TMP", 0, 3), AF.Square)
+    ts(ap("LP", 2, 5, 2), ap("TMP", 4, 6), 8.0, A.mult, -3.0, A.add)
+    ts(ap("LP", 6, 7), ap("TMP", 6, 7), 8.0, A.mult, -163.0, A.add)
+    iota(ap("RD", 0, 2 * TRI), [[0, 2 * TRI]], -1, 0)
+    for b in range(8):
+        iota(ap("RD", 8 * b * (b + 1), 8 * b * (b + 1) + TRI + 1, TRI), [[0, 2]], 4096, 0)
+    iota(ap("AD", 1024, 1152), [[0, 128]], 0, 0)
+    for m in range(1, STEPS):
+        iota(ap("MS", (m - 1) * 8 * BLK + 4, m * 8 * BLK, FLD), [[0, 128]], 0, 0)
+    copy(ap("LE", 0, 256), ap("LEI", 0, 256))
+    for j in range(0, 1024, 256):
+        copy(ap("AD", j, j + 256), ap("ADI", j, j + 256))
+
+    ts(lst("ML", 0, 0, 8), ap("CBI", 0, 8), CS, A.mult)
+    copy(ap("CF", 0, 8), ap("CBI", 0, 8))
+    tt(full("CE"), ind(ap("CF", 0, 8), ap("LC", 0, 8)), full("M1"), A.mult)
+    mm([(ap("PU1", 0, 128), [(full("WU"), ap("ZB", z1, z1 + 128))])])
+    mm([(ap("PU0", 0, 128), [(full("BO"), full("CE"))])])
+    act(ap("ML", 2, 8 * BLK, FLD), ap("PU0", 0, 128), AF.Copy, None, CS)
+    copy(full("Y"), ap("PU1", 0, 128))
+    ts(full("YU"), full("Y"), 4095, A.bitwise_and)
+    ts(ap("ML", 1, 8 * BLK, FLD), full("YU"), -2048.0, A.add)
+    for h in range(2):
+        act(ap("PU%d" % h, 256, 320), ap("T16", 64 * h, 64 * h + 64), AF.Copy)
+        act(ap("PU%d" % h, 320, 324), ap("T16", 0, 64, 16), AF.Identity, K16X)
+
+    for m in range(1, STEPS + 1):
+        last = m == STEPS
+        seen.clear()
+        q = 128 * (m & 1)
+        q8 = 8 * (m & 1)
+        lew = ap("LEI", 0, 256) if m == 1 else ap("LE", 0, 256)
+        VFW = ap("W", 0, 2048)
+
+        for h in range(2):
+            PN, PE_, PF = "PN%d" % h, "PE%d" % h, "PF%d" % h
+            quarters = [(HALF * h, HALF * h + 32), (HALF * h + 32, HALF * h + HALF)]
+            cur[0] = "AB"[h]
+            if m > 1:
+                add("n", "recv", (m - 1, h), [ap("TOK", 2 * m + h - 2, 2 * m + h - 1)],
+                    [blk("ML", m - 1, b) for b in range(4 * h, 4 * h + 4) if (b + m - 1) % NR], "arr%d_%d" % (m - 1, h))
+                act(hs("ZB", h, q), fld("ML", m - 1, h, 0), AF.Copy)
+                act(hs("AB", h, q), fld("ML", m - 1, h, 3), AF.Copy)
+            c16 = ap("C16", q8 + 4 * h, q8 + 4 * h + 4)
+            ts(c16, lst("ML", m - 1, 4 * h, 4 * h + 4), 1.0 / CS, A.mult, 0.25, A.add)
+            copy(hs("S16", h, q), ind(lew, c16))
+            act(ap(PN, 64, 128), fld("ML", m - 1, h, 1), AF.Identity, K2, KA1)
+            tt(hs("PI", h), ap(PN, 64, 128), fld("ML", m - 1, h, 2), A.add)
+            ts(hs("AI", h, q), hs("PI", h), 5, A.arith_shift_right, 1023, A.bitwise_and)
+            copy(hs("A16", h, q), hs("AI", h, q))
+            for b in range(4 * h, 4 * h + 4):
+                o = 8 * b * (b + 1)
+                a0 = (m - 1) * 8 * BLK
+                act(ap("DD", o, o + 16 * b + 16), ap("ML", a0 + 2, a0 + (b + 1) * BLK, FLD), AF.Abs,
+                    ap("ML", a0 + b * BLK + 4, a0 + b * BLK + 5), -1.0)
+            for t0, t1 in quarters:
+                if m == 1:
+                    copy(ap("G", 16 * t0, 16 * t1), ind(ap("ADI", 0, 1024), ap("A16", q + t0, q + t1)))
+                else:
+                    gather(ap("G", 16 * t0, 16 * t1), ind(ap("AD", 0, 1024), ap("A16", q + t0, q + t1)))
+            for t0, t1 in quarters:
+                gather(ap("W", 2048 + 16 * t0, 2048 + 16 * t1), ind(VFW, ap("S16", q + t0, q + t1)))
+            mm([(ap(PN, 0, 64), [(ap("SELN", 128 * k, 128 * k + 128), ap("G", 1024 * h + k, 1024 * h + 1024, 16))
+                                 for k in range(16)])])
+            copy(hs("N16", h), ap(PN, 0, 64))
+            act(hs("NF", h), ap(PN, 0, 64), AF.Copy)
+            for t0, t1 in quarters:
+                tt(ap("D", 16 * t0, 16 * t1), ind(VFW, ap("N16", t0, t1)), ap("W", 2048 + 16 * t0, 2048 + 16 * t1),
+                   A.subtract)
+                act(ap("DA", 16 * t0, 16 * t1), ap("D", 16 * t0, 16 * t1), AF.Abs)
+            pre = [(full("M32"), hs("AB", h, q))] if m > 1 else []
+            mm([(ap(PE_, 0, 64), pre + [(ap("SELE", 128 * k, 128 * k + 128), ap("DA", 1024 * h + k, 1024 * h + 1024, 16))
+                                        for k in range(16)])])
+            okh = hs("OK", h)
+            ts(okh, ap(PE_, 0, 64), TH, A.is_le)
+            if not last:
+                act(hs("KEY", h), ap(PE_, 0, 64), AF.Identity, K15, 16.0)
+            r1, r2 = ap(PF, 128, 192), ap("PU%d" % h, 128, 192)
+            mm([(ap(PF, 0, 64), [(full("TR"), okh)]), (ap(PF, 64, 128), [(full("BO"), okh)])])
+            mm([(r2, [(full("ID"), ap("BASE", 64 * h, 64 * h + 64)), (full("DK"), okh)])], True, False)
+            tt(ap("FL", 128 * h, 128 * h + 128), ap(PF, 0, 128), full("CMP"), A.is_lt)
+            fh, sq = ap("FL", 128 * h, 128 * h + 64), ap("FL", 128 * h + 64, 128 * h + 128)
+            mm([(r2, [(full("NEG"), sq)])], False, True)
+            mm([(r1, [(full("ID"), ap("BASE", 64 * h + 1, 64 * h + 65)), (full("WK"), fh), (full("NEG"), sq)])])
+            tt(hs("X1", h), r2, hs("NF", h), A.max)
+            tt(hs("X2", h), r1, hs("X1", h), A.max)
+            copy(hs("F16", h), hs("X2", h))
+            if not last:
+                if m > 1:
+                    mm([(ap(PN, 256, 320), [(full("ID"), hs("AB", h, q)), (full("ID"), sq)])])
+                    act(fld("MS", m - 1, h, 3), ap(PN, 256, 320), AF.Copy)
+                else:
+                    act(fld("MS", m - 1, h, 3), sq, AF.Copy)
+            for t0, t1 in quarters:
+                gather(ap("FV", 16 * t0, 16 * t1), ind(ap("W", 0, 3072 + 1024 * h), ap("F16", t0, t1)))
+                scan(ap("MX", 16 * t0, 16 * t1), ap("KEEP", 0, 512), ap("FV", 16 * t0, 16 * t1), A.mult, A.max)
+                scan(ap("MN", 16 * t0, 16 * t1), ap("RST", 0, 512), ap("FV", 16 * t0, 16 * t1), A.max, A.min)
+
+        cur[0] = "W"
+        scan(ap("RR", 0, TRI), ap("RD", 0, TRI), ap("DD", 0, TRI), A.add, A.min)
+        ts(ap("XD", 0, 16), ind(ap("RR", 0, TRI), ap("LP", 2, 3)), KM15, A.not_equal, 2 * BIG, A.mult)
+        tt(ap("YD", 0, 8), ap("XD", 0, 8), lst("ML", m - 1, 0, 8), A.add)
+        tt(ap("ZD", 0, 8), ap("YD", 0, 8), ap("DUMP", 0, 8), A.min)
+        ts(ap("O16", 0, 8), ap("ZD", 0, 8), 1.0 / CS, A.mult, 0.25, A.add)
+        for h in range(2):
+            tt(hs("SN", h), ind(lew, ap("C16", q8 + 4 * h, q8 + 4 * h + 4)), hs("NF", h), A.subtract)
+            tt(hs("SO", h), hs("SN", h), hs("OK", h), A.mult)
+
+        for h in range(2):
+            PE_, PU, PF = "PE%d" % h, "PU%d" % h, "PF%d" % h
+            y0 = 72 * h
+            cur[0] = "cd"[h]
+            tt(ind(ap("LE", 0, 384), ap("O16", 4 * h, 4 * h + 4)), hs("SO", h), hs("NF", h), A.add)
+            ii = ap(PF, 256, 320)
+            if not last:
+                transp(hs("KT", h), hs("KEY", h))
+                scan(hs("KS", h), ap("KEEP", 0, 64), hs("KT", h), A.mult, A.max)
+                tt(hs("IT", h), ind(hs("KS", h), ap("LB", 0, 4)), hs("KT", h), A.is_equal)
+                transp(ii, hs("IT", h))
+                tt(hs("IA", h), ii, hs("AI", h, q), A.mult)
+                act(hs("NI", h), ii, AF.Identity, 1.0, -1.0)
+                mm([(hs("PN0", h, 128), [(full("ID"), ap("BM", 0, 64)), (full("BOH"), hs("IA", h))]),
+                    (hs("PN1", h, 128), [(full("BOH"), hs("IA", h))])])
+                scan(hs("AL", h), ap("RST", 0, 64), hs("PN0", h, 128), A.max, A.min)
+                for b in range(4 * h, 4 * h + 4):
+                    o = TRI + 8 * b * (b + 1)
+                    act(ap("DD", o, o + 16 * b + 16), ap("PN1", 128, 128 + 16 * b + 16), AF.Abs,
+                        ap("AL", 16 * b + 15, 16 * b + 16), -1.0)
+                r0, r1 = TRI + 160 * h, TRI + 160 + 416 * h
+                o0 = 8 + 4 * h
+                scan(ap("RR", r0, r1), ap("RD", r0, r1), ap("DD", r0, r1), A.add, A.min)
+                ts(ap("XD", 16 + 16 * h, 32 + 16 * h), ind(ap("RR", r0, r1), ap("LP", 4 + 2 * h, 5 + 2 * h)), KM15,
+                   A.not_equal, 2 * BIG, A.mult)
+                tt(ap("YD", o0, o0 + 4), ap("XD", 16 + 16 * h, 20 + 16 * h), ap("AL", 64 * h + 15, 64 * h + 64, 16), A.add)
+                tt(ap("ZD", o0, o0 + 4), ap("YD", o0, o0 + 4), ap("DUMP", o0, o0 + 4), A.min)
+                ts(ap("O16", o0, o0 + 4), ap("ZD", o0, o0 + 4), 1.0 / CS, A.mult, 0.25, A.add)
+                tt(hs("T1", h), ind(ap("AD", 0, 1152), ap("O16", o0, o0 + 4)), hs("NI", h), A.mult)
+            cur[0] = "ab"[h]
+            mm([(ap(PE_, 64, 128), [(full("ID"), hs("ZB", h, q)), (full("ID"), ap("QC", 0, 64)),
+                                    (full("MH"), ap("MX", 1024 * h + 15, 1024 * h + 1024, 16)),
+                                    (full("MH"), ap("MN", 1024 * h + 15, 1024 * h + 1024, 16))])])
+            act(hs("ZR", h), ap(PE_, 64, 128), AF.Identity, MGP)
+            act(hs("Z16", h), hs("ZR", h), AF.Abs, MGN)
+            masked = (ap(PU, 64, 128), [(full("ID"), ap("BM", 0, 64)), (full("WU"), hs("Z16", h))])
+            if not last:
+                act(fld("MS", m - 1, h, 0), hs("ZR", h), AF.Abs, MGN)
+                mm([masked, (ap(PU, 0, 64), [(full("WU"), hs("Z16", h))])])
+            else:
+                mm([masked])
+            scan(hs("XS", h), ap("RST", 0, 64), ap(PU, 64, 128), A.max, A.min)
+            copy(ap("Y", y0 + 64, y0 + 68), ap("XS", 64 * h + 15, 64 * h + 64, 16))
+            lo = y0 + (64 if last else 0)
+            if not last:
+                copy(ap("Y", y0, y0 + 64), ap(PU, 0, 64))
+            ts(ap("YL", lo, y0 + 68), ap("Y", lo, y0 + 68), 15, A.bitwise_and)
+            tt(ap("WF", lo, y0 + 68), ap("YL", lo, y0 + 68), ap(PU, 256 + lo - y0, 324), A.add)
+            copy(ap("W16", 4 * h, 4 * h + 4), ap("WF", y0 + 64, y0 + 68))
+            if not last:
+                tt(hs("T2", h), ap("WF", y0, y0 + 64), ii, A.mult)
+                tt(ind(ap("AD", 0, 1152), ap("O16", 8 + 4 * h, 12 + 4 * h)), hs("T1", h), hs("T2", h), A.add)
+                ts(ap("YU", y0, y0 + 68), ap("Y", y0, y0 + 68), 4095, A.bitwise_and)
+                ts(fld("MS", m - 1, h, 1), ap("YU", y0, y0 + 64), -2048.0, A.add)
+                ts(ap("YM", y0, y0 + 68), ap("YU", y0, y0 + 68), 1103.0, A.mult)
+                ts(ap("YC", y0, y0 + 68), ap("YM", y0, y0 + 68), 4, A.arith_shift_right, 255, A.bitwise_and)
+                ts(fld("MS", m - 1, h, 2), ap("YC", y0, y0 + 64), CS, A.mult)
+                ts(lst("MS", m - 1, 4 * h, 4 * h + 4), ap("YC", y0 + 64, y0 + 68), CS, A.mult)
+                away = []
+                for b in range(4 * h, 4 * h + 4):
+                    if (b + m) % NR:
+                        away.append(blk("MS", m - 1, b))
+                    else:
+                        act(blk("ML", m, b), blk("MS", m - 1, b), AF.Copy)
+                add("g", "send", (m, h), away, [ap("TOK", 2 * m + h, 2 * m + h + 1)], "none")
+            copy(ind(ap("W", 1024 * h, 1024 * h + 1024), ap("W16", 4 * h, 4 * h + 4)), hs("Z16", h))
+
+    add("s", "store", ("yl", None, ap("LE", 0, 256)), [ap("LE", 0, 256)], [], "st_yl")
+    add("s", "store", ("yz", None, full("Z16")), [full("Z16")], [], "st_yz")
+    add("s", "store", ("yv", (0, 1024), ap("W", 0, 1024)), [ap("W", 0, 1024)], [], "st_yv0")
+    add("a", "store", ("yv", (1024, 2048), ap("W", 1024, 2048)), [ap("W", 1024, 2048)], [], "st_yv1")
+    return ops
+
+
+def dependencies(ops):
+    acc = {}
+    deps = []
+    for i, o in enumerate(ops):
+        d = set()
+        rd, wr = {}, {}
+        for x in o["r"]:
+            rd[x[0]] = rd.get(x[0], 0) | bits(x)
+        for x in o["w"]:
+            wr[x[0]] = wr.get(x[0], 0) | bits(x)
+        for n in set(rd) | set(wr):
+            r, w = rd.get(n, 0), wr.get(n, 0)
+            keep = []
+            for j, jr, jw in acc.get(n, []):
+                if (jw & (r | w)) or (jr & w):
+                    d.add(j)
+                jr &= ~w
+                jw &= ~w
+                if jr or jw:
+                    keep.append((j, jr, jw))
+            keep.append((i, r, w))
+            acc[n] = keep
+        deps.append(sorted(d))
+    return deps
+
+
+def with_banks(ops, deps, order):
+    last, done, out = {}, set(), [None] * len(ops)
+    for i in order:
+        assert all([j in done for j in deps[i]])
+        done.add(i)
+        extra = []
+        for b in set([x[0] for x in ops[i]["r"] + ops[i]["w"] if x[0] in PS]):
+            extra += [x for e, x in last.get(b, {}).items() if e != ops[i]["e"]]
+            last.setdefault(b, {})[ops[i]["e"]] = i
+        out[i] = sorted(set(deps[i] + extra))
+    return out
+
+
+def routes(T, topo, m, h):
+    out = []
+    for r in range(NR):
+        src, mine, used = T.cores[r], [], []
+        for b in range(4 * h, 4 * h + 4):
+            if (b + m) % NR == 0:
+                continue
+            dst = T.cores[(r + b + m) % NR]
+            via = None
+            if not topo.may_write(src, dst):
+                able = [c for c in topo.cores_of(src) if c != src and T.rank_of(c) is None and topo.may_write(c, dst)]
+                able.sort(key=lambda c: (c in used, topo.die(c) != topo.die(src), c))
+                via = able[0]
+                used.append(via)
+            mine.append((b, dst, via))
+        out.append(mine)
+    return out
+
+
+def engine_masks(topo, src, mine):
+    direct = [x for x in mine if x[2] is None]
+    relay = [x for x in mine if x[2] is not None]
+    off = topo.engines(src, direct[0][1])
+    on = [e for e in topo.engines(src, relay[0][2]) if e not in off]
+    res = {}
+    for group, eng in ((direct, off), (relay, on)):
+        k = len(eng) // len(group)
+        for i, x in enumerate(group):
+            res[x[0]] = eng[i * k:(i + 1) * k]
+    return res
+
+
+def as_mask(eng):
+    return sum([1 << e for e in eng])
+
+
+def arrivals(T, topo, m, h, core):
+    total = 0
+    for r, mine in enumerate(routes(T, topo, m, h)):
+        em = engine_masks(topo, T.cores[r], mine)
+        for b, dst, via in mine:
+            if dst == core:
+                total += len(em[b]) if via is None else len(topo.engines(via, dst))
+    return total
+
+
+def relay_program(g, core, T, topo):
+    sent = 0
+    for m in range(1, STEPS):
+        for h in range(2):
+            for r, mine in enumerate(routes(T, topo, m, h)):
+                for b, dst, via in mine:
+                    if via == core:
+                        sem = T.sem["arr%d_%d" % (m, h)]
+                        g.wait_ge(sem, len(engine_masks(topo, T.cores[r], mine)[b]))
+                        blk = T["ML"][:, m * 8 * BLK + b * BLK:m * 8 * BLK + b * BLK + BLK]
+                        rid, pid = topo.addr(dst, core)
+                        g.remote_dma(blk, blk, sem, T.sem["sent"], pid, rid, topo.mask(core, dst))
+                        sent += len(topo.engines(core, dst))
+    if sent:
+        g.wait_ge(T.sem["sent"], sent)
+
+
+_CACHE = {}
+
+
+def rank_program(g, core, T, topo):
+    rank = T.rank_of(core)
+    if rank is None:
+        relay_program(g, core, T, topo)
+        return
+    if "plan" not in _CACHE:
+        ops = build_ops()
+        order = [DIGITS.index(ORDER[i]) * 62 + DIGITS.index(ORDER[i + 1]) for i in range(0, len(ORDER), 2)]
+        order = order or list(range(len(ops)))
+        assert sorted(order) == list(range(len(ops)))
+        _CACHE["plan"] = (ops, with_banks(ops, dependencies(ops), order), order)
+    ops, deps, order = _CACHE["plan"]
+    Q = {"v": g.vector, "a": g.scalar, "p": g.tensor, "g": g, "s": g.sync}
+
+    def P(x):
+        if not isinstance(x, tuple):
+            return x
+        if x[4] is not None:
+            return T[x[0]][:, x[1]:x[2]].indirect(P(x[4]))
+        if x[3] == 1:
+            return T[x[0]][:, x[1]:x[2]]
+        return T[x[0]][:, x[1]:x[2]:x[3]]
+
+    count = {"v": 0, "a": 0, "p": 0, "g": 0}
+    known = {"v": {}, "a": {}, "p": {}, "g": {}, "s": {}}
+    done = {}
+    sent = 0
+    own = []
+    for i in order:
+        o = ops[i]
+        e, k, a = o["e"], o["k"], o["a"]
+        if k == "recv":
+            done[i] = (o["sem"], arrivals(T, topo, a[0], a[1], core), {})
+            continue
+        q, kn = Q[e], known[e]
+        need = {}
+        for j in deps[i]:
+            if done[j][0] != "none":
+                need[done[j][0]] = max(need.get(done[j][0], (0, 0)), (done[j][1], j))
+        for s in sorted(need, key=lambda s: -need[s][1]):
+            v, j = need[s]
+            if kn.get(s, 0) < v:
+                q.wait_ge(T.sem[s], v)
+                kn[s] = v
+                for s2, v2 in done[j][2].items():
+                    if kn.get(s2, 0) < v2:
+                        kn[s2] = v2
+        if k == "load" or k == "store":
+            if k == "load":
+                ins = q.dma_start(P(a[0]), T[a[1]][:])
+            else:
+                ins = q.dma_start(T[a[0]][:] if a[1] is None else T[a[0]][:, a[1][0]:a[1][1]], P(a[2]))
+            ins.then_inc(T.sem[o["sem"]], 16)
+            done[i] = (o["sem"], 16, dict(kn))
+            own.append(o["sem"])
+            continue
+        if k == "send":
+            m, h = a
+            mine = routes(T, topo, m, h)[rank]
+            em = engine_masks(topo, core, mine)
+            trs = []
+            for b, dst, via in mine:
+                rid, pid = topo.addr(dst if via is None else via, core)
+                trs.append(RemoteDMATransfer(
+                    dst_ids=[DstId(rid=rid, pnc=pid)], dma_engine_mask=as_mask(em[b]),
+                    remote_sem=T.sem["arr%d_%d" % (m, h)],
+                    src=T["MS"][:, (m - 1) * 8 * BLK + b * BLK:(m - 1) * 8 * BLK + b * BLK + BLK],
+                    dst=T["ML"][:, m * 8 * BLK + b * BLK:m * 8 * BLK + b * BLK + BLK]))
+                sent += len(em[b])
+            g.remote_dma_fused(trs, local_sem=T.sem["sent"])
+            done[i] = ("none", 0, {})
+            continue
+        if k == "mm":
+            for x in a:
+                q.matmul(P(x[0]), P(x[1]), P(x[2]), x[3], x[4]).then_inc(T.sem[CNT[e]], 1)
+            count[e] += len(a)
+            done[i] = (CNT[e], count[e], dict(kn))
+            continue
+        if k == "copy":
+            ins = q.tensor_copy(P(a[0]), P(a[1]))
+        elif k == "tt":
+            ins = q.tensor_tensor(P(a[0]), P(a[1]), P(a[2]), a[3])
+        elif k == "ts":
+            if a[5] is None:
+                ins = q.tensor_scalar(P(a[0]), P(a[1]), P(a[2]), None, a[4])
+            else:
+                ins = q.tensor_scalar(P(a[0]), P(a[1]), P(a[2]), P(a[3]), a[4], a[5])
+        elif k == "scan":
+            ins = q.tensor_tensor_scan(P(a[0]), P(a[1]), P(a[2]), a[3], a[4], a[5])
+        elif k == "tr":
+            ins = q.transpose(P(a[0]), P(a[1]))
+        elif k == "memset":
+            ins = q.memset(P(a[0]), a[1])
+        elif k == "asel":
+            ins = q.affine_select(P(a[0]), P(a[1]), [[1, 128]], a[2], a[3], 0, -1)
+        elif k == "iota":
+            if _S[a[0][0]][0] == I32:
+                ins = q.iota(P(a[0]), a[1], a[2], a[3])
+            else:
+                ins = q.iota(P(a[0]), a[1], a[2], a[3], allow_small_or_imprecise_dtypes=True)
+        else:
+            kw = {}
+            if a[3] is not None:
+                kw["bias"] = P(a[3])
+            if a[4] is not None:
+                kw["scale"] = P(a[4])
+            ins = q.activation(P(a[0]), P(a[1]), a[2], **kw)
+        ins.then_inc(T.sem[CNT[e]], 1)
+        count[e] += 1
+        done[i] = (CNT[e], count[e], dict(kn))
+    for e in count:
+        g.wait_ge(T.sem[CNT[e]], count[e])
+    g.wait_ge(T.sem["sent"], sent)
+    for s in own:
+        g.wait_ge(T.sem[s], 16)

@@ -13,7 +13,8 @@ _S = {
     "W": (BF, 4096), "ADI": (I32, 1024), "LEI": (I32, 256), "AD": (F32, 1152), "LE": (F32, 384),
     "G": (F16, 2048), "D": (BF, 2048), "DA": (BF, 2048), "FV": (BF, 2048), "MX": (BF, 2048), "MN": (BF, 2048),
     "SELN": (BF, 2048), "SELE": (BF, 2048),
-    "ML": (F32, 5 * 8 * BLK), "MS": (F32, 4 * 8 * BLK),
+    "ML": (F16, 5 * 8 * BLK), "MS": (F16, 4 * 8 * BLK),
+    "KH": (BF, 128), "NID": (BF, 128), "KL": (BF, 128), "IDH": (F16, 128), "CL": (F32, 16),
     "CBI": (I32, 8), "KAI": (I32, 8), "THI": (I32, 8), "CF": (F32, 8), "COL": (F32, 16), "COLI": (I32, 16),
     "JM": (F32, 128), "JG": (F32, 128), "TMP": (F32, 8), "IOT": (I32, 8), "IOF": (F32, 16), "MK": (F32, 16),
     "ID": (BF, 128), "BO": (BF, 128), "BOH": (F16, 128), "TR": (BF, 128), "WK": (BF, 128), "WU": (BF, 128),
@@ -24,7 +25,7 @@ _S = {
     "LB": (U16, 8), "LC": (U16, 8), "LP": (U16, 8),
     "C16": (U16, 16), "S16": (U16, 256), "A16": (U16, 256), "N16": (U16, 128), "F16": (U16, 128), "W16": (U16, 8),
     "O16": (U16, 16),
-    "PI": (I32, 128), "AI": (I32, 256), "AB": (BF, 256), "ZB": (BF, 256), "NF": (F32, 128),
+    "PI": (I32, 128), "AI": (I32, 256), "ZB": (BF, 128), "NF": (F32, 128),
     "OK": (BF, 128), "FL": (BF, 256), "X1": (F32, 128), "X2": (F32, 128), "ZR": (F32, 128), "Z16": (BF, 128),
     "XS": (F32, 128), "Y": (I32, 144), "YU": (I32, 144), "YM": (I32, 144), "YC": (I32, 144), "YL": (I32, 144),
     "WF": (F32, 144),
@@ -47,6 +48,18 @@ CNT = {"v": "cv", "a": "ca", "p": "cp", "g": "cg"}
 
 ENG = "aaaaaaaavaavvavaaaaavaavvavaavaavaavaaaavaaavaavaavaaaaa"
 ORDER = "0102071k03051e000608040c0b0M090d0a1l0e0n180o0j0g0q0t1q0h0p1g0P0S0N0f1a1p0x0m1h0J0l0s0I1s150E1P1S140A1Q160D1R0y0w1V1T2F0K1W0R220F1X1U2G2H23241f0Q250Y2I0H262J0L1i270G2K2c120B2e2d0u0z0Z0v130C2S2Q2g1w2f2P2h0U172T0V2l0O112R1B2j1A0W1C0X1D100T1z2m1y1x2U1j1E2W192k1G1m2N2n1b2Y2L1n2i2X1F1H282o1N2Z2q1I2r2s3n2O2t1J2u1L2a302M2v2b1r292w2V0i2p2x1t1M2z311K3334350k3s362C371u383t391v3a2B2A1c3f2D2E3o3K3i323L3g3M3c3h3O463P3R3Q3j3X472y3Z3N3Y401Z3S1Y411o420r3e433b213d201d3p4o3u3k3T4p1O4q4K4r3v4s3l3w4t3x3y4v4u3U4B3z4D3A4C3B4E3m3C4F3D4G484H4I4w494x4a3E4b4c4y3F3V4d3G3r4e4g5r4f4J4h3H4i3I4j3J443q4k454l4z4m3W4n4A4P4M4Q4U4N4W4R4V4T4S4L4O4Y4X4Z50515u5w525B5x5D5v5A5y5H5z545F5E5G565I555J5L575C58535N5M5t5K5s59685O5b5c5d6d5a5e5f695P5g6a5h6b5i6c5l5o5j5Q5k5m5R5S5T5q5n5p6f6A6e6i6h6B6C5U6D6E6j6g5V5W6F606H6G5X616N5Y6P5Z6Q656O6R6S6k6T6W6l6X6m6I6Y6o626J6p667A676Z6r636t6q6s646n716K707e6V727f6u6U7g7h7i6v737j777l7k766w7r747m757t7s7u6L7v7w7n787x7y6x7o6y796z7a6M8h7z7b7p7c7d7q7D7F7C7G7B7E7M7L7H7K7J7I7N7O7Q7P7R7S7T7U7W7V8m8j8i8n8k7X8o8l8p8u8v7Y8x8w8y7Z8z8081828A8D8r8q8t8s8B8E838C93848598898699878a8F888b8e8G8g8H8I8J8K8c8L8M8Q8N9M8O8R9N8P8d8V8f9a9q9b9c9r8X9e9s8S8W9u9v9x9w9f9D9y9t9F9h9E9G9i9z9g9I9j9H9d8T9J8U94a4958Ya5a69Oaqa79Ba89P8Z9Ra9abaa9Qah9S9Aajaiak9Tal9Wam9k9Vao909l9X919U9m96an9nac9o9Y9pb79Zada09Ka1aea29Cafa392ag97ap9LatavasawazauaAaCaxaFayaGaEaDaBaraHbabcb9bdbhbjbebgbfb8bbblaIaKbkaMbnbobmaLbpbtaNaJaObqbrbubiaPbTbsaRbVaSaTbUaQaUaVbvaWbYaXbZaYbOb1c0aZbwc1bybWbzbPbAb4b3bBbCbGb2bDc2bEb0bQbxbFb5c4bLb6cCc5cgcDbRcEchbMcibIbNckclcncmbSctcFcjcvc7cucwc9cGc8cyc6cxbHbJc3czcIcHbKcacUcocbcpcccVcqcdcWcJdgcXcecrcYcMcfcKcLcZd1cNd0d7d2d9d8dad3dcdbbXddded4cBcOcAdUdfcPd5cQcscRcScTd6djdldqdkdidrdmdvdndodtdudwe3dxdsdpdhdXdZdWe0e4dYe6e1dyeae2e7e8dAe9ebdCdBecegdDdzdEedeeehe5dVdFeDefdGeFdHdIeEdJdKeidLdMdNeydOezejeAekeGeleBemdReCeneoepeqereHevdTdQdPesdSexeIeweJeteKeueLeMeTeNeOeUePeVeQeWf4eReXf5eYeZf0f1f2eSf6f3"
+ENG = "aaaaaaaaavavvaavaaaavaavvavaaaaaavaavaavaaaaavaaaaavaaaa"
+ORDER = "0002071m0103050608040c0b1q090d1r0e0o0n1k0q0t0f1M1v0j1w0a0m0p0g0N0M1a0H0G0D0h0l0I1n0L141Y1W0B16210x150P1X0Q0R0C17221Z191b1V181c23201l2M0F282b0S2O2P0A0u2a0z2c2Q0K2d0J2R0v2e0Y2S2l2j1o0w2k0E2Z1C2Y0y302n2X2m2o1d312q1e0X1f101G110U1K0O1H122s0Z1E0T1D0V1F2r1J1I1s320W0i13362t1t1L1h2u2p34331g37292v1R352x2y2z1S1i2A2B2w382C2N1x0r2D2h1y2E0s1z0k2G1T1U1p1B393v2J3b1A3c2I2H3x3a2i2L2F2f2K2U2V3d2g3S2T3A2W3w3e3f4e3T3g1u3B3U3h3V4f3j3W3i263C3k3X3Z3Y3D453E473G46483n404a493m4b3l24253o273F3p1j1N3H4S4g4w3I3q3L4x3J4h4y3r4i3K1Q4z4A4j4k1O4B1P4D4C3s4J3t4L414M4K4N4O3M424P4Q3u3N4l3y4n3O3z4p4m4o3P4E3Q5y4F4c4d4q434r3R4s444t4G4u4H4v4R4I4U4W534X524T504Y514V4Z5455575658595a5b5A5C5G5I5d5J5c5H5D5z5e5E5F5B5L5K5f6e5M5O5g6j6f6k6g5i5N5j5P5k5R5l5m5q5h5Q5r5n5T5S5o6o5U5p6p5s5v5V6h5t5u5X5x5W5w5Y5Z606G6q6162726H66636i6I646J73676K656r686L6N6M6s6T6u6O6V6U6W6b6P6X6Y6l6Z6a696t6c6d7G6Q6m7k74707l7m6n7n7o6v7p6z7r6x7q6w756y7x767z77787y7A6A7B7C717D7E7s6B7t796C7u7a6D7c6R7b6E7F7d8m6F7e7v7f7g6S7h7i7j7w7H7I7K7Q7L7R7P7M7O7J7N7S7T7V7U7W7X7Y7Z8o8q8v818u8w808r8n828s8t8p8y8z83978x8C848A92989386878D8B888F898a8e8E858b8H8G8f8c948I8d958g8j8J968h8i8L8k8K8l8M8N8O9u9c9Q8P8Q9d9v8U8R9R9w8S9x8V9y8T8Z9z9B9A9H9C9J9I9K8W9D9L9M919N909E8X8Yau99a89S9ea99T9faa9aab9gac9U9h9i9Vadafae9jal9nag9manam9l9kaoahap9Waq9Oaras9o9X9pa1ai9q9Y9Fa09raj9Z9satba9b9ta2a3a4a59P9Ga6a7akawayaDazaFavaEaAaCaxaBaGaHaIaKaJaLaNbebcaMbiaPblbjaObfbbaQbgbhbnbmaRbdbkbVbqboaSbQbWbRaUaVbrbpaWbtaXaYb2aTbsaZbvbub3b0c0bwb1c1b4b7bxbSb6b8bzb9byb5bAbBbCcic2bDbEcEcjbIbFc3ckbGclc4cmbHbTc5c6bNcncpcoc7cvcFcxcwcybKbUczcAbPcBbOcqcbc8bLc9cabMbJdicccGcWcrcHcdcXcIcscYcecZctcJd0bXcKcfd1d3d2cLd9cPd4dbcMdacNdcd5cOdddecQdfdgcgbZbYcRcDchdVcScud7cTcCd6cUdhcVd8djdkdmdldtdrdndsdqdodpdudvdwdydxdzdBdZdXdAe6e0dWdCe1e2dYe8e7dDe9ebeDdEeceeeadFe4ege3e5efeddGeyehdHdIdJeEdKeFdLeidMezdNeAdOeBdSeCejeHekelemdPeGeneoepeqerdUevdQdRdTesexeIeweJeteKeueLeMeTeNeOeUePeVeQeWf4eReXf5eYeZf0f1f2eSf6f3"
+LIN = "v" * 200
+DQ = "vvav"
+ENG = "aaaaaaaaavavvaavaaaavaavvavaaaaaavaavaavaaaaavavaaavaaaa"
+ORDER = "010002071m080b0c0d1r0e0n0o031q090j0g0l0q1M0t0p060J0C0H1l0a0f0M0T0R0m1w1v1n0h1k0L0N1L1s1C1J1o1t1e0u1E0v1H1F1D1I141Y1W151621170F0x0A0Q1a0S0I18191X1Z201V1b222M231c282b2P2O2a2c2Q2d2R2e2S0G0E0z0X0B110Z0Y0D0w0O0y042k2j052m0U0K2Z102l2Y2X2n300V132o312q2s2r0P0W321d362t122u3433371h2N2p291g2g2i0r1u2v1R0i2x2y2z1S2A2B352f382C1x2D1y2E1T3x1p1U2G3v2I0k393c3b2J2h2W1i2w2V1z272H0s2K2L3A3d3S3a2U3B3w4e3e3f3g1B3T1f2F3U3h3V4f3i3W1A3C3k3X3Z3Y3D453E473G46483n1O1j2T40494a3m3l3o3p4b4S4w244x4y4g3H1G1K3q1Q4h3r4i4A3j3J4k4B4D4C3s4J3t4L4z251N414M3u4K4O263K3I3L3M4N423y3N4l433O3z3P4c3Q4Q5y4j4m4p4o4n3F4q4E4r3R4s4d444t4F4u4H4G4v4R4I4W4X4Y4T4Z4V4U51534P501P5455575658595a525A5b5C5d5c5I5D5e6j5E5z5F5B5L5K5J5G5H5f5M5O5g6e6k6f6g5i5N5j5P5k5m5q5R5l5n5T5S5h5Q5o6o5U5p5v6p5s6h5t5u5x5V5W5w5Y5Z6G606q6i61625X5r6H6I6K6372646r65736J686L6N6M6s6T6O6V6U6W6b6P6X6Y6Z696a6l6c6d7G6Q6m6u706v74667k7l7m7o6n7p7r7q756x6w6t7n6y6z7x767z787y7A6A677B7C7E7s6B7t797a716C7u6D7F8m6E777d7c7b7e6F7f6R7g7v7h6S7i7j7w7I7P7R7K7L7M7H7N7Q7O7T7J7S7V7U7W7X7Z7Y7D8o8q81808w8n978r8s828v8t8y8p8z83848x8u9892938C8A86878D8B888a898e8F8G8E8b8H8c8d948g958f8I8h8i858j8k8J8K8l968M8N8O9u8P8Q8L9Q8R9c8S8T9v9w8U9y9x9d8Z9z9B9A9R9H9C9J9I9K8W9D9M9L9N90919Eau8X8Ya8a9aa9e9S999T9fab9U9a9gac9iadafae9j8Valaganamaoahapaq9W9Oas9l9m9k9h9n9o9X9Y9p9Fai9q9b9rbaa1a09Za29sa3aja49ta5ata69G9P9Va7akawaDaFaCayazaAaBavaHaGaraEaxaIaKaJaLaNbeaMbcaOaPbbbjaQbfbgbhbdbnbibmaRaSbVblbkbqbobQbWbRaUaVbrbpaWb2aXaYbtbuaTaZbvb0c0bwb1c1b4b7bsbxbSb6b9b8byb5bAbBbCcic2bDbEbzcjckbFcEbGc3b3clbHc4bTbIcmc6bNcncpcoc7cvcFcxcwcybKbUcAczbPbOcBbLbMdicqcac8c9cbcccGcWcrcdcXcYcHcecscIctbXcfd0cKd1d3d2cLcMcZbJcJcNcPcOc5d9d4dbdadcd5dddedgcgbZd7chcQcCcRdVbYcScucTd6cUcDcVdhd8dmdndjdodldkdrdtdpdudsdvdwdqdfdydxdzdBdZdAdXe6e0e1dWe2dYdCe8e7dDe9ebeceDdEeeeadFegede4e3e5efdGeydHdIdJeEezdKdLeheidMdNeAdOeBeFeCeHejeGekelemdPdSeneoepeqerevesdQdUdTdReIewexeJeteueKeLeMeTeNeOeUePeVf4eQeWeRf5eXeYeZf0f1f2eSf6f3"
+DQ = "vavv"
+LIN = "vvvvvvvvvvvvvvvvvvavavvvavvvvvvvvvvvvvvvavvvvvvvvvvvvvvvvvvvvvavvavvavvvvvvvvvvvvvvvavavvvavvvvvvvvvvv"
+ENG = "aaaaaaaavavaaaavavaavavaavavavaavavaavavavaavavaaaavavaa"
+ORDER = "040102001s070b0c1l0d0o060n03091N0M080e0R0j0g1n1r0f0m1o1w0l0a0t0N0Q0V0U0p0P0h1x0G1a0w0B1Z141X1y1Y2215200J0H1j0T0z0S0O161z1W1723291b242Q1c2S2119182c0A0Y0I0K130E0L0F0y0C2b2T2U2d0u1e1D1p1u0v052V2e1V2f1d2l2m2W2k31322n0Z0D0x11342o332p0s352r2t1T360W0X122s2u3a0i381U2w102v2x1A1h2q2y3b2z3z0k1K1f1F1L1t1G1H1I1J1M1m2B392C2D1R1g2E0q2F3c2G2R2A371B2H1q1i2J0r2a2I2N1S3B3E3d3F1C3A3f3g2K3h2P3i3j3k2O3l2h2Y2g2M2L2i3e2X4i2Z2j303G3W3X4j3H3m4k4l3I3Y3r3Z1E3u403K4143424m493o3L4b4c4o4a4e4d4f4p3C3v3s3p3M4q3P3O4s4r3N3q3t4t1v28264W3Q3w443x4A3y25454B4C3D1Q3n3J4D4E4u4F4H4G3R4N464P3S4Q4O4n274R1P3T4S474U4g4I3U4v3V4J4w4T1k4K5F484x4V4y4L4z4h4M4Y1O565550514X52534Z5859545a5b575c5d5f5h5J5K5H5L5G5e5Q5N5i5k5M5R5I5S5V5U5j5g5l5P5O5W5m605T5n5Y5o615p5r5Z6q5q5s5t5u6v5x5v6w5y5X625w5z6l6x6m6y6n6z6o5C63655B5A666B6768696p6A6C6D6G6F645E5D6d6a796N6b7a6c7b6E6H6O6P7c6Q6f6R6r7d7f6I6S6U6T7g70726i71736J7574766h6V6K6g6k6e7h7j7i7k7N6j7r6s7l6W6L7s7t6t7m7n7u6Y7v6X7w7y7x7o7E7z7G7F7H7A7J7B7e7I7L6M7p6Z776u8w7C7M7q7D787K7P7X7W7V7R7S7O7T7U7Z807Q83818284867Y888A8B8C8x858y898F8G8D8b8I8z8J8M8L8c878a8N8R8E8K8H8d8P8S8f8e9c8O8Q8g8h8i9h8j8k9m8l9n8m9d8n9e8q8t8T8U8W8X8o8p8V8u8r8s8va08Y9Ea19o8Z909Fa29G9I919Ha39294a493a69f9J969L9K9R9p9T9S9U9g9W999V9qa79X97989sa89tab95a99u9v9b9aaE9i9jaaa59Mac9x9waiajakal9yamad9k9zaeanapao9AavafaxawayaAaqaz9rar9BasaC9N9C9O9Pat9Dag9Y9Q9lahbn9ZaDaGaOaNaMaIauaJaFaKaLaHaQaSaRaBaTaPaUaVaXaWaZbrbsbtbobpb0bvbub2bzc8bAbDbqbCaYb1b3bBbEb4bIbwbybxb5b7bGbFb6bJb8bHb9c3c9babbbccdbKbdcebec4bhbkbLbmbMbNbOblbibjcvbPcfcRc5bQbfbRcSbVbScwcxcTcybgczbTbUcUcAcCc0cBcVcIcXcgcKcJcLc6cMbXcNcYchcOcjd0d2c1c2ckbYbZcnbWd1cZcodvcad9cldadbcmcid3cDc7cbccd4dcdddedgdfcEdmcpdodndpcqdrcGdqdtdhcrcQcsdid5dsdjcWcFctebcPd6cud7cHdud8dkdxdFdEdDdGdzdAdwdBdldCdydHdJdIdKdLdMdOdQefegdNeheceddRdTekeieneeeoereqdUdPdSelepejemesdVewdWeuexdXdZdYe0eTe1eUe2eteveye3e4eOe5eVePezeQeAe8eReBeCe7eDeEeFeGeSeHeLeWe6eae9eXeIeYeNeMeZeKeJf0f1f2f9f3f4faf5fbf6fcf7fdflfefffgfhfif8fjfmfk"
+LIN = "vvvvvvvvvvvvvvvvvvavavvavvvvvvvvvvavvvvvavvvvvvvvvvvvvvvavvvvvavvaaaavvvvvavvvvvvvvvavavvvavvvvvvvvvvv" + "vv"
+ORDER = "00010504021s070c0b0d090n030o1N060M080e0P0R0g0j0p1w1r0f1l1n0a0t0l1x1o0h140s160N0Q0S0U0V0H0w0F0B0G0J1j0A0T1a1Z0m1W151X17191b1Y20222Q231c29240i2b2S180C212c2d2T2U2e1y1D1H1I2V2f1U2l110z0Y0Z0X0O0I2n0D0E0x0y0L0K2m2W2k323134332o2p1d1z1T2r352t13122s102u363a1V382w2v0W2x3b0q1A1h1g2q0r2y2z1p0k3z1q1F1u1M0u1G0v2B2A2D3E1R391e1L1f1J1t1m2C2E2F3c2G2H2J2R1i372a2I2N3F3B1S3d1C1B3A3f3g2K3h2P3i3j3k2O3l2L2M2j2Y3e3G4i2X2i2g2h30262Z3W3m4j3H4k3X3Y3Z3r1K1E3u403I4l3K4143424m493o3L4b4o4a4c4e4d4p4q274t3C3t3s3q3p3P3O4s3v4f4W443w1v3x4A4r4u3y283M3N3Q4B4C4n253D454E4F4H4G3R4N464P3S4Q4O3n1Q4D474S1O4R4T3T4v4I4U3U4w4J5F4g1k3J4K1P4V3V4x484y4L4z4h4M4Y5051524X5356594Z585457555b5a5c5d5f5h5J5K5H5G5L5e5Q5N5i5k5M5R5I5S5V5U5l5g5j5W5m605P5T5O5n5Y5o615p5r5Z6v6q5q5s5t5u5x5y5X5v6w625w5z6l6x6m6y6n6z6B6o5C6365665A5B676d68696C6G645E5D6A6F6a797a6N6b7b6c6p7c6D6E6H6e6O6P6f6Q6R7d6r7f6S6U6T6I707g726i71736J7574766h6g7j7h7i7e7k7N6j6k6s6V7r7l6W7s7t6K6L6t7m7u6X7v6Y7n7w7y7x7o7E7z7G7F7H7A7J7I7B7L8w6M7p6Z7M6u777C7q787D7P7V7W7Y7K7R7S7O7T7U7Q7Z808381827X8486888A8B8x8C8y8F8G858b898D8I8z8J8M8L8a8c878N8R8E8K8H8d8P8f8e9c8S8Q8O8g8h8i8j8k9m9h8l9n8m9d8n9e8q8t8T8U8V8u8s8v8ra08W8X8Y9Ea19o8Z909Fa29G8o8p9H9I91a392a4939f9Ja5969L9K9p9R9g9T9S9U9994a6a79W9V9q9X98979sa89tabaaa99v959u9w9x9b9aaEacaiajakal9jad9y9iam9Mae9k9zanapao9AavafaxawayaAaqaz9raB9BaraC9C9l9Nas9O9D9Pagat9Q9ZahaDbn9YaGaPaIauaJaOaFaKaLaRaHaQaSaMaNaTaUaVaZaWaXbpbvbrbsb2b0bobtbubzc8bAbDbqbCb1aYb3bEb4bIbBbwbyb5bGbJbxb6b7bHb9c3c9b8babbbccdbKbdcebec4bhbFbkbLbNbMbObmbibjblcvbPcRcfc5cSbQbRbSbTcwcxcTbfbVbgcybUcUczcAcCc0cBcVcIcXcgcKcJcLbXc6cMcNcYchcOcjd2d1cZd0c2c1bZbYckdvcad9bWd3c7cDcbcccEcWcncodadbdcddd4dedgdfclcmdmcpdodndpcqdrdhdqdtcGcrd5dicQcsdjcidscFd6ctebducudkd7cHcPd8dxdDdGdzdAdwdBdldydCdHdJdEdIdFdKdLdMdOefegehdQdNeddTdRekeceieneeeoereqdUdSdPelepejesdVewdWeuexetdXdZdYe0eTe2e1eveyeUe3e4emeOe5ePeQeRezeAe8eVeBeCe7eDeEeFeSeGeHeLeae6eWeIe9eYeNeXeMeZeKeJf0f1f2f9f3f4faf5fbfkf6fcf7flfdfefffgfhfif8fmfj"
 DIGITS = "0123456789abcdefghijklmnopqrstuvwxyzABCDEFGHIJKLMNOPQRSTUVWXYZ"
 
 
@@ -73,7 +86,7 @@ def build_ops():
     ops = []
     cur = ["-"]
     seen = {}
-    flex = [0]
+    flex = [0, 0]
     A = AluOpType
     AF = ActivationFunctionType
 
@@ -93,6 +106,21 @@ def build_ops():
 
     def copy(out, x):
         add("v", "copy", (out, x), [x], [out])
+
+    def lin(out, x, plus=None, mul=None):
+        e = LIN[flex[1]]
+        flex[1] += 1
+        if e == "a":
+            act(out, x, AF.Copy if plus is None else AF.Identity, plus, mul)
+        elif plus is not None:
+            ts(out, x, plus, A.add)
+        elif mul is not None:
+            ts(out, x, mul, A.mult)
+        elif x[0] == "ML":
+            ts(out, x, 0.25, A.add)
+        else:
+            copy(out, x)
+        ops[-1]["lin"] = True
 
     def tt(out, x, y, op):
         add("v", "tt", (out, x, y, op), [x, y], [out])
@@ -154,7 +182,7 @@ def build_ops():
     def blk(buf, m, b):
         return ap(buf, m * 8 * BLK + b * BLK, m * 8 * BLK + b * BLK + BLK)
 
-    z1 = 128
+    z1 = 0
     for e, name, out in (("s", "z0", ap("ZB", z1, z1 + 128)), ("s", "cb", ap("CBI", 0, 8)), ("a", "ka", ap("KAI", 0, 1)),
                          ("a", "le", ap("LEI", 0, 256)), ("s", "ad", ap("ADI", 0, 1024)), ("s", "vf", ap("W", 0, 2048)),
                          ("a", "th", ap("THI", 0, 1))):
@@ -190,7 +218,13 @@ def build_ops():
     iota(ap("SELE", 1024, 2048), [[0, 1024]], 0, 0)
     for k in range(16):
         act(ap("SELE", 129 * k, 128 * k + 128, 16), ap("BO", 0, 128, 16), AF.Copy)
-    ts(KA1, ap("KAI", 0, 1), 1184.0, A.add)
+    ts(ap("COLI", 8, 9), ap("KAI", 0, 1), 1184.0, A.add)
+    ts(ap("COLI", 9, 10), ap("COLI", 8, 9), 63, A.bitwise_and)
+    ts(ap("COLI", 10, 11), ap("COLI", 8, 9), 8128, A.bitwise_and)
+    copy(ap("COL", 13, 15), ap("COLI", 9, 11))
+    act(full("KL"), full("ID"), AF.Copy, None, col(13))
+    act(full("KH"), full("ID"), AF.Copy, None, col(14))
+    act(full("IDH"), full("ID"), AF.Copy, None, CS)
     ts(ap("COLI", 3, 4), ap("KAI", 0, 1), 15, A.bitwise_and)
     ts(K2, ap("COLI", 3, 4), 2048.0, A.mult)
     copy(TH, ap("THI", 0, 1))
@@ -199,6 +233,7 @@ def build_ops():
     act(full("NEG"), full("ID"), AF.Copy, None, -4096.0)
     act(full("DK"), full("ID"), AF.Copy, None, K16)
     act(full("MH"), full("ID"), AF.Copy, None, -0.5)
+    act(full("NID"), full("ID"), AF.Copy, None, -1.0)
     act(full("M32"), full("ID"), AF.Copy, None, -32.0)
     memset(ap("QC", 0, 64), 0.25)
     iota(ap("BASE", 0, 144), [[16, 144]], 2032, 0)
@@ -223,17 +258,17 @@ def build_ops():
         iota(ap("RD", 8 * b * (b + 1), 8 * b * (b + 1) + TRI + 1, TRI), [[0, 2]], 4096, 0)
     iota(ap("AD", 1024, 1152), [[0, 128]], 0, 0)
     for m in range(1, STEPS):
-        iota(ap("MS", (m - 1) * 8 * BLK + 4, m * 8 * BLK, FLD), [[0, 128]], 0, 0)
+        act(ap("MS", (m - 1) * 8 * BLK + 4, m * 8 * BLK, FLD), full("JM"), AF.Copy)
     copy(ap("LE", 0, 256), ap("LEI", 0, 256))
     for j in range(0, 1024, 256):
         copy(ap("AD", j, j + 256), ap("ADI", j, j + 256))
 
-    ts(lst("ML", 0, 0, 8), ap("CBI", 0, 8), CS, A.mult)
+    copy(lst("ML", 0, 0, 8), ap("CBI", 0, 8))
     copy(ap("CF", 0, 8), ap("CBI", 0, 8))
     tt(full("CE"), ind(ap("CF", 0, 8), ap("LC", 0, 8)), full("M1"), A.mult)
     mm([(ap("PU1", 0, 128), [(full("WU"), ap("ZB", z1, z1 + 128))])])
     mm([(ap("PU0", 0, 128), [(full("BO"), full("CE"))])])
-    act(ap("ML", 2, 8 * BLK, FLD), ap("PU0", 0, 128), AF.Copy, None, CS)
+    act(ap("ML", 2, 8 * BLK, FLD), ap("PU0", 0, 128), AF.Copy)
     copy(full("Y"), ap("PU1", 0, 128))
     ts(full("YU"), full("Y"), 4095, A.bitwise_and)
     ts(ap("ML", 1, 8 * BLK, FLD), full("YU"), -2048.0, A.add)
@@ -256,20 +291,22 @@ def build_ops():
             if m > 1:
                 add("n", "recv", (m - 1, h), [ap("TOK", 2 * m + h - 2, 2 * m + h - 1)],
                     [blk("ML", m - 1, b) for b in range(4 * h, 4 * h + 4) if (b + m - 1) % NR], "arr%d_%d" % (m - 1, h))
-                act(hs("ZB", h, q), fld("ML", m - 1, h, 0), AF.Copy)
-                act(hs("AB", h, q), fld("ML", m - 1, h, 3), AF.Copy)
+            zh = hs("ZB", h) if m == 1 else fld("ML", m - 1, h, 0)
+            ah = fld("ML", m - 1, h, 3)
             c16 = ap("C16", q8 + 4 * h, q8 + 4 * h + 4)
-            ts(c16, lst("ML", m - 1, 4 * h, 4 * h + 4), 1.0 / CS, A.mult, 0.25, A.add)
+            lin(c16, lst("ML", m - 1, 4 * h, 4 * h + 4))
+            act(ap("CL", q8 + 4 * h, q8 + 4 * h + 4), lst("ML", m - 1, 4 * h, 4 * h + 4), AF.Copy, None, CS)
             copy(hs("S16", h, q), ind(lew, c16))
-            act(ap(PN, 64, 128), fld("ML", m - 1, h, 1), AF.Identity, K2, KA1)
-            tt(hs("PI", h), ap(PN, 64, 128), fld("ML", m - 1, h, 2), A.add)
+            mm([(ap(PN, 64, 128), [(full("KH"), fld("ML", m - 1, h, 1)), (full("KL"), fld("ML", m - 1, h, 1)),
+                                   (full("IDH"), fld("ML", m - 1, h, 2))])])
+            lin(hs("PI", h), ap(PN, 64, 128), K2)
             ts(hs("AI", h, q), hs("PI", h), 5, A.arith_shift_right, 1023, A.bitwise_and)
-            copy(hs("A16", h, q), hs("AI", h, q))
+            lin(hs("A16", h, q), hs("AI", h, q))
             for b in range(4 * h, 4 * h + 4):
                 o = 8 * b * (b + 1)
                 a0 = (m - 1) * 8 * BLK
                 act(ap("DD", o, o + 16 * b + 16), ap("ML", a0 + 2, a0 + (b + 1) * BLK, FLD), AF.Abs,
-                    ap("ML", a0 + b * BLK + 4, a0 + b * BLK + 5), -1.0)
+                    ap("CL", q8 + b, q8 + b + 1), -CS)
             for t0, t1 in quarters:
                 if m == 1:
                     copy(ap("G", 16 * t0, 16 * t1), ind(ap("ADI", 0, 1024), ap("A16", q + t0, q + t1)))
@@ -279,13 +316,21 @@ def build_ops():
                 gather(ap("W", 2048 + 16 * t0, 2048 + 16 * t1), ind(VFW, ap("S16", q + t0, q + t1)))
             mm([(ap(PN, 0, 64), [(ap("SELN", 128 * k, 128 * k + 128), ap("G", 1024 * h + k, 1024 * h + 1024, 16))
                                  for k in range(16)])])
-            copy(hs("N16", h), ap(PN, 0, 64))
+            lin(hs("N16", h), ap(PN, 0, 64))
             act(hs("NF", h), ap(PN, 0, 64), AF.Copy)
             for t0, t1 in quarters:
+                if DQ[t0 // 32] == "a":
+                    act(ap("D", 16 * t0, 16 * t1), ind(VFW, ap("N16", t0, t1)), AF.Copy)
+                    for j in range(2):
+                        c0 = 16 * t0 + 256 * j
+                        pd = ap("PE%d" % (h ^ j ^ 1), 128, 384)
+                        mm([(pd, [(full("NID"), ap("W", 2048 + c0, 2304 + c0)), (full("ID"), ap("D", c0, c0 + 256))])])
+                        act(ap("DA", c0, c0 + 256), pd, AF.Abs)
+                    continue
                 tt(ap("D", 16 * t0, 16 * t1), ind(VFW, ap("N16", t0, t1)), ap("W", 2048 + 16 * t0, 2048 + 16 * t1),
                    A.subtract)
                 act(ap("DA", 16 * t0, 16 * t1), ap("D", 16 * t0, 16 * t1), AF.Abs)
-            pre = [(full("M32"), hs("AB", h, q))] if m > 1 else []
+            pre = [(full("M32"), ah)] if m > 1 else []
             mm([(ap(PE_, 0, 64), pre + [(ap("SELE", 128 * k, 128 * k + 128), ap("DA", 1024 * h + k, 1024 * h + 1024, 16))
                                         for k in range(16)])])
             okh = hs("OK", h)
@@ -301,10 +346,10 @@ def build_ops():
             mm([(r1, [(full("ID"), ap("BASE", 64 * h + 1, 64 * h + 65)), (full("WK"), fh), (full("NEG"), sq)])])
             tt(hs("X1", h), r2, hs("NF", h), A.max)
             tt(hs("X2", h), r1, hs("X1", h), A.max)
-            copy(hs("F16", h), hs("X2", h))
+            lin(hs("F16", h), hs("X2", h))
             if not last:
                 if m > 1:
-                    mm([(ap(PN, 256, 320), [(full("ID"), hs("AB", h, q)), (full("ID"), sq)])])
+                    mm([(ap(PN, 256, 320), [(full("ID"), ah), (full("ID"), sq)])])
                     act(fld("MS", m - 1, h, 3), ap(PN, 256, 320), AF.Copy)
                 else:
                     act(fld("MS", m - 1, h, 3), sq, AF.Copy)
@@ -316,7 +361,7 @@ def build_ops():
         cur[0] = "W"
         scan(ap("RR", 0, TRI), ap("RD", 0, TRI), ap("DD", 0, TRI), A.add, A.min)
         ts(ap("XD", 0, 16), ind(ap("RR", 0, TRI), ap("LP", 2, 3)), KM15, A.not_equal, 2 * BIG, A.mult)
-        tt(ap("YD", 0, 8), ap("XD", 0, 8), lst("ML", m - 1, 0, 8), A.add)
+        tt(ap("YD", 0, 8), ap("XD", 0, 8), ap("CL", q8, q8 + 8), A.add)
         tt(ap("ZD", 0, 8), ap("YD", 0, 8), ap("DUMP", 0, 8), A.min)
         ts(ap("O16", 0, 8), ap("ZD", 0, 8), 1.0 / CS, A.mult, 0.25, A.add)
         for h in range(2):
@@ -353,7 +398,8 @@ def build_ops():
                 ts(ap("O16", o0, o0 + 4), ap("ZD", o0, o0 + 4), 1.0 / CS, A.mult, 0.25, A.add)
                 tt(hs("T1", h), ind(ap("AD", 0, 1152), ap("O16", o0, o0 + 4)), hs("NI", h), A.mult)
             cur[0] = "ab"[h]
-            mm([(ap(PE_, 64, 128), [(full("ID"), hs("ZB", h, q)), (full("ID"), ap("QC", 0, 64)),
+            zh = hs("ZB", h) if m == 1 else fld("ML", m - 1, h, 0)
+            mm([(ap(PE_, 64, 128), [(full("ID"), zh), (full("ID"), ap("QC", 0, 64)),
                                     (full("MH"), ap("MX", 1024 * h + 15, 1024 * h + 1024, 16)),
                                     (full("MH"), ap("MN", 1024 * h + 15, 1024 * h + 1024, 16))])])
             act(hs("ZR", h), ap(PE_, 64, 128), AF.Identity, MGP)
@@ -365,22 +411,22 @@ def build_ops():
             else:
                 mm([masked])
             scan(hs("XS", h), ap("RST", 0, 64), ap(PU, 64, 128), A.max, A.min)
-            copy(ap("Y", y0 + 64, y0 + 68), ap("XS", 64 * h + 15, 64 * h + 64, 16))
+            lin(ap("Y", y0 + 64, y0 + 68), ap("XS", 64 * h + 15, 64 * h + 64, 16))
             lo = y0 + (64 if last else 0)
             if not last:
-                copy(ap("Y", y0, y0 + 64), ap(PU, 0, 64))
+                lin(ap("Y", y0, y0 + 64), ap(PU, 0, 64))
             ts(ap("YL", lo, y0 + 68), ap("Y", lo, y0 + 68), 15, A.bitwise_and)
             tt(ap("WF", lo, y0 + 68), ap("YL", lo, y0 + 68), ap(PU, 256 + lo - y0, 324), A.add)
-            copy(ap("W16", 4 * h, 4 * h + 4), ap("WF", y0 + 64, y0 + 68))
+            lin(ap("W16", 4 * h, 4 * h + 4), ap("WF", y0 + 64, y0 + 68))
             if not last:
                 tt(hs("T2", h), ap("WF", y0, y0 + 64), ii, A.mult)
                 tt(ind(ap("AD", 0, 1152), ap("O16", 8 + 4 * h, 12 + 4 * h)), hs("T1", h), hs("T2", h), A.add)
                 ts(ap("YU", y0, y0 + 68), ap("Y", y0, y0 + 68), 4095, A.bitwise_and)
                 ts(fld("MS", m - 1, h, 1), ap("YU", y0, y0 + 64), -2048.0, A.add)
-                ts(ap("YM", y0, y0 + 68), ap("YU", y0, y0 + 68), 1103.0, A.mult)
+                lin(ap("YM", y0, y0 + 68), ap("YU", y0, y0 + 68), None, 1103.0)
                 ts(ap("YC", y0, y0 + 68), ap("YM", y0, y0 + 68), 4, A.arith_shift_right, 255, A.bitwise_and)
-                ts(fld("MS", m - 1, h, 2), ap("YC", y0, y0 + 64), CS, A.mult)
-                ts(lst("MS", m - 1, 4 * h, 4 * h + 4), ap("YC", y0 + 64, y0 + 68), CS, A.mult)
+                lin(fld("MS", m - 1, h, 2), ap("YC", y0, y0 + 64))
+                lin(lst("MS", m - 1, 4 * h, 4 * h + 4), ap("YC", y0 + 64, y0 + 68))
                 away = []
                 for b in range(4 * h, 4 * h + 4):
                     if (b + m) % NR:
@@ -562,16 +608,16 @@ def rank_program(g, core, T, topo):
             m, h = a
             mine = routes(T, topo, m, h)[rank]
             em = engine_masks(topo, core, mine)
-            trs = []
+            trs = {True: [], False: []}
             for b, dst, via in mine:
                 rid, pid = topo.addr(dst if via is None else via, core)
-                trs.append(RemoteDMATransfer(
+                trs[via is None].append(RemoteDMATransfer(
                     dst_ids=[DstId(rid=rid, pnc=pid)], dma_engine_mask=as_mask(em[b]),
                     remote_sem=T.sem["arr%d_%d" % (m, h)],
                     src=T["MS"][:, (m - 1) * 8 * BLK + b * BLK:(m - 1) * 8 * BLK + b * BLK + BLK],
                     dst=T["ML"][:, m * 8 * BLK + b * BLK:m * 8 * BLK + b * BLK + BLK]))
                 sent += len(em[b])
-            g.remote_dma_fused(trs, local_sem=T.sem["sent"])
+            g.remote_dma_fused(trs[False] + trs[True], local_sem=T.sem["sent"])
             done[i] = ("none", 0, {})
             continue
         if k == "mm":

@@ -2,38 +2,35 @@ from concourse.bass import DstId, RemoteDMATransfer
 from concourse.mybir import AluOpType, ActivationFunctionType
 
 F32, BF, F16, I32, U16 = "float32", "bfloat16", "float16", "int32", "uint16"
-STEPS, NR, HALF, FLD = 5, 8, 64, 5
-BLK = 16 * FLD
-CS = 19616.0
+STEPS, NR, HALF = 5, 8, 64
+BLK = 32
+SLOT = 8 * BLK
+SEG = 66
 BIG = float(2 ** 25)
-MAGIC = 12582912.0
-TRI = 576
+MAGIC = 1.5 * 2 ** 23
+HALVES = (1, 0)
 
 _S = {
-    "W": (BF, 4096), "ADI": (I32, 1024), "LEI": (I32, 256), "AD": (F32, 1152), "LE": (F32, 384),
+    "W": (BF, 4096), "ADI": (I32, 1024), "LEI": (I32, 256), "AD": (F32, 1088), "LE": (F32, 320),
     "G": (F16, 2048), "D": (BF, 2048), "DA": (BF, 2048), "FV": (BF, 2048), "MX": (BF, 2048), "MN": (BF, 2048),
-    "SELN": (BF, 2048), "SELE": (BF, 2048),
-    "ML": (F16, 5 * 8 * BLK), "MS": (F16, 4 * 8 * BLK),
-    "KH": (BF, 128), "NID": (BF, 128), "KL": (BF, 128), "IDH": (F16, 128), "CL": (F32, 16),
-    "CBI": (I32, 8), "KAI": (I32, 8), "THI": (I32, 8), "CF": (F32, 8), "COL": (F32, 16), "COLI": (I32, 16),
-    "JM": (F32, 128), "JG": (F32, 128), "TMP": (F32, 8), "IOT": (I32, 8), "IOF": (F32, 16), "MK": (F32, 16),
-    "ID": (BF, 128), "BO": (BF, 128), "BOH": (F16, 128), "TR": (BF, 128), "WK": (BF, 128), "WU": (BF, 128),
-    "NEG": (BF, 128), "DK": (BF, 128), "MH": (BF, 128), "BM": (BF, 64), "M1": (BF, 128), "QC": (BF, 64),
-    "M32": (BF, 128), "CE": (BF, 128), "CE2": (BF, 128),
-    "BASE": (BF, 144), "KEEP": (BF, 512), "RST": (BF, 512), "CMP": (F32, 128), "T16": (F32, 128), "DUMP": (F32, 16),
-    "RD": (BF, 2 * TRI), "DD": (BF, 2 * TRI), "RR": (BF, 2 * TRI),
-    "LB": (U16, 8), "LC": (U16, 8), "LP": (U16, 8),
-    "C16": (U16, 16), "S16": (U16, 256), "A16": (U16, 256), "N16": (U16, 128), "F16": (U16, 128), "W16": (U16, 8),
-    "O16": (U16, 16),
-    "PI": (I32, 128), "AI": (I32, 256), "ZB": (BF, 128), "NF": (F32, 128),
-    "OK": (BF, 128), "FL": (BF, 256), "X1": (F32, 128), "X2": (F32, 128), "ZR": (F32, 128), "Z16": (BF, 128),
-    "XS": (F32, 128), "Y": (I32, 144), "YU": (I32, 144), "YM": (I32, 144), "YC": (I32, 144), "YL": (I32, 144),
-    "WF": (F32, 144),
-    "KEY": (F32, 128), "KT": (F32, 128), "KS": (F32, 128), "IT": (F32, 128), "NI": (F32, 128),
-    "IA": (F16, 128), "AL": (F32, 128), "XD": (F32, 48), "YD": (F32, 16), "ZD": (F32, 16),
-    "SN": (F32, 128), "SO": (F32, 128), "T1": (F32, 128), "T2": (F32, 128),
+    "SELN": (BF, 2048), "EE": (BF, 144), "ML": (F16, 5 * SLOT), "MS": (F16, 5 * SLOT),
+    "CBI": (I32, 8), "KAI": (I32, 8), "THI": (I32, 8), "CF": (F32, 8), "COL": (F32, 32), "COLI": (I32, 16),
+    "JJ": (BF, 256), "JM": (BF, 128), "JG": (BF, 128), "JP": (BF, 8 * SEG), "IOT": (I32, 8), "IOF": (F32, 8),
+    "MK": (F32, 16), "CT": (BF, 512), "CA": (F16, 64), "T01": (BF, 128),
+    "WP": (F16, 128), "WN": (F16, 128), "BT": (F16, 256), "AP": (F16, 256), "AN": (F16, 256),
+    "BM": (BF, 64), "M16": (BF, 128), "CE": (BF, 128), "CE2": (BF, 128), "TB": (BF, 192), "BASE": (BF, 144),
+    "KEEP": (BF, 512), "RST": (BF, 512), "CMP": (BF, 128),
+    "RD": (F16, 8 * SEG), "DD": (F16, 16 * SEG), "RR": (F16, 16 * SEG),
+    "LB": (U16, 8), "LC": (U16, 8), "C16": (U16, 8), "S16": (U16, 128), "A16": (U16, 128), "N16": (U16, 128),
+    "F16": (U16, 128), "W16": (U16, 8), "O16": (U16, 16),
+    "ZB": (BF, 128), "SF": (F16, 128), "NF": (F16, 128), "OK": (BF, 128), "FL": (BF, 256), "X1": (F32, 128),
+    "X2": (F32, 128), "Z16": (BF, 128), "XS": (F32, 128), "LV": (F32, 256),
+    "KEY": (F32, 128), "KT": (F32, 128), "KS": (F32, 128), "IT": (BF, 128), "II": (BF, 128), "IA": (F16, 128),
+    "AL": (F32, 256), "T1": (F32, 128), "T2": (F32, 128),
 }
-PS = ["PN0", "PN1", "PE0", "PE1", "PF0", "PF1", "PU0", "PU1"]
+for _n in ("ID", "NID", "MH", "BO", "TR", "WK", "DK", "NEG", "POS", "B32", "S32", "SC", "SU", "D4"):
+    _S[_n] = (BF, 128)
+PS = [b + h for b in ("PA", "PB", "PC", "PD") for h in "01"]
 SCRATCH = {}
 for _n in _S:
     SCRATCH[_n] = ("sbuf", [128, _S[_n][1]], _S[_n][0])
@@ -46,21 +43,11 @@ SEMAPHORES = ["cv", "ca", "cp", "cg", "sent"] + ["ld_" + x for x in LOADS] + ["s
     ["arr%d_%d" % (m, h) for m in range(1, STEPS) for h in range(2)]
 CNT = {"v": "cv", "a": "ca", "p": "cp", "g": "cg"}
 
-ENG = "aaaaaaaavaavvavaaaaavaavvavaavaavaavaaaavaaavaavaavaaaaa"
-ORDER = "0102071k03051e000608040c0b0M090d0a1l0e0n180o0j0g0q0t1q0h0p1g0P0S0N0f1a1p0x0m1h0J0l0s0I1s150E1P1S140A1Q160D1R0y0w1V1T2F0K1W0R220F1X1U2G2H23241f0Q250Y2I0H262J0L1i270G2K2c120B2e2d0u0z0Z0v130C2S2Q2g1w2f2P2h0U172T0V2l0O112R1B2j1A0W1C0X1D100T1z2m1y1x2U1j1E2W192k1G1m2N2n1b2Y2L1n2i2X1F1H282o1N2Z2q1I2r2s3n2O2t1J2u1L2a302M2v2b1r292w2V0i2p2x1t1M2z311K3334350k3s362C371u383t391v3a2B2A1c3f2D2E3o3K3i323L3g3M3c3h3O463P3R3Q3j3X472y3Z3N3Y401Z3S1Y411o420r3e433b213d201d3p4o3u3k3T4p1O4q4K4r3v4s3l3w4t3x3y4v4u3U4B3z4D3A4C3B4E3m3C4F3D4G484H4I4w494x4a3E4b4c4y3F3V4d3G3r4e4g5r4f4J4h3H4i3I4j3J443q4k454l4z4m3W4n4A4P4M4Q4U4N4W4R4V4T4S4L4O4Y4X4Z50515u5w525B5x5D5v5A5y5H5z545F5E5G565I555J5L575C58535N5M5t5K5s59685O5b5c5d6d5a5e5f695P5g6a5h6b5i6c5l5o5j5Q5k5m5R5S5T5q5n5p6f6A6e6i6h6B6C5U6D6E6j6g5V5W6F606H6G5X616N5Y6P5Z6Q656O6R6S6k6T6W6l6X6m6I6Y6o626J6p667A676Z6r636t6q6s646n716K707e6V727f6u6U7g7h7i6v737j777l7k766w7r747m757t7s7u6L7v7w7n787x7y6x7o6y796z7a6M8h7z7b7p7c7d7q7D7F7C7G7B7E7M7L7H7K7J7I7N7O7Q7P7R7S7T7U7W7V8m8j8i8n8k7X8o8l8p8u8v7Y8x8w8y7Z8z8081828A8D8r8q8t8s8B8E838C93848598898699878a8F888b8e8G8g8H8I8J8K8c8L8M8Q8N9M8O8R9N8P8d8V8f9a9q9b9c9r8X9e9s8S8W9u9v9x9w9f9D9y9t9F9h9E9G9i9z9g9I9j9H9d8T9J8U94a4958Ya5a69Oaqa79Ba89P8Z9Ra9abaa9Qah9S9Aajaiak9Tal9Wam9k9Vao909l9X919U9m96an9nac9o9Y9pb79Zada09Ka1aea29Cafa392ag97ap9LatavasawazauaAaCaxaFayaGaEaDaBaraHbabcb9bdbhbjbebgbfb8bbblaIaKbkaMbnbobmaLbpbtaNaJaObqbrbubiaPbTbsaRbVaSaTbUaQaUaVbvaWbYaXbZaYbOb1c0aZbwc1bybWbzbPbAb4b3bBbCbGb2bDc2bEb0bQbxbFb5c4bLb6cCc5cgcDbRcEchbMcibIbNckclcncmbSctcFcjcvc7cucwc9cGc8cyc6cxbHbJc3czcIcHbKcacUcocbcpcccVcqcdcWcJdgcXcecrcYcMcfcKcLcZd1cNd0d7d2d9d8dad3dcdbbXddded4cBcOcAdUdfcPd5cQcscRcScTd6djdldqdkdidrdmdvdndodtdudwe3dxdsdpdhdXdZdWe0e4dYe6e1dyeae2e7e8dAe9ebdCdBecegdDdzdEedeeehe5dVdFeDefdGeFdHdIeEdJdKeidLdMdNeydOezejeAekeGeleBemdReCeneoepeqereHevdTdQdPesdSexeIeweJeteKeueLeMeTeNeOeUePeVeQeWf4eReXf5eYeZf0f1f2eSf6f3"
-ENG = "aaaaaaaaavavvaavaaaavaavvavaaaaaavaavaavaaaaavaaaaavaaaa"
-ORDER = "0002071m0103050608040c0b1q090d1r0e0o0n1k0q0t0f1M1v0j1w0a0m0p0g0N0M1a0H0G0D0h0l0I1n0L141Y1W0B16210x150P1X0Q0R0C17221Z191b1V181c23201l2M0F282b0S2O2P0A0u2a0z2c2Q0K2d0J2R0v2e0Y2S2l2j1o0w2k0E2Z1C2Y0y302n2X2m2o1d312q1e0X1f101G110U1K0O1H122s0Z1E0T1D0V1F2r1J1I1s320W0i13362t1t1L1h2u2p34331g37292v1R352x2y2z1S1i2A2B2w382C2N1x0r2D2h1y2E0s1z0k2G1T1U1p1B393v2J3b1A3c2I2H3x3a2i2L2F2f2K2U2V3d2g3S2T3A2W3w3e3f4e3T3g1u3B3U3h3V4f3j3W3i263C3k3X3Z3Y3D453E473G46483n404a493m4b3l24253o273F3p1j1N3H4S4g4w3I3q3L4x3J4h4y3r4i3K1Q4z4A4j4k1O4B1P4D4C3s4J3t4L414M4K4N4O3M424P4Q3u3N4l3y4n3O3z4p4m4o3P4E3Q5y4F4c4d4q434r3R4s444t4G4u4H4v4R4I4U4W534X524T504Y514V4Z5455575658595a5b5A5C5G5I5d5J5c5H5D5z5e5E5F5B5L5K5f6e5M5O5g6j6f6k6g5i5N5j5P5k5R5l5m5q5h5Q5r5n5T5S5o6o5U5p6p5s5v5V6h5t5u5X5x5W5w5Y5Z606G6q6162726H66636i6I646J73676K656r686L6N6M6s6T6u6O6V6U6W6b6P6X6Y6l6Z6a696t6c6d7G6Q6m7k74707l7m6n7n7o6v7p6z7r6x7q6w756y7x767z77787y7A6A7B7C717D7E7s6B7t796C7u7a6D7c6R7b6E7F7d8m6F7e7v7f7g6S7h7i7j7w7H7I7K7Q7L7R7P7M7O7J7N7S7T7V7U7W7X7Y7Z8o8q8v818u8w808r8n828s8t8p8y8z83978x8C848A92989386878D8B888F898a8e8E858b8H8G8f8c948I8d958g8j8J968h8i8L8k8K8l8M8N8O9u9c9Q8P8Q9d9v8U8R9R9w8S9x8V9y8T8Z9z9B9A9H9C9J9I9K8W9D9L9M919N909E8X8Yau99a89S9ea99T9faa9aab9gac9U9h9i9Vadafae9jal9nag9manam9l9kaoahap9Waq9Oaras9o9X9pa1ai9q9Y9Fa09raj9Z9satba9b9ta2a3a4a59P9Ga6a7akawayaDazaFavaEaAaCaxaBaGaHaIaKaJaLaNbebcaMbiaPblbjaObfbbaQbgbhbnbmaRbdbkbVbqboaSbQbWbRaUaVbrbpaWbtaXaYb2aTbsaZbvbub3b0c0bwb1c1b4b7bxbSb6b8bzb9byb5bAbBbCcic2bDbEcEcjbIbFc3ckbGclc4cmbHbTc5c6bNcncpcoc7cvcFcxcwcybKbUczcAbPcBbOcqcbc8bLc9cabMbJdicccGcWcrcHcdcXcIcscYcecZctcJd0bXcKcfd1d3d2cLd9cPd4dbcMdacNdcd5cOdddecQdfdgcgbZbYcRcDchdVcScud7cTcCd6cUdhcVd8djdkdmdldtdrdndsdqdodpdudvdwdydxdzdBdZdXdAe6e0dWdCe1e2dYe8e7dDe9ebeDdEeceeeadFe4ege3e5efeddGeyehdHdIdJeEdKeFdLeidMezdNeAdOeBdSeCejeHekelemdPeGeneoepeqerdUevdQdRdTesexeIeweJeteKeueLeMeTeNeOeUePeVeQeWf4eReXf5eYeZf0f1f2eSf6f3"
-LIN = "v" * 200
-DQ = "vvav"
-ENG = "aaaaaaaaavavvaavaaaavaavvavaaaaaavaavaavaaaaavavaaavaaaa"
-ORDER = "010002071m080b0c0d1r0e0n0o031q090j0g0l0q1M0t0p060J0C0H1l0a0f0M0T0R0m1w1v1n0h1k0L0N1L1s1C1J1o1t1e0u1E0v1H1F1D1I141Y1W151621170F0x0A0Q1a0S0I18191X1Z201V1b222M231c282b2P2O2a2c2Q2d2R2e2S0G0E0z0X0B110Z0Y0D0w0O0y042k2j052m0U0K2Z102l2Y2X2n300V132o312q2s2r0P0W321d362t122u3433371h2N2p291g2g2i0r1u2v1R0i2x2y2z1S2A2B352f382C1x2D1y2E1T3x1p1U2G3v2I0k393c3b2J2h2W1i2w2V1z272H0s2K2L3A3d3S3a2U3B3w4e3e3f3g1B3T1f2F3U3h3V4f3i3W1A3C3k3X3Z3Y3D453E473G46483n1O1j2T40494a3m3l3o3p4b4S4w244x4y4g3H1G1K3q1Q4h3r4i4A3j3J4k4B4D4C3s4J3t4L4z251N414M3u4K4O263K3I3L3M4N423y3N4l433O3z3P4c3Q4Q5y4j4m4p4o4n3F4q4E4r3R4s4d444t4F4u4H4G4v4R4I4W4X4Y4T4Z4V4U51534P501P5455575658595a525A5b5C5d5c5I5D5e6j5E5z5F5B5L5K5J5G5H5f5M5O5g6e6k6f6g5i5N5j5P5k5m5q5R5l5n5T5S5h5Q5o6o5U5p5v6p5s6h5t5u5x5V5W5w5Y5Z6G606q6i61625X5r6H6I6K6372646r65736J686L6N6M6s6T6O6V6U6W6b6P6X6Y6Z696a6l6c6d7G6Q6m6u706v74667k7l7m7o6n7p7r7q756x6w6t7n6y6z7x767z787y7A6A677B7C7E7s6B7t797a716C7u6D7F8m6E777d7c7b7e6F7f6R7g7v7h6S7i7j7w7I7P7R7K7L7M7H7N7Q7O7T7J7S7V7U7W7X7Z7Y7D8o8q81808w8n978r8s828v8t8y8p8z83848x8u9892938C8A86878D8B888a898e8F8G8E8b8H8c8d948g958f8I8h8i858j8k8J8K8l968M8N8O9u8P8Q8L9Q8R9c8S8T9v9w8U9y9x9d8Z9z9B9A9R9H9C9J9I9K8W9D9M9L9N90919Eau8X8Ya8a9aa9e9S999T9fab9U9a9gac9iadafae9j8Valaganamaoahapaq9W9Oas9l9m9k9h9n9o9X9Y9p9Fai9q9b9rbaa1a09Za29sa3aja49ta5ata69G9P9Va7akawaDaFaCayazaAaBavaHaGaraEaxaIaKaJaLaNbeaMbcaOaPbbbjaQbfbgbhbdbnbibmaRaSbVblbkbqbobQbWbRaUaVbrbpaWb2aXaYbtbuaTaZbvb0c0bwb1c1b4b7bsbxbSb6b9b8byb5bAbBbCcic2bDbEbzcjckbFcEbGc3b3clbHc4bTbIcmc6bNcncpcoc7cvcFcxcwcybKbUcAczbPbOcBbLbMdicqcac8c9cbcccGcWcrcdcXcYcHcecscIctbXcfd0cKd1d3d2cLcMcZbJcJcNcPcOc5d9d4dbdadcd5dddedgcgbZd7chcQcCcRdVbYcScucTd6cUcDcVdhd8dmdndjdodldkdrdtdpdudsdvdwdqdfdydxdzdBdZdAdXe6e0e1dWe2dYdCe8e7dDe9ebeceDdEeeeadFegede4e3e5efdGeydHdIdJeEezdKdLeheidMdNeAdOeBeFeCeHejeGekelemdPdSeneoepeqerevesdQdUdTdReIewexeJeteueKeLeMeTeNeOeUePeVf4eQeWeRf5eXeYeZf0f1f2eSf6f3"
-DQ = "vavv"
-LIN = "vvvvvvvvvvvvvvvvvvavavvvavvvvvvvvvvvvvvvavvvvvvvvvvvvvvvvvvvvvavvavvavvvvvvvvvvvvvvvavavvvavvvvvvvvvvv"
-ENG = "aaaaaaaavavaaaavavaavavaavavavaavavaavavavaavavaaaavavaa"
-ORDER = "040102001s070b0c1l0d0o060n03091N0M080e0R0j0g1n1r0f0m1o1w0l0a0t0N0Q0V0U0p0P0h1x0G1a0w0B1Z141X1y1Y2215200J0H1j0T0z0S0O161z1W1723291b242Q1c2S2119182c0A0Y0I0K130E0L0F0y0C2b2T2U2d0u1e1D1p1u0v052V2e1V2f1d2l2m2W2k31322n0Z0D0x11342o332p0s352r2t1T360W0X122s2u3a0i381U2w102v2x1A1h2q2y3b2z3z0k1K1f1F1L1t1G1H1I1J1M1m2B392C2D1R1g2E0q2F3c2G2R2A371B2H1q1i2J0r2a2I2N1S3B3E3d3F1C3A3f3g2K3h2P3i3j3k2O3l2h2Y2g2M2L2i3e2X4i2Z2j303G3W3X4j3H3m4k4l3I3Y3r3Z1E3u403K4143424m493o3L4b4c4o4a4e4d4f4p3C3v3s3p3M4q3P3O4s4r3N3q3t4t1v28264W3Q3w443x4A3y25454B4C3D1Q3n3J4D4E4u4F4H4G3R4N464P3S4Q4O4n274R1P3T4S474U4g4I3U4v3V4J4w4T1k4K5F484x4V4y4L4z4h4M4Y1O565550514X52534Z5859545a5b575c5d5f5h5J5K5H5L5G5e5Q5N5i5k5M5R5I5S5V5U5j5g5l5P5O5W5m605T5n5Y5o615p5r5Z6q5q5s5t5u6v5x5v6w5y5X625w5z6l6x6m6y6n6z6o5C63655B5A666B6768696p6A6C6D6G6F645E5D6d6a796N6b7a6c7b6E6H6O6P7c6Q6f6R6r7d7f6I6S6U6T7g70726i71736J7574766h6V6K6g6k6e7h7j7i7k7N6j7r6s7l6W6L7s7t6t7m7n7u6Y7v6X7w7y7x7o7E7z7G7F7H7A7J7B7e7I7L6M7p6Z776u8w7C7M7q7D787K7P7X7W7V7R7S7O7T7U7Z807Q83818284867Y888A8B8C8x858y898F8G8D8b8I8z8J8M8L8c878a8N8R8E8K8H8d8P8S8f8e9c8O8Q8g8h8i9h8j8k9m8l9n8m9d8n9e8q8t8T8U8W8X8o8p8V8u8r8s8va08Y9Ea19o8Z909Fa29G9I919Ha39294a493a69f9J969L9K9R9p9T9S9U9g9W999V9qa79X97989sa89tab95a99u9v9b9aaE9i9jaaa59Mac9x9waiajakal9yamad9k9zaeanapao9AavafaxawayaAaqaz9rar9BasaC9N9C9O9Pat9Dag9Y9Q9lahbn9ZaDaGaOaNaMaIauaJaFaKaLaHaQaSaRaBaTaPaUaVaXaWaZbrbsbtbobpb0bvbub2bzc8bAbDbqbCaYb1b3bBbEb4bIbwbybxb5b7bGbFb6bJb8bHb9c3c9babbbccdbKbdcebec4bhbkbLbmbMbNbOblbibjcvbPcfcRc5bQbfbRcSbVbScwcxcTcybgczbTbUcUcAcCc0cBcVcIcXcgcKcJcLc6cMbXcNcYchcOcjd0d2c1c2ckbYbZcnbWd1cZcodvcad9cldadbcmcid3cDc7cbccd4dcdddedgdfcEdmcpdodndpcqdrcGdqdtdhcrcQcsdid5dsdjcWcFctebcPd6cud7cHdud8dkdxdFdEdDdGdzdAdwdBdldCdydHdJdIdKdLdMdOdQefegdNeheceddRdTekeieneeeoereqdUdPdSelepejemesdVewdWeuexdXdZdYe0eTe1eUe2eteveye3e4eOe5eVePezeQeAe8eReBeCe7eDeEeFeGeSeHeLeWe6eae9eXeIeYeNeMeZeKeJf0f1f2f9f3f4faf5fbf6fcf7fdflfefffgfhfif8fjfmfk"
-LIN = "vvvvvvvvvvvvvvvvvvavavvavvvvvvvvvvavvvvvavvvvvvvvvvvvvvvavvvvvavvaaaavvvvvavvvvvvvvvavavvvavvvvvvvvvvv" + "vv"
-ORDER = "00010504021s070c0b0d090n030o1N060M080e0P0R0g0j0p1w1r0f1l1n0a0t0l1x1o0h140s160N0Q0S0U0V0H0w0F0B0G0J1j0A0T1a1Z0m1W151X17191b1Y20222Q231c29240i2b2S180C212c2d2T2U2e1y1D1H1I2V2f1U2l110z0Y0Z0X0O0I2n0D0E0x0y0L0K2m2W2k323134332o2p1d1z1T2r352t13122s102u363a1V382w2v0W2x3b0q1A1h1g2q0r2y2z1p0k3z1q1F1u1M0u1G0v2B2A2D3E1R391e1L1f1J1t1m2C2E2F3c2G2H2J2R1i372a2I2N3F3B1S3d1C1B3A3f3g2K3h2P3i3j3k2O3l2L2M2j2Y3e3G4i2X2i2g2h30262Z3W3m4j3H4k3X3Y3Z3r1K1E3u403I4l3K4143424m493o3L4b4o4a4c4e4d4p4q274t3C3t3s3q3p3P3O4s3v4f4W443w1v3x4A4r4u3y283M3N3Q4B4C4n253D454E4F4H4G3R4N464P3S4Q4O3n1Q4D474S1O4R4T3T4v4I4U3U4w4J5F4g1k3J4K1P4V3V4x484y4L4z4h4M4Y5051524X5356594Z585457555b5a5c5d5f5h5J5K5H5G5L5e5Q5N5i5k5M5R5I5S5V5U5l5g5j5W5m605P5T5O5n5Y5o615p5r5Z6v6q5q5s5t5u5x5y5X5v6w625w5z6l6x6m6y6n6z6B6o5C6365665A5B676d68696C6G645E5D6A6F6a797a6N6b7b6c6p7c6D6E6H6e6O6P6f6Q6R7d6r7f6S6U6T6I707g726i71736J7574766h6g7j7h7i7e7k7N6j6k6s6V7r7l6W7s7t6K6L6t7m7u6X7v6Y7n7w7y7x7o7E7z7G7F7H7A7J7I7B7L8w6M7p6Z7M6u777C7q787D7P7V7W7Y7K7R7S7O7T7U7Q7Z808381827X8486888A8B8x8C8y8F8G858b898D8I8z8J8M8L8a8c878N8R8E8K8H8d8P8f8e9c8S8Q8O8g8h8i8j8k9m9h8l9n8m9d8n9e8q8t8T8U8V8u8s8v8ra08W8X8Y9Ea19o8Z909Fa29G8o8p9H9I91a392a4939f9Ja5969L9K9p9R9g9T9S9U9994a6a79W9V9q9X98979sa89tabaaa99v959u9w9x9b9aaEacaiajakal9jad9y9iam9Mae9k9zanapao9AavafaxawayaAaqaz9raB9BaraC9C9l9Nas9O9D9Pagat9Q9ZahaDbn9YaGaPaIauaJaOaFaKaLaRaHaQaSaMaNaTaUaVaZaWaXbpbvbrbsb2b0bobtbubzc8bAbDbqbCb1aYb3bEb4bIbBbwbyb5bGbJbxb6b7bHb9c3c9b8babbbccdbKbdcebec4bhbFbkbLbNbMbObmbibjblcvbPcRcfc5cSbQbRbSbTcwcxcTbfbVbgcybUcUczcAcCc0cBcVcIcXcgcKcJcLbXc6cMcNcYchcOcjd2d1cZd0c2c1bZbYckdvcad9bWd3c7cDcbcccEcWcncodadbdcddd4dedgdfclcmdmcpdodndpcqdrdhdqdtcGcrd5dicQcsdjcidscFd6ctebducudkd7cHcPd8dxdDdGdzdAdwdBdldydCdHdJdEdIdFdKdLdMdOefegehdQdNeddTdRekeceieneeeoereqdUdSdPelepejesdVewdWeuexetdXdZdYe0eTe2e1eveyeUe3e4emeOe5ePeQeRezeAe8eVeBeCe7eDeEeFeSeGeHeLeae6eWeIe9eYeNeXeMeZeKeJf0f1f2f9f3f4faf5fbfkf6fcf7flfdfefffgfhfif8fmfj"
-DIGITS = "0123456789abcdefghijklmnopqrstuvwxyzABCDEFGHIJKLMNOPQRSTUVWXYZ"
+CUT = {"G": (32, 32), "S": (32, 32), "F": (32, 32), "D": ((16, "v"), (16, "a"), (16, "v"), (16, "a"))}
+PIN = {}
+ASIDE = ("DD", "KT", "KS", "IT", "II", "IA", "RR", "O16", "T1", "T2", "LV", "KEY", "XS", "W16", "LE", "AD", "PB")
+PLAN = {"cy": 0.95, "pe": 0.5, "ga": 1.56, "sc": 3.8, "hop": 80.0, "send": 800.0, "way": 4000.0, "dma": 2000.0,
+        "bw": 200.0, "look": 200.0, "spare": 0.0, "plus": 200.0, "slip": 30.0, "lead": 2000.0}
 
 
 def ap(n, a, b, s=1):
@@ -84,13 +71,11 @@ def bits(x):
 
 def build_ops():
     ops = []
-    cur = ["-"]
-    seen = {}
-    flex = [0, 0]
+    cur, seen = ["-"], {}
     A = AluOpType
     AF = ActivationFunctionType
 
-    def add(e, kind, args, r, w, sem=None):
+    def add(alt, r, w, sem=None):
         rr = []
         for x in r:
             if isinstance(x, tuple):
@@ -100,71 +85,80 @@ def build_ops():
         for x in w:
             if x[4] is not None:
                 rr.append(x[4])
-        tag = cur[0] + (w[0][0] if w else kind)
+        tag = (w[0][0] if w else "out") + cur[0]
         seen[tag] = seen.get(tag, 0) + 1
-        ops.append({"tag": tag + str(seen[tag]), "e": e, "k": kind, "a": args, "r": rr, "w": w, "sem": sem})
+        tag += str(seen[tag])
+        if tag in PIN and len(alt) > 1:
+            alt = {PIN[tag]: alt[PIN[tag]]}
+        ops.append({"alt": alt, "r": rr, "w": w, "sem": sem, "tag": tag})
+
+    def k_ts(out, x, s1, op0, s2=None, op1=None):
+        return ("ts", (out, x, s1, s2, op0, op1))
+
+    def k_act(out, x, func, bias=None, scale=None):
+        return ("act", (out, x, func, bias, scale))
 
     def copy(out, x):
-        add("v", "copy", (out, x), [x], [out])
+        add({"v": ("copy", (out, x))}, [x], [out])
 
-    def lin(out, x, plus=None, mul=None):
-        e = LIN[flex[1]]
-        flex[1] += 1
-        if e == "a":
-            act(out, x, AF.Copy if plus is None else AF.Identity, plus, mul)
-        elif plus is not None:
-            ts(out, x, plus, A.add)
-        elif mul is not None:
-            ts(out, x, mul, A.mult)
-        elif x[0] == "ML":
-            ts(out, x, 0.25, A.add)
+    def lin(out, x, mul=None, plus=None):
+        if mul is None and plus is None:
+            v = ("copy", (out, x))
+        elif plus is None:
+            v = k_ts(out, x, mul, A.mult)
+        elif mul is None:
+            v = k_ts(out, x, plus, A.add)
         else:
-            copy(out, x)
-        ops[-1]["lin"] = True
+            v = k_ts(out, x, mul, A.mult, plus, A.add)
+        add({"v": v, "a": k_act(out, x, AF.Copy if plus is None else AF.Identity, plus, mul)}, [x, mul, plus], [out])
 
     def tt(out, x, y, op):
-        add("v", "tt", (out, x, y, op), [x, y], [out])
+        add({"v": ("tt", (out, x, y, op))}, [x, y], [out])
 
     def ts(out, x, s1, op0, s2=None, op1=None):
-        add("v", "ts", (out, x, s1, s2, op0, op1), [x, s1, s2], [out])
+        add({"v": k_ts(out, x, s1, op0, s2, op1)}, [x, s1, s2], [out])
 
     def scan(out, d0, d1, op0, op1):
-        add("v", "scan", (out, d0, d1, 0.0, op0, op1), [d0, d1], [out])
+        add({"v": ("scan", (out, d0, d1, 0.0, op0, op1))}, [d0, d1], [out])
 
     def transp(out, x):
-        add("v", "tr", (out, x), [x], [out])
+        add({"v": ("tr", (out, x))}, [x], [out])
 
     def memset(out, val):
-        add("v", "memset", (out, val), [], [out])
+        add({"v": ("memset", (out, val))}, [], [out])
 
     def act(out, x, func, bias=None, scale=None):
-        add("a", "act", (out, x, func, bias, scale), [x, bias, scale], [out])
+        add({"a": k_act(out, x, func, bias, scale)}, [x, bias, scale], [out])
 
     def mm(groups, first=True, final=True):
         lst, r, w = [], [], []
         for out, terms in groups:
             w.append(out)
+            (r if first and final else w).append(ap("lock" + out[0], 0, 1))
             for i, (l, x) in enumerate(terms):
                 lst.append((out, l, x, first and i == 0, final and i == len(terms) - 1))
                 r += [l, x]
-        add("p", "mm", lst, r, w)
+        add({"p": ("mm", lst)}, r, w)
+
+    def mm2(out, early, late):
+        if early:
+            mm([(out, early)], True, False)
+        return lambda: mm([(out, late)], not early, True)
 
     def iota(out, pattern, base, cm):
-        add("g", "iota", (out, pattern, base, cm), [], [out])
+        add({"g": ("iota", (out, pattern, base, cm))}, [], [out])
 
     def asel(out, x, op, fill):
-        add("g", "asel", (out, x, op, fill), [x], [out])
-
-    def gather(out, x):
-        e = ENG[flex[0]]
-        flex[0] += 1
-        if e == "v":
-            copy(out, x)
-        else:
-            act(out, x, AF.Copy)
+        add({"g": ("asel", (out, x, op, fill))}, [x], [out])
 
     def col(j):
         return ap("COL", j, j + 1)
+
+    def coli(j):
+        return ap("COLI", j, j + 1)
+
+    def mk(j):
+        return ap("MK", j, j + 1)
 
     def full(n):
         return ap(n, 0, 128)
@@ -173,273 +167,273 @@ def build_ops():
         return ap(n, o + HALF * h, o + HALF * h + HALF)
 
     def fld(buf, m, h, f):
-        a = m * 8 * BLK + h * 4 * BLK
-        return ap(buf, a + f, a + 4 * BLK, FLD)
-
-    def lst(buf, m, b0, b1):
-        return ap(buf, m * 8 * BLK + b0 * BLK + 4, m * 8 * BLK + b1 * BLK, BLK)
+        a = m * SLOT + h * 4 * BLK
+        return ap(buf, a + f, a + 4 * BLK, 2)
 
     def blk(buf, m, b):
-        return ap(buf, m * 8 * BLK + b * BLK, m * 8 * BLK + b * BLK + BLK)
+        return ap(buf, m * SLOT + b * BLK, m * SLOT + b * BLK + BLK)
 
-    z1 = 0
-    for e, name, out in (("s", "z0", ap("ZB", z1, z1 + 128)), ("s", "cb", ap("CBI", 0, 8)), ("a", "ka", ap("KAI", 0, 1)),
+    def sele(k):
+        return ap("EE", 15 - k, 143 - k)
+
+    def pieces(name, h):
+        t, out = HALF * h, []
+        for x in CUT[name]:
+            n = x[0] if name == "D" else x
+            out.append((t, t + n, x[1]) if name == "D" else (t, t + n))
+            t += n
+        return out
+
+    ID, NID, MH, BO = full("ID"), full("NID"), full("MH"), full("BO")
+    ONE, QC, MG, M15, M5, MT, C0 = [ap("CT", 64 * j, 64 * j + 64) for j in range(7)]
+
+    for e, name, out in (("s", "z0", full("ZB")), ("a", "ka", ap("KAI", 0, 1)), ("s", "cb", ap("CBI", 0, 8)),
                          ("a", "le", ap("LEI", 0, 256)), ("s", "ad", ap("ADI", 0, 1024)), ("s", "vf", ap("W", 0, 2048)),
                          ("a", "th", ap("THI", 0, 1))):
-        add(e, "load", (out, name), [], [out], "ld_" + name)
+        add({e: ("load", (out, name))}, [], [out], "ld_" + name)
 
-    K, G16, KM15, K15, K16, WUC, KA1, K2, TH, KCS, K16X, MGN, MGP = [col(j) for j in range(13)]
-    iota(ap("COLI", 0, 1), [[0, 1]], 0, 1)
+    P, K, G16, K15, K16, WUC, VC, TH, MGN, W1, K2, C19, C4, MSC, MBI, B1, B2, B3 = [col(j) for j in range(18)]
+    iota(coli(0), [[0, 1]], 0, 1)
     iota(full("JG"), [[16, 8], [0, 16]], 0, 0)
+    iota(ap("JJ", 0, 256), [[1, 256]], 0, 0)
     iota(full("JM"), [[0, 8], [1, 16]], 0, 0)
     iota(ap("IOT", 0, 8), [[1, 8]], 0, 0)
-    ts(ap("COLI", 1, 2), ap("COLI", 0, 1), 15, A.bitwise_and)
-    ts(ap("COLI", 2, 3), ap("COLI", 0, 1), 112, A.bitwise_and)
-    copy(ap("COL", 0, 2), ap("COLI", 1, 3))
-    ts(full("BO"), full("JG"), G16, A.is_equal)
-    ts(full("M1"), full("JM"), K, A.is_equal)
+    iota(MGN, [[0, 1]], -int(MAGIC), 0)
+    iota(ap("JP", 0, 8 * SEG), [[0, 2], [-16, 4], [1, SEG]], 0, 0)
+    iota(ap("IOF", 0, 8), [[768, 2], [16, 4]], 256, 0)
+    iota(ap("AD", 1024, 1088), [[0, 64]], 0, 0)
+    ts(coli(1), coli(0), 15, A.bitwise_and)
+    ts(coli(2), coli(0), 112, A.bitwise_and)
+    copy(ap("COL", 0, 3), ap("COLI", 0, 3))
+    ts(BO, full("JG"), G16, A.is_equal)
+    ts(ID, ap("JJ", 0, 128), P, A.is_equal)
+    ts(ap("EE", 0, 144), ap("JJ", 0, 144), -15.0, A.add, G16, A.is_equal)
     ts(ap("MK", 0, 16), ap("JM", 0, 16), K, A.is_equal)
+    ts(full("M16"), full("JM"), K, A.is_equal, 16.0, A.mult)
+    ts(ap("BM", 0, 64), ap("JM", 0, 64), K, A.not_equal, BIG, A.mult)
     copy(ap("LC", 0, 8), ap("IOT", 0, 8))
     ts(ap("LB", 0, 8), ap("IOT", 0, 8), 16.0, A.mult, 15.0, A.add)
-    for c, mul, plus in ((WUC, 14.0, 1.0), (KM15, 1.0, -15.0), (K15, -1.0, 4111.0), (K16, 1.0, 16.0)):
+    for c, mul, plus in ((WUC, 14.0, 1.0), (K15, -1.0, 4111.0), (K16, 1.0, 16.0)):
         ts(c, K, mul, A.mult, plus, A.add)
-    act(K16X, K, AF.Copy, None, 16.0)
-    act(KCS, K, AF.Copy, None, CS)
-    act(full("WU"), full("BO"), AF.Copy, None, WUC)
-    act(full("WK"), full("BO"), AF.Copy, None, K)
-    act(full("BOH"), full("BO"), AF.Copy, None, CS)
-    ts(ap("BM", 0, 64), ap("JM", 0, 64), K, A.not_equal, BIG, A.mult)
-    asel(full("ID"), full("BO"), A.is_equal, 0.0)
-    asel(full("CE2"), full("BO"), A.is_gt, 0.0)
-    asel(full("TR"), full("CE2"), A.not_equal, -1.0)
+    for t, val in ((ONE, 1.0), (QC, 0.25), (MG, MAGIC), (M15, MAGIC * 2 ** 15), (M5, MAGIC * 2 ** 5)):
+        memset(t, val)
+    lin(ap("CA", 0, 64), ONE, 16368.0)
+    for name, mul in (("NID", -1.0), ("MH", -0.5), ("NEG", -4096.0), ("POS", 4096.0), ("DK", K16), ("D4", mk(4))):
+        lin(full(name), ID, mul)
+    tt(C19, mk(1), mk(9), A.add)
+    for name, mul in (("WK", K), ("B32", 1.0 / 32), ("SC", C19), ("WP", WUC)):
+        lin(full(name), BO, mul)
+    ts(full("S32"), BO, mk(4), A.mult, -32.0, A.mult)
+    ts(full("SU"), BO, mk(2), A.mult, 1.0 / 2048, A.mult)
+    ts(full("CE2"), ID, 2048.0, A.mult)
     for k in range(16):
-        act(ap("SELN", 128 * k, 128 * k + 128), full("ID"), AF.Copy, None, ap("MK", k, k + 1))
-    memset(ap("SELE", 0, 1024), 0.0)
-    iota(ap("SELE", 1024, 2048), [[0, 1024]], 0, 0)
-    for k in range(16):
-        act(ap("SELE", 129 * k, 128 * k + 128, 16), ap("BO", 0, 128, 16), AF.Copy)
-    ts(ap("COLI", 8, 9), ap("KAI", 0, 1), 1184.0, A.add)
-    ts(ap("COLI", 9, 10), ap("COLI", 8, 9), 63, A.bitwise_and)
-    ts(ap("COLI", 10, 11), ap("COLI", 8, 9), 8128, A.bitwise_and)
-    copy(ap("COL", 13, 15), ap("COLI", 9, 11))
-    act(full("KL"), full("ID"), AF.Copy, None, col(13))
-    act(full("KH"), full("ID"), AF.Copy, None, col(14))
-    act(full("IDH"), full("ID"), AF.Copy, None, CS)
-    ts(ap("COLI", 3, 4), ap("KAI", 0, 1), 15, A.bitwise_and)
-    ts(K2, ap("COLI", 3, 4), 2048.0, A.mult)
+        lin(ap("SELN", 128 * k, 128 * k + 128), full("CE2"), mk(k))
+    asel(full("T01"), BO, A.is_gt, 0.0)
+    asel(full("TR"), full("T01"), A.not_equal, -1.0)
+    lin(ap("WP", 1, 128, 16), ap("BO", 0, 128, 16), 0.0)
+    lin(full("WN"), full("WP"), -1.0)
+    ts(ap("CE", 0, 64), ONE, K, A.mult, 2.0, A.is_lt)
+    ts(C0, ap("CE", 0, 64), 2040.0, A.mult, 8.0, A.add)
+    ts(ap("CE", 64, 128), ap("CE", 0, 64), MAGIC * 16 * 255, A.mult, MAGIC * 16, A.add)
+    ts(C4, K, 4.0, A.is_lt)
+    lin(MT, ap("CE", 64, 128), C4)
+    ts(MSC, K, 2.0, A.is_ge, 1.0 / 16, A.max)
+    ts(B1, K, 2.0, A.is_lt, 1279.53125, A.mult)
+    ts(B2, K, 4.0, A.is_ge, -7.5, A.mult)
+    ts(B3, K, 8.0, A.is_ge, -1280.0, A.mult)
+    ts(MBI, B1, B2, A.add, B3, A.add)
+    ts(coli(3), ap("KAI", 0, 1), 2208.0, A.add)
+    ts(coli(4), coli(3), 2047, A.bitwise_and)
+    ts(W1, coli(4), -1024.0, A.add, 16.0, A.mult)
+    ts(K2, ap("KAI", 0, 1), -2048.0, A.add)
+    lin(ap("BT", 0, 256), ap("JJ", 0, 256), 0.0)
+    lin(ap("BT", 0, 128, 8), ap("BO", 0, 128, 8), W1)
+    lin(ap("BT", 1, 128, 8), ap("BO", 0, 128, 8), -13152.0)
+    for r, mul in ((2, K2), (3, 3232.0), (8, 25.0 / 2048)):
+        lin(ap("BT", 128 + r, 256, 16), ap("BO", 0, 128, 16), mul)
+    for name, bank, sign in (("AP", "PA0", ID), ("AN", "PA1", NID)):
+        mm([(ap(bank, 128 + j, 256 + j), [(ap("BT", j, j + 128), sign)]) for j in (0, 128)])
+        lin(ap(name, 0, 256), ap(bank, 128, 384))
     copy(TH, ap("THI", 0, 1))
-    iota(MGP, [[0, 1]], int(MAGIC), 0)
-    iota(MGN, [[0, 1]], -int(MAGIC), 0)
-    act(full("NEG"), full("ID"), AF.Copy, None, -4096.0)
-    act(full("DK"), full("ID"), AF.Copy, None, K16)
-    act(full("MH"), full("ID"), AF.Copy, None, -0.5)
-    act(full("NID"), full("ID"), AF.Copy, None, -1.0)
-    act(full("M32"), full("ID"), AF.Copy, None, -32.0)
-    memset(ap("QC", 0, 64), 0.25)
-    iota(ap("BASE", 0, 144), [[16, 144]], 2032, 0)
-    memset(ap("KEEP", 0, 512), 1.0)
-    memset(ap("KEEP", 0, 512, 16), 0.0)
-    iota(ap("RST", 0, 512), [[0, 512]], 0, 0)
-    memset(ap("RST", 0, 512, 16), 2 * BIG)
+    ts(ap("TB", 0, 192), ap("JJ", 0, 192), -128.0, A.add, 1.0 / 128, A.mult)
+    ts(ap("BASE", 0, 144), ap("JJ", 0, 144), 16.0, A.mult, 2032.0, A.add)
+    wide = 16 * max(CUT["F"] + (4,))
+    memset(ap("KEEP", 0, wide), 1.0)
+    memset(ap("KEEP", 0, wide, 16), 0.0)
+    memset(ap("RST", 0, wide), 0.0)
+    memset(ap("RST", 0, wide, 16), 2 * BIG)
     memset(ap("CMP", 0, 64), -0.5)
     memset(ap("CMP", 64, 128), 6.5)
-    iota(ap("T16", 0, 128), [[16, 128]], 0, 0)
-    iota(ap("IOF", 0, 16), [[768, 2], [16, 8]], 256, 0)
-    act(ap("DUMP", 0, 16), ap("IOF", 0, 16), AF.Identity, KCS, CS)
-    ts(ap("COLI", 4, 5), ap("COLI", 0, 1), 7, A.bitwise_and)
-    ts(ap("COLI", 5, 6), ap("COLI", 0, 1), 3, A.bitwise_and)
-    ts(ap("TMP", 0, 2), ap("COLI", 4, 6), 1.5, A.add)
-    ts(ap("TMP", 2, 3), ap("COLI", 5, 6), 5.5, A.add)
-    act(ap("TMP", 4, 7), ap("TMP", 0, 3), AF.Square)
-    ts(ap("LP", 2, 5, 2), ap("TMP", 4, 6), 8.0, A.mult, -3.0, A.add)
-    ts(ap("LP", 6, 7), ap("TMP", 6, 7), 8.0, A.mult, -163.0, A.add)
-    iota(ap("RD", 0, 2 * TRI), [[0, 2 * TRI]], -1, 0)
-    for b in range(8):
-        iota(ap("RD", 8 * b * (b + 1), 8 * b * (b + 1) + TRI + 1, TRI), [[0, 2]], 4096, 0)
-    iota(ap("AD", 1024, 1152), [[0, 128]], 0, 0)
-    for m in range(1, STEPS):
-        act(ap("MS", (m - 1) * 8 * BLK + 4, m * 8 * BLK, FLD), full("JM"), AF.Copy)
-    copy(ap("LE", 0, 256), ap("LEI", 0, 256))
-    for j in range(0, 1024, 256):
-        copy(ap("AD", j, j + 256), ap("ADI", j, j + 256))
-
-    copy(lst("ML", 0, 0, 8), ap("CBI", 0, 8))
-    copy(ap("CF", 0, 8), ap("CBI", 0, 8))
-    tt(full("CE"), ind(ap("CF", 0, 8), ap("LC", 0, 8)), full("M1"), A.mult)
-    mm([(ap("PU1", 0, 128), [(full("WU"), ap("ZB", z1, z1 + 128))])])
-    mm([(ap("PU0", 0, 128), [(full("BO"), full("CE"))])])
-    act(ap("ML", 2, 8 * BLK, FLD), ap("PU0", 0, 128), AF.Copy)
-    copy(full("Y"), ap("PU1", 0, 128))
-    ts(full("YU"), full("Y"), 4095, A.bitwise_and)
-    ts(ap("ML", 1, 8 * BLK, FLD), full("YU"), -2048.0, A.add)
+    ts(ap("RD", 0, 8 * SEG), ap("JP", 0, 8 * SEG), K, A.is_equal, -8.0, A.mult)
+    ts(ap("RD", 0, 8 * SEG, SEG), ap("RD", 0, 8 * SEG, SEG), 3.0, A.add)
+    ts(ap("RD", 64, 8 * SEG, SEG), ap("JP", 64, 8 * SEG, SEG), 0.0, A.mult, 8.0, A.add)
+    ts(ap("RD", 65, 8 * SEG, SEG), ap("IOF", 0, 8), K, A.add, -1.0 / 2048, A.mult)
     for h in range(2):
-        act(ap("PU%d" % h, 256, 320), ap("T16", 64 * h, 64 * h + 64), AF.Copy)
-        act(ap("PU%d" % h, 320, 324), ap("T16", 0, 64, 16), AF.Identity, K16X)
+        ts(ap("DD", 8 * SEG * h, 8 * SEG * (h + 1)), ap("JP", 0, 8 * SEG), 0.0, A.mult, 4.0, A.add)
+    lin(ap("LE", 0, 256), ap("LEI", 0, 256))
+    for j in range(0, 1024, 256):
+        lin(ap("AD", j, j + 256), ap("ADI", j, j + 256), 1.0 / 2048)
+
+    def state(h, z, early, out):
+        reg = ap("PD%d" % h, 320, 384)
+        close = mm2(reg, [(ID, C0), (MH, ONE)] + early,
+                    [(full("WN"), z), (ID, MT), (NID, MT), (full("WP"), z)])
+        return lambda: (close(), lin(out, reg, MSC, MBI))
+
+    copy(ap("CF", 0, 8), ap("CBI", 0, 8))
+    tt(full("CE"), ind(ap("CF", 0, 8), ap("LC", 0, 8)), full("M16"), A.mult)
+    for h in HALVES:
+        reg = ap("PD%d" % h, 320, 384)
+        mm([(reg, [(ID, C0), (MH, ONE), (full("WN"), hs("ZB", h)), (ID, MT), (NID, MT), (full("WP"), hs("ZB", h)),
+                   (sele(1), hs("CE", h))])])
+        lin(fld("ML", 0, h, 1), reg, MSC, MBI)
+    ts(coli(5), coli(1), 15442.0, A.mult, 3151.0, A.add)
+    ts(coli(6), coli(5), 4095, A.bitwise_and)
+    ts(VC, coli(6), -2048.0, A.add)
+    lin(ap("WP", 1, 128, 16), ap("BO", 0, 128, 16), VC)
+    lin(ap("WN", 1, 128, 16), ap("WP", 1, 128, 16), -1.0)
 
     for m in range(1, STEPS + 1):
         last = m == STEPS
-        seen.clear()
-        q = 128 * (m & 1)
-        q8 = 8 * (m & 1)
-        lew = ap("LEI", 0, 256) if m == 1 else ap("LE", 0, 256)
         VFW = ap("W", 0, 2048)
-
-        for h in range(2):
-            PN, PE_, PF = "PN%d" % h, "PE%d" % h, "PF%d" % h
-            quarters = [(HALF * h, HALF * h + 32), (HALF * h + 32, HALF * h + HALF)]
-            cur[0] = "AB"[h]
+        tails = []
+        seen.clear()
+        for s, h in enumerate(HALVES):
+            PA, PB, PC, PD = ["P%s%d" % (x, h) for x in "ABCD"]
+            cur[0] = "<>"[s]
+            vs = 2048 + 1024 * s - 1024 * h
             if m > 1:
-                add("n", "recv", (m - 1, h), [ap("TOK", 2 * m + h - 2, 2 * m + h - 1)],
+                add({"n": ("recv", (m - 1, h))}, [ap("TOK", 2 * m + h - 2, 2 * m + h - 1)],
                     [blk("ML", m - 1, b) for b in range(4 * h, 4 * h + 4) if (b + m - 1) % NR], "arr%d_%d" % (m - 1, h))
             zh = hs("ZB", h) if m == 1 else fld("ML", m - 1, h, 0)
-            ah = fld("ML", m - 1, h, 3)
-            c16 = ap("C16", q8 + 4 * h, q8 + 4 * h + 4)
-            lin(c16, lst("ML", m - 1, 4 * h, 4 * h + 4))
-            act(ap("CL", q8 + 4 * h, q8 + 4 * h + 4), lst("ML", m - 1, 4 * h, 4 * h + 4), AF.Copy, None, CS)
-            copy(hs("S16", h, q), ind(lew, c16))
-            mm([(ap(PN, 64, 128), [(full("KH"), fld("ML", m - 1, h, 1)), (full("KL"), fld("ML", m - 1, h, 1)),
-                                   (full("IDH"), fld("ML", m - 1, h, 2))])])
-            lin(hs("PI", h), ap(PN, 64, 128), K2)
-            ts(hs("AI", h, q), hs("PI", h), 5, A.arith_shift_right, 1023, A.bitwise_and)
-            lin(hs("A16", h, q), hs("AI", h, q))
-            for b in range(4 * h, 4 * h + 4):
-                o = 8 * b * (b + 1)
-                a0 = (m - 1) * 8 * BLK
-                act(ap("DD", o, o + 16 * b + 16), ap("ML", a0 + 2, a0 + (b + 1) * BLK, FLD), AF.Abs,
-                    ap("CL", q8 + b, q8 + b + 1), -CS)
-            for t0, t1 in quarters:
-                if m == 1:
-                    copy(ap("G", 16 * t0, 16 * t1), ind(ap("ADI", 0, 1024), ap("A16", q + t0, q + t1)))
-                else:
-                    gather(ap("G", 16 * t0, 16 * t1), ind(ap("AD", 0, 1024), ap("A16", q + t0, q + t1)))
-            for t0, t1 in quarters:
-                gather(ap("W", 2048 + 16 * t0, 2048 + 16 * t1), ind(VFW, ap("S16", q + t0, q + t1)))
-            mm([(ap(PN, 0, 64), [(ap("SELN", 128 * k, 128 * k + 128), ap("G", 1024 * h + k, 1024 * h + 1024, 16))
-                                 for k in range(16)])])
-            lin(hs("N16", h), ap(PN, 0, 64))
-            act(hs("NF", h), ap(PN, 0, 64), AF.Copy)
-            for t0, t1 in quarters:
-                if DQ[t0 // 32] == "a":
-                    act(ap("D", 16 * t0, 16 * t1), ind(VFW, ap("N16", t0, t1)), AF.Copy)
-                    for j in range(2):
-                        c0 = 16 * t0 + 256 * j
-                        pd = ap("PE%d" % (h ^ j ^ 1), 128, 384)
-                        mm([(pd, [(full("NID"), ap("W", 2048 + c0, 2304 + c0)), (full("ID"), ap("D", c0, c0 + 256))])])
-                        act(ap("DA", c0, c0 + 256), pd, AF.Abs)
+            mh = fld("ML", m - 1, h, 1)
+            adr = ap(PA, 0, 64)
+            mm2(adr, [(ID, ap("CA", 0, 64))],
+                [(ap("AN", 0, 128), mh), (ap("AN", 128, 256), mh), (ID, M15), (NID, M15),
+                 (ap("AP", 0, 128), mh), (ap("AP", 128, 256), mh), (ID, M5), (NID, M5)])()
+            lin(hs("A16", h), adr, 1.0 / 32)
+            c16 = ap("C16", 4 * h, 4 * h + 4)
+            mm([(ap(PB, 64, 128), [(ID, ap("BM", 0, 64)), (full("SC"), mh)]), (ap(PB, 0, 64), [(full("SC"), mh)])])
+            scan(ap("AL", 128 * h, 128 * h + 64), ap("RST", 0, 64), ap(PB, 64, 128), A.max, A.min)
+            if m == 1:
+                lin(c16, ap("CBI", 4 * h, 4 * h + 4))
+                copy(hs("SF", h), ind(ap("LEI", 0, 256), c16))
+            else:
+                lin(c16, ap("AL", 128 * h + 15, 128 * h + 64, 16))
+                lin(hs("SF", h), ind(ap("LE", 0, 256), c16))
+            lin(hs("S16", h), hs("SF", h))
+
+            def differ(key, row):
+                for b in range(4):
+                    o = SEG * (8 * h + 4 * key + b)
+                    out, x = ap("DD", o, o + 16 * b + 16), ap(PB, row, row + 16 * b + 16)
+                    own = ap("AL", 128 * h + 64 * key + 16 * b + 15, 128 * h + 64 * key + 16 * b + 16)
+                    add({"a": k_act(out, x, AF.Abs, own, -1.0), "v": k_ts(out, x, own, A.not_equal)}, [x, own], [out])
+            differ(0, 0)
+            for t0, t1 in pieces("G", h):
+                lin(ap("G", 16 * t0, 16 * t1), ind(ap("AD", 0, 1024), ap("A16", t0, t1)))
+            for t0, t1 in pieces("S", h):
+                lin(ap("W", vs + 16 * t0, vs + 16 * t1), ind(VFW, ap("S16", t0, t1)))
+            nn = ap(PA, 64, 128)
+            mm([(nn, [(ap("SELN", 128 * k, 128 * k + 128), ap("G", 1024 * h + k, 1024 * h + 1024, 16))
+                      for k in range(16)])])
+            lin(hs("N16", h), nn)
+            lin(hs("NF", h), nn)
+            side = 0
+            for t0, t1, e in pieces("D", h):
+                if e == "v":
+                    tt(ap("D", 16 * t0, 16 * t1), ind(VFW, ap("N16", t0, t1)), ap("W", vs + 16 * t0, vs + 16 * t1),
+                       A.subtract)
+                    act(ap("DA", 16 * t0, 16 * t1), ap("D", 16 * t0, 16 * t1), AF.Abs)
                     continue
-                tt(ap("D", 16 * t0, 16 * t1), ind(VFW, ap("N16", t0, t1)), ap("W", 2048 + 16 * t0, 2048 + 16 * t1),
-                   A.subtract)
-                act(ap("DA", 16 * t0, 16 * t1), ap("D", 16 * t0, 16 * t1), AF.Abs)
-            pre = [(full("M32"), ah)] if m > 1 else []
-            mm([(ap(PE_, 0, 64), pre + [(ap("SELE", 128 * k, 128 * k + 128), ap("DA", 1024 * h + k, 1024 * h + 1024, 16))
-                                        for k in range(16)])])
+                act(ap("D", 16 * t0, 16 * t1), ind(VFW, ap("N16", t0, t1)), AF.Copy)
+                for c0 in range(16 * t0, 16 * t1, 256):
+                    c1 = min(c0 + 256, 16 * t1)
+                    pd = ap((PA, PC)[side], 128, 128 + c1 - c0)
+                    side ^= 1
+                    mm([(pd, [(NID, ap("W", vs + c0, vs + c1)), (ID, ap("D", c0, c1))])])
+                    act(ap("DA", c0, c1), pd, AF.Abs)
+            ee = ap(PC, 0, 64)
+            mm([(ee, ([(full("S32"), mh)] if m > 1 else []) +
+                 [(sele(k), ap("DA", 1024 * h + k, 1024 * h + 1024, 16)) for k in range(16)])])
+            r1, r2 = ap(PA, 384, 448), ap(PD, 128, 192)
             okh = hs("OK", h)
-            ts(okh, ap(PE_, 0, 64), TH, A.is_le)
-            if not last:
-                act(hs("KEY", h), ap(PE_, 0, 64), AF.Identity, K15, 16.0)
-            r1, r2 = ap(PF, 128, 192), ap("PU%d" % h, 128, 192)
-            mm([(ap(PF, 0, 64), [(full("TR"), okh)]), (ap(PF, 64, 128), [(full("BO"), okh)])])
-            mm([(r2, [(full("ID"), ap("BASE", 64 * h, 64 * h + 64)), (full("DK"), okh)])], True, False)
-            tt(ap("FL", 128 * h, 128 * h + 128), ap(PF, 0, 128), full("CMP"), A.is_lt)
             fh, sq = ap("FL", 128 * h, 128 * h + 64), ap("FL", 128 * h + 64, 128 * h + 128)
-            mm([(r2, [(full("NEG"), sq)])], False, True)
-            mm([(r1, [(full("ID"), ap("BASE", 64 * h + 1, 64 * h + 65)), (full("WK"), fh), (full("NEG"), sq)])])
+            close1 = mm2(r1, [(ID, ap("BASE", 64 * s + 1, 64 * s + 65))], [(full("WK"), fh), (full("NEG"), sq)])
+            ts(okh, ee, TH, A.is_le)
+            if not last:
+                lin(hs("KEY", h), ee, 16.0, K15)
+            closez = mm2(ap(PC, 64, 128), [(ID, zh), (ID, QC)],
+                         [(MH, ap("MX", 1024 * h + 15, 1024 * h + 1024, 16)),
+                          (MH, ap("MN", 1024 * h + 15, 1024 * h + 1024, 16)), (ID, MG)])
+            mm([(ap(PD, 0, 64), [(full("TR"), okh)]), (ap(PD, 64, 128), [(BO, okh)])])
+            close2 = mm2(r2, [(ID, ap("BASE", 64 * s, 64 * s + 64)), (full("DK"), okh)], [(full("NEG"), sq)])
+            tt(ap("FL", 128 * h, 128 * h + 128), ap(PD, 0, 128), full("CMP"), A.is_lt)
+            close2()
+            close1()
             tt(hs("X1", h), r2, hs("NF", h), A.max)
             tt(hs("X2", h), r1, hs("X1", h), A.max)
             lin(hs("F16", h), hs("X2", h))
-            if not last:
-                if m > 1:
-                    mm([(ap(PN, 256, 320), [(full("ID"), ah), (full("ID"), sq)])])
-                    act(fld("MS", m - 1, h, 3), ap(PN, 256, 320), AF.Copy)
-                else:
-                    act(fld("MS", m - 1, h, 3), sq, AF.Copy)
-            for t0, t1 in quarters:
-                gather(ap("FV", 16 * t0, 16 * t1), ind(ap("W", 0, 3072 + 1024 * h), ap("F16", t0, t1)))
-                scan(ap("MX", 16 * t0, 16 * t1), ap("KEEP", 0, 512), ap("FV", 16 * t0, 16 * t1), A.mult, A.max)
-                scan(ap("MN", 16 * t0, 16 * t1), ap("RST", 0, 512), ap("FV", 16 * t0, 16 * t1), A.max, A.min)
-
-        cur[0] = "W"
-        scan(ap("RR", 0, TRI), ap("RD", 0, TRI), ap("DD", 0, TRI), A.add, A.min)
-        ts(ap("XD", 0, 16), ind(ap("RR", 0, TRI), ap("LP", 2, 3)), KM15, A.not_equal, 2 * BIG, A.mult)
-        tt(ap("YD", 0, 8), ap("XD", 0, 8), ap("CL", q8, q8 + 8), A.add)
-        tt(ap("ZD", 0, 8), ap("YD", 0, 8), ap("DUMP", 0, 8), A.min)
-        ts(ap("O16", 0, 8), ap("ZD", 0, 8), 1.0 / CS, A.mult, 0.25, A.add)
-        for h in range(2):
-            tt(hs("SN", h), ind(lew, ap("C16", q8 + 4 * h, q8 + 4 * h + 4)), hs("NF", h), A.subtract)
-            tt(hs("SO", h), hs("SN", h), hs("OK", h), A.mult)
-
-        for h in range(2):
-            PE_, PU, PF = "PE%d" % h, "PU%d" % h, "PF%d" % h
-            y0 = 72 * h
-            cur[0] = "cd"[h]
-            tt(ind(ap("LE", 0, 384), ap("O16", 4 * h, 4 * h + 4)), hs("SO", h), hs("NF", h), A.add)
-            ii = ap(PF, 256, 320)
+            for t0, t1 in pieces("F", h):
+                n = 16 * (t1 - t0)
+                lin(ap("FV", 16 * t0, 16 * t1), ind(ap("W", 0, 3072 + 1024 * s), ap("F16", t0, t1)))
+                scan(ap("MX", 16 * t0, 16 * t1), ap("KEEP", 0, n), ap("FV", 16 * t0, 16 * t1), A.mult, A.max)
+                scan(ap("MN", 16 * t0, 16 * t1), ap("RST", 0, n), ap("FV", 16 * t0, 16 * t1), A.max, A.min)
+            mm([(ap(PD, 192, 256), [(ID, hs("SF", h)), (full("NEG"), ONE), (full("POS"), okh)]),
+                (ap(PD, 256, 320), [(ID, hs("NF", h)), (full("NEG"), okh)])])
+            lin(ap("LV", 128 * h, 128 * h + 128), ap(PD, 192, 320))
             if not last:
                 transp(hs("KT", h), hs("KEY", h))
                 scan(hs("KS", h), ap("KEEP", 0, 64), hs("KT", h), A.mult, A.max)
                 tt(hs("IT", h), ind(hs("KS", h), ap("LB", 0, 4)), hs("KT", h), A.is_equal)
-                transp(ii, hs("IT", h))
-                tt(hs("IA", h), ii, hs("AI", h, q), A.mult)
-                act(hs("NI", h), ii, AF.Identity, 1.0, -1.0)
-                mm([(hs("PN0", h, 128), [(full("ID"), ap("BM", 0, 64)), (full("BOH"), hs("IA", h))]),
-                    (hs("PN1", h, 128), [(full("BOH"), hs("IA", h))])])
-                scan(hs("AL", h), ap("RST", 0, 64), hs("PN0", h, 128), A.max, A.min)
-                for b in range(4 * h, 4 * h + 4):
-                    o = TRI + 8 * b * (b + 1)
-                    act(ap("DD", o, o + 16 * b + 16), ap("PN1", 128, 128 + 16 * b + 16), AF.Abs,
-                        ap("AL", 16 * b + 15, 16 * b + 16), -1.0)
-                r0, r1 = TRI + 160 * h, TRI + 160 + 416 * h
-                o0 = 8 + 4 * h
-                scan(ap("RR", r0, r1), ap("RD", r0, r1), ap("DD", r0, r1), A.add, A.min)
-                ts(ap("XD", 16 + 16 * h, 32 + 16 * h), ind(ap("RR", r0, r1), ap("LP", 4 + 2 * h, 5 + 2 * h)), KM15,
-                   A.not_equal, 2 * BIG, A.mult)
-                tt(ap("YD", o0, o0 + 4), ap("XD", 16 + 16 * h, 20 + 16 * h), ap("AL", 64 * h + 15, 64 * h + 64, 16), A.add)
-                tt(ap("ZD", o0, o0 + 4), ap("YD", o0, o0 + 4), ap("DUMP", o0, o0 + 4), A.min)
-                ts(ap("O16", o0, o0 + 4), ap("ZD", o0, o0 + 4), 1.0 / CS, A.mult, 0.25, A.add)
-                tt(hs("T1", h), ind(ap("AD", 0, 1152), ap("O16", o0, o0 + 4)), hs("NI", h), A.mult)
-            cur[0] = "ab"[h]
-            zh = hs("ZB", h) if m == 1 else fld("ML", m - 1, h, 0)
-            mm([(ap(PE_, 64, 128), [(full("ID"), zh), (full("ID"), ap("QC", 0, 64)),
-                                    (full("MH"), ap("MX", 1024 * h + 15, 1024 * h + 1024, 16)),
-                                    (full("MH"), ap("MN", 1024 * h + 15, 1024 * h + 1024, 16))])])
-            act(hs("ZR", h), ap(PE_, 64, 128), AF.Identity, MGP)
-            act(hs("Z16", h), hs("ZR", h), AF.Abs, MGN)
-            masked = (ap(PU, 64, 128), [(full("ID"), ap("BM", 0, 64)), (full("WU"), hs("Z16", h))])
+                transp(hs("II", h), hs("IT", h))
+                tt(hs("IA", h), adr, hs("II", h), A.mult)
+                mm([(ap(PB, 192, 256), [(ID, ap("BM", 0, 64)), (full("B32"), hs("IA", h))]),
+                    (ap(PB, 128, 192), [(full("B32"), hs("IA", h))])])
+                scan(ap("AL", 128 * h + 64, 128 * h + 128), ap("RST", 0, 64), ap(PB, 192, 256), A.max, A.min)
+                differ(1, 128)
+            nk = 4 if last else 8
+            d0 = 8 * SEG * h
+            lin(ap("DD", d0 + 65, d0 + SEG * nk, SEG), ap("AL", 128 * h + 15, 128 * h + 16 * nk, 16), -1.0 / 2048)
+            scan(ap("RR", d0, d0 + SEG * nk), ap("RD", 0, SEG * nk), ap("DD", d0, d0 + SEG * nk), A.add, A.min)
+            lin(ap("O16", 8 * h, 8 * h + nk), ap("RR", d0 + 65, d0 + SEG * nk, SEG), -2048.0)
             if not last:
-                act(fld("MS", m - 1, h, 0), hs("ZR", h), AF.Abs, MGN)
-                mm([masked, (ap(PU, 0, 64), [(full("WU"), hs("Z16", h))])])
-            else:
-                mm([masked])
-            scan(hs("XS", h), ap("RST", 0, 64), ap(PU, 64, 128), A.max, A.min)
-            lin(ap("Y", y0 + 64, y0 + 68), ap("XS", 64 * h + 15, 64 * h + 64, 16))
-            lo = y0 + (64 if last else 0)
+                tt(hs("T1", h), ind(ap("AD", 0, 1088), ap("O16", 8 * h + 4, 8 * h + 8)), hs("II", h), A.subtract)
+            zo = hs("Z16", h) if last else fld("MS", m - 1, h, 0)
+            early = [] if last else ([(full("D4"), mh)] if m > 1 else []) + [(full("D4"), sq)]
+            tails.append((closez, zo, state(h, zo, early, fld("MS", m - 1, h, 1))))
+
+        for s, h in enumerate(HALVES):
+            PB, PC = "PB%d" % h, "PC%d" % h
+            cur[0] = "<>"[s]
+            closez, zo, closem = tails[s]
+            mo = fld("MS", m - 1, h, 1)
+            closez()
+            act(zo, ap(PC, 64, 128), AF.Abs, MGN)
+            closem()
             if not last:
-                lin(ap("Y", y0, y0 + 64), ap(PU, 0, 64))
-            ts(ap("YL", lo, y0 + 68), ap("Y", lo, y0 + 68), 15, A.bitwise_and)
-            tt(ap("WF", lo, y0 + 68), ap("YL", lo, y0 + 68), ap(PU, 256 + lo - y0, 324), A.add)
-            lin(ap("W16", 4 * h, 4 * h + 4), ap("WF", y0 + 64, y0 + 68))
-            if not last:
-                tt(hs("T2", h), ap("WF", y0, y0 + 64), ii, A.mult)
-                tt(ind(ap("AD", 0, 1152), ap("O16", 8 + 4 * h, 12 + 4 * h)), hs("T1", h), hs("T2", h), A.add)
-                ts(ap("YU", y0, y0 + 68), ap("Y", y0, y0 + 68), 4095, A.bitwise_and)
-                ts(fld("MS", m - 1, h, 1), ap("YU", y0, y0 + 64), -2048.0, A.add)
-                lin(ap("YM", y0, y0 + 68), ap("YU", y0, y0 + 68), None, 1103.0)
-                ts(ap("YC", y0, y0 + 68), ap("YM", y0, y0 + 68), 4, A.arith_shift_right, 255, A.bitwise_and)
-                lin(fld("MS", m - 1, h, 2), ap("YC", y0, y0 + 64))
-                lin(lst("MS", m - 1, 4 * h, 4 * h + 4), ap("YC", y0 + 64, y0 + 68))
                 away = []
                 for b in range(4 * h, 4 * h + 4):
                     if (b + m) % NR:
                         away.append(blk("MS", m - 1, b))
                     else:
-                        act(blk("ML", m, b), blk("MS", m - 1, b), AF.Copy)
-                add("g", "send", (m, h), away, [ap("TOK", 2 * m + h, 2 * m + h + 1)], "none")
-            copy(ind(ap("W", 1024 * h, 1024 * h + 1024), ap("W16", 4 * h, 4 * h + 4)), hs("Z16", h))
+                        lin(blk("ML", m, b), blk("MS", m - 1, b))
+                add({"g": ("send", (m, h))}, away, [ap("TOK", 2 * m + h, 2 * m + h + 1)], "none")
+            mm([(ap(PB, 320, 384), [(ID, ap("BM", 0, 64)), (ID, ap("TB", 128, 192)), (full("SU"), mo)])])
+            scan(hs("XS", h), ap("RST", 0, 64), ap(PB, 320, 384), A.max, A.min)
+            lin(ap("W16", 4 * h, 4 * h + 4), ap("XS", 64 * h + 15, 64 * h + 64, 16), 2048.0)
+            tt(ind(ap("LE", 0, 320), ap("O16", 8 * h, 8 * h + 4)), ap("LV", 128 * h, 128 * h + 64),
+               ap("LV", 128 * h + 64, 128 * h + 128), A.max)
+            if not last:
+                mm([(ap(PB, 256, 320), [(ID, hs("TB", h)), (full("SU"), mo)])])
+                tt(hs("T2", h), ap(PB, 256, 320), hs("II", h), A.add)
+                tt(ind(ap("AD", 0, 1088), ap("O16", 8 * h + 4, 8 * h + 8)), hs("T1", h), hs("T2", h), A.max)
+            copy(ind(ap("W", 1024 * h, 1024 * h + 1024), ap("W16", 4 * h, 4 * h + 4)), zo)
 
-    add("s", "store", ("yl", None, ap("LE", 0, 256)), [ap("LE", 0, 256)], [], "st_yl")
-    add("s", "store", ("yz", None, full("Z16")), [full("Z16")], [], "st_yz")
-    add("s", "store", ("yv", (0, 1024), ap("W", 0, 1024)), [ap("W", 0, 1024)], [], "st_yv0")
-    add("a", "store", ("yv", (1024, 2048), ap("W", 1024, 2048)), [ap("W", 1024, 2048)], [], "st_yv1")
+    add({"s": ("store", ("yl", None, ap("LE", 0, 256)))}, [ap("LE", 0, 256)], [], "st_yl")
+    add({"s": ("store", ("yz", None, full("Z16")))}, [full("Z16")], [], "st_yz")
+    add({"s": ("store", ("yv", (1024, 2048), ap("W", 1024, 2048)))}, [ap("W", 1024, 2048)], [], "st_yv1")
+    add({"a": ("store", ("yv", (0, 1024), ap("W", 0, 1024)))}, [ap("W", 0, 1024)], [], "st_yv0")
     return ops
 
 
@@ -469,17 +463,80 @@ def dependencies(ops):
     return deps
 
 
-def with_banks(ops, deps, order):
-    last, done, out = {}, set(), [None] * len(ops)
-    for i in order:
-        assert all([j in done for j in deps[i]])
-        done.add(i)
-        extra = []
-        for b in set([x[0] for x in ops[i]["r"] + ops[i]["w"] if x[0] in PS]):
-            extra += [x for e, x in last.get(b, {}).items() if e != ops[i]["e"]]
-            last.setdefault(b, {})[ops[i]["e"]] = i
-        out[i] = sorted(set(deps[i] + extra))
-    return out
+def cost(o, e, c):
+    k, a = o["alt"][e]
+    if k == "send":
+        return c["send"]
+    if k in ("load", "store", "recv"):
+        return 50.0
+    if k == "mm":
+        return sum([max(64, cnt(x[2])) for x in a]) * c["pe"]
+    n = cnt(o["w"][0])
+    if e == "g":
+        return (170 + 2 * n) * c["cy"]
+    if o["w"][0][4] is not None:
+        return (60 + n * c["sc"]) * c["cy"]
+    if [x for x in o["r"] if x[4] is not None]:
+        return ((60 if e == "v" else 78) + n * c["ga"]) * c["cy"]
+    if e == "v":
+        if k == "tt":
+            n *= 1 if [x for x in o["r"] if x[0] in PS] else 2
+        elif all([x[0] in _S and _S[x[0]][0] in (BF, F16, U16) for x in o["r"] + o["w"] if cnt(x) > 1]):
+            n /= 2
+    return max(64, n) * c["cy"]
+
+
+def plan(ops, c):
+    deps = dependencies(ops)
+    n = len(ops)
+    costs = [{e: cost(o, e, c) for e in o["alt"]} for o in ops]
+    late = [0.0] * n
+    for i, o in enumerate(ops):
+        k, a = list(o["alt"].values())[0]
+        if k == "send":
+            late[i] = c["way"]
+        elif k in ("load", "store"):
+            x = a[0] if k == "load" else a[2]
+            late[i] = c["dma"] + 128 * cnt(x) * (4 if _S[x[0]][0] in (F32, I32) else 2) / c["bw"]
+    succ = [[] for _ in ops]
+    for i in range(n):
+        for j in deps[i]:
+            succ[j].append(i)
+    togo = [0.0] * n
+    for i in range(n - 1, -1, -1):
+        togo[i] = min(costs[i].values()) + late[i] + max([togo[j] + c["hop"] for j in succ[i]] + [0.0])
+    rank = [togo[i] + (c["lead"] if "<" in o["tag"] and not o["tag"].startswith(ASIDE) else 0.0)
+            for i, o in enumerate(ops)]
+    banks = [set([x[0] for x in o["r"] + o["w"] if x[0] in PS]) for o in ops]
+    left = [len(d) for d in deps]
+    ready = [i for i in range(n) if not left[i]]
+    free, fin, eng, used, order, waits = {}, [0.0] * n, [None] * n, {}, [], [None] * n
+    while ready:
+        cand = []
+        for i in ready:
+            best = None
+            for e, t in costs[i].items():
+                w = [j for j in deps[i] if not (e == "p" and eng[j] == "p")]
+                w += [j for b in banks[i] for x, j in used.get(b, {}).items() if x != e]
+                at = max([free.get(e, 0.0)] + [fin[j] + c["hop"] for j in w])
+                end = at + t + (c["spare"] * t + c["plus"] if e == "v" else 0.0)
+                if best is None or end < best[4]:
+                    best = (at, t, e, w, end)
+            cand.append((i,) + best[:4])
+        soon = min([x[1] for x in cand]) + c["look"]
+        pick = max([x for x in cand if x[1] <= soon], key=lambda x: (rank[x[0]], -x[0]))
+        fill = [x for x in cand if x[3] == pick[3] and x[1] + x[2] <= pick[1] + c["slip"] and x is not pick]
+        i, at, t, e, w = max(fill, key=lambda x: (rank[x[0]], -x[0])) if fill else pick
+        ready.remove(i)
+        order.append(i)
+        eng[i], waits[i], free[e], fin[i] = e, sorted(set(w)), at + t, at + t + late[i]
+        for b in banks[i]:
+            used.setdefault(b, {})[e] = i
+        for j in succ[i]:
+            left[j] -= 1
+            if not left[j]:
+                ready.append(j)
+    return order, eng, waits
 
 
 def routes(T, topo, m, h):
@@ -531,13 +588,13 @@ def arrivals(T, topo, m, h, core):
 def relay_program(g, core, T, topo):
     sent = 0
     for m in range(1, STEPS):
-        for h in range(2):
+        for h in HALVES:
             for r, mine in enumerate(routes(T, topo, m, h)):
                 for b, dst, via in mine:
                     if via == core:
                         sem = T.sem["arr%d_%d" % (m, h)]
                         g.wait_ge(sem, len(engine_masks(topo, T.cores[r], mine)[b]))
-                        blk = T["ML"][:, m * 8 * BLK + b * BLK:m * 8 * BLK + b * BLK + BLK]
+                        blk = T["ML"][:, m * SLOT + b * BLK:m * SLOT + b * BLK + BLK]
                         rid, pid = topo.addr(dst, core)
                         g.remote_dma(blk, blk, sem, T.sem["sent"], pid, rid, topo.mask(core, dst))
                         sent += len(topo.engines(core, dst))
@@ -555,11 +612,8 @@ def rank_program(g, core, T, topo):
         return
     if "plan" not in _CACHE:
         ops = build_ops()
-        order = [DIGITS.index(ORDER[i]) * 62 + DIGITS.index(ORDER[i + 1]) for i in range(0, len(ORDER), 2)]
-        order = order or list(range(len(ops)))
-        assert sorted(order) == list(range(len(ops)))
-        _CACHE["plan"] = (ops, with_banks(ops, dependencies(ops), order), order)
-    ops, deps, order = _CACHE["plan"]
+        _CACHE["plan"] = (ops,) + plan(ops, PLAN)
+    ops, order, eng, deps = _CACHE["plan"]
     Q = {"v": g.vector, "a": g.scalar, "p": g.tensor, "g": g, "s": g.sync}
 
     def P(x):
@@ -577,8 +631,8 @@ def rank_program(g, core, T, topo):
     sent = 0
     own = []
     for i in order:
-        o = ops[i]
-        e, k, a = o["e"], o["k"], o["a"]
+        o, e = ops[i], eng[i]
+        k, a = o["alt"][e]
         if k == "recv":
             done[i] = (o["sem"], arrivals(T, topo, a[0], a[1], core), {})
             continue
@@ -614,8 +668,8 @@ def rank_program(g, core, T, topo):
                 trs[via is None].append(RemoteDMATransfer(
                     dst_ids=[DstId(rid=rid, pnc=pid)], dma_engine_mask=as_mask(em[b]),
                     remote_sem=T.sem["arr%d_%d" % (m, h)],
-                    src=T["MS"][:, (m - 1) * 8 * BLK + b * BLK:(m - 1) * 8 * BLK + b * BLK + BLK],
-                    dst=T["ML"][:, m * 8 * BLK + b * BLK:m * 8 * BLK + b * BLK + BLK]))
+                    src=T["MS"][:, (m - 1) * SLOT + b * BLK:(m - 1) * SLOT + b * BLK + BLK],
+                    dst=T["ML"][:, m * SLOT + b * BLK:m * SLOT + b * BLK + BLK]))
                 sent += len(em[b])
             g.remote_dma_fused(trs[False] + trs[True], local_sem=T.sem["sent"])
             done[i] = ("none", 0, {})

@@ -12,25 +12,25 @@ HALVES = (1, 0)
 
 _S = {
     "W": (BF, 4096), "ADI": (I32, 1024), "LEI": (I32, 256), "AD": (F32, 1088), "LE": (F32, 320),
-    "G": (F16, 2048), "D": (BF, 2048), "DA": (BF, 2048), "FV": (BF, 2048), "MX": (BF, 2048), "MN": (BF, 2048),
-    "SELN": (BF, 2048), "EE": (BF, 144), "ML": (F16, 5 * SLOT), "MS": (F16, 5 * SLOT),
+    "G": (F16, 2048), "D": (BF, 2048), "DA": (BF, 2048), "FV": (F16, 2048), "MX": (F16, 2048), "MN": (F16, 2176),
+    "SELN": (BF, 2048), "EE": (BF, 144), "EN": (BF, 144), "ML": (F16, 5 * SLOT), "MS": (F16, 5 * SLOT),
     "CBI": (I32, 8), "KAI": (I32, 8), "THI": (I32, 8), "CF": (F32, 8), "COL": (F32, 32), "COLI": (I32, 16),
     "JJ": (BF, 256), "JM": (BF, 128), "JG": (BF, 128), "JP": (BF, 8 * SEG), "IOT": (I32, 8), "IOF": (F32, 8),
-    "MK": (F32, 16), "CT": (BF, 512), "CA": (F16, 64), "T01": (BF, 128),
-    "WP": (F16, 128), "WN": (F16, 128), "BT": (F16, 256), "AP": (F16, 256), "AN": (F16, 256),
-    "BM": (BF, 64), "M16": (BF, 128), "CE": (BF, 128), "CE2": (BF, 128), "TB": (BF, 192), "BASE": (BF, 144),
-    "KEEP": (BF, 512), "RST": (BF, 512), "CMP": (BF, 128),
+    "MK": (F32, 16), "CT": (BF, 512), "ZC": (BF, 128), "OG": (F16, 128), "RAMP": (BF, 512), "CA": (F16, 64),
+    "WP": (F16, 128), "WN": (F16, 128), "BT": (F16, 256), "AP": (F16, 256), "AN": (F16, 256), "T01": (BF, 128),
+    "BM": (BF, 64), "M1": (BF, 128), "CE": (BF, 128), "CE2": (BF, 128), "TB": (BF, 192), "BASE": (BF, 144),
+    "KEEP": (BF, 512), "RST": (BF, 512),
     "RD": (F16, 8 * SEG), "DD": (F16, 16 * SEG), "RR": (F16, 16 * SEG),
     "LB": (U16, 8), "LC": (U16, 8), "C16": (U16, 8), "S16": (U16, 128), "A16": (U16, 128), "N16": (U16, 128),
     "F16": (U16, 128), "W16": (U16, 8), "O16": (U16, 16),
-    "ZB": (BF, 128), "SF": (F16, 128), "NF": (F16, 128), "OK": (BF, 128), "FL": (BF, 256), "X1": (F32, 128),
+    "ZB": (BF, 128), "SF": (F16, 128), "NF": (F16, 128), "OK": (BF, 128), "FL": (BF, 128), "X1": (F32, 128),
     "X2": (F32, 128), "Z16": (BF, 128), "XS": (F32, 128), "LV": (F32, 256),
-    "KEY": (F32, 128), "KT": (F32, 128), "KS": (F32, 128), "IT": (BF, 128), "II": (BF, 128), "IA": (F16, 128),
+    "KT": (F32, 128), "KS": (F32, 128), "IT": (BF, 128), "II": (BF, 128), "IA": (F16, 128),
     "AL": (F32, 256), "T1": (F32, 128), "T2": (F32, 128),
 }
-for _n in ("ID", "NID", "MH", "BO", "TR", "WK", "DK", "NEG", "POS", "B32", "S32", "SC", "SU", "D4"):
+for _n in ("ID", "NID", "MH", "BO", "TR", "WK", "DK", "NEG", "POS", "B32", "S32", "SC", "SU", "D4", "N15", "SQ4"):
     _S[_n] = (BF, 128)
-PS = [b + h for b in ("PA", "PB", "PC", "PD") for h in "01"]
+PS = ["P%d" % b for b in range(8)]
 SCRATCH = {}
 for _n in _S:
     SCRATCH[_n] = ("sbuf", [128, _S[_n][1]], _S[_n][0])
@@ -38,16 +38,29 @@ for _n in PS:
     SCRATCH[_n] = ("psum", [128, 512], F32)
 
 LOADS = ["z0", "cb", "ka", "le", "th", "ad", "vf"]
-STORES = ["yv0", "yv1", "yl", "yz"]
-SEMAPHORES = ["cv", "ca", "cp", "cg", "sent"] + ["ld_" + x for x in LOADS] + ["st_" + x for x in STORES] + \
-    ["arr%d_%d" % (m, h) for m in range(1, STEPS) for h in range(2)]
+SEMAPHORES = ["cv", "ca", "cp", "cg", "sent", "st_yl", "st_yz"] + ["ld_" + x for x in LOADS] + \
+    ["st_yv%d" % p for p in range(4)] + ["arr%d_%d" % (m, p) for m in range(1, STEPS) for p in range(4)]
 CNT = {"v": "cv", "a": "ca", "p": "cp", "g": "cg"}
 
-CUT = {"G": (32, 32), "S": (32, 32), "F": (32, 32), "D": ((16, "v"), (16, "a"), (16, "v"), (16, "a"))}
-PIN = {}
-ASIDE = ("DD", "KT", "KS", "IT", "II", "IA", "RR", "O16", "T1", "T2", "LV", "KEY", "XS", "W16", "LE", "AD", "PB")
-PLAN = {"cy": 0.95, "pe": 0.5, "ga": 1.56, "sc": 3.8, "hop": 80.0, "send": 800.0, "way": 4000.0, "dma": 2000.0,
-        "bw": 200.0, "look": 200.0, "spare": 0.0, "plus": 200.0, "slip": 30.0, "lead": 2000.0}
+PARTS = [[{'G': (16, 48), 'S': (28, 36), 'D': ((16, 'a'), (24, 'v'), (24, 'v')), 'F': ((32, 'r'), (32, 'a'))}],
+         [{'G': (16, 16, 16, 16), 'S': (40, 24), 'D': ((16, 'a'), (16, 'a'), (32, 'v')),
+           'F': ((16, 'r'), (24, 'a'), (24, 'a'))}]]
+OPT = {'apart': (0, 1), 'old': (1, 0), 'run': 16}
+PIN = {'DD>9': 'a', 'Wa2': 'v', 'C16b1': 'a', 'DD>2': 'a', 'Gb3': 'a', 'SFb1': 'v', 'Wb1': 'a', 'F16b1': 'a', 'T2>1': 'v',
+       'DD>5': 'a', 'N16a1': 'a', 'DD<2': 'a', 'Wa1': 'a', 'DD<7': 'a', 'Wb2': 'v', 'F16a1': 'v', 'DD>3': 'a',
+       'DD<3': 'a', 'MLa2': 'a', 'Gb4': 'v', 'MSb1': 'v', 'DD<5': 'a', 'NFb1': 'a', 'LV<1': 'a', 'W16<1': 'a',
+       'DD<10': 'a', 'Gb1': 'a', 'A16a1': 'a', 'DD<8': 'a', 'MLa1': 'a'}
+PLAN = {"cy": 0.9, "pe": 0.58, "ga": 1.56, "sc": 3.8, "hop": 115.0, "same": 115.0, "callv": 62.0, "calla": 45.0,
+        "send": 800.0, "way": 5400.0, "dma": 2000.0,
+        "bw": 250.0, "look": 60.0, "spare": 0.15, "plus": 200.0, "slip": 30.0, "lead": 1500.0}
+
+
+def parts():
+    out = []
+    for s, h in enumerate(HALVES):
+        n = HALF // len(PARTS[s])
+        out += [(HALF * h + HALF - n * (j + 1), HALF * h + HALF - n * j) for j in range(len(PARTS[s]))]
+    return out
 
 
 def ap(n, a, b, s=1):
@@ -65,13 +78,14 @@ def cnt(x):
 
 
 def bits(x):
-    n = len(range(x[1], x[2], x[3]))
-    return (((1 << (n * x[3])) - 1) // ((1 << x[3]) - 1)) << x[1]
+    r = range(x[1], x[2], x[3])
+    s = abs(x[3])
+    return (((1 << (len(r) * s)) - 1) // ((1 << s) - 1)) << min(r[0], r[-1])
 
 
 def build_ops():
     ops = []
-    cur, seen = ["-"], {}
+    cur, seen = ["-", 0, 0], {}
     A = AluOpType
     AF = ActivationFunctionType
 
@@ -90,7 +104,7 @@ def build_ops():
         tag += str(seen[tag])
         if tag in PIN and len(alt) > 1:
             alt = {PIN[tag]: alt[PIN[tag]]}
-        ops.append({"alt": alt, "r": rr, "w": w, "sem": sem, "tag": tag})
+        ops.append({"alt": alt, "r": rr, "w": w, "sem": sem, "tag": tag, "lead": cur[1], "step": cur[2]})
 
     def k_ts(out, x, s1, op0, s2=None, op1=None):
         return ("ts", (out, x, s1, s2, op0, op1))
@@ -118,8 +132,8 @@ def build_ops():
     def ts(out, x, s1, op0, s2=None, op1=None):
         add({"v": k_ts(out, x, s1, op0, s2, op1)}, [x, s1, s2], [out])
 
-    def scan(out, d0, d1, op0, op1):
-        add({"v": ("scan", (out, d0, d1, 0.0, op0, op1))}, [d0, d1], [out])
+    def scan(out, d0, d1, op0, op1, first=0.0):
+        add({"v": ("scan", (out, d0, d1, first, op0, op1))}, [d0, d1], [out])
 
     def transp(out, x):
         add({"v": ("tr", (out, x))}, [x], [out])
@@ -141,9 +155,13 @@ def build_ops():
         add({"p": ("mm", lst)}, r, w)
 
     def mm2(out, early, late):
-        if early:
-            mm([(out, early)], True, False)
-        return lambda: mm([(out, late)], not early, True)
+        mm([(out, early)], True, False)
+        return lambda: mm([(out, late)], False, True)
+
+    def lanes(out, terms, first):
+        n = OPT["run"]
+        for j in range(0, 16, n):
+            mm([(out, terms[j:j + n])], first and j == 0, j + n >= 16)
 
     def iota(out, pattern, base, cm):
         add({"g": ("iota", (out, pattern, base, cm))}, [], [out])
@@ -163,12 +181,8 @@ def build_ops():
     def full(n):
         return ap(n, 0, 128)
 
-    def hs(n, h, o=0):
-        return ap(n, o + HALF * h, o + HALF * h + HALF)
-
-    def fld(buf, m, h, f):
-        a = m * SLOT + h * 4 * BLK
-        return ap(buf, a + f, a + 4 * BLK, 2)
+    def fld(buf, m, t0, t1, f):
+        return ap(buf, m * SLOT + 2 * t0 + f, m * SLOT + 2 * t1, 2)
 
     def blk(buf, m, b):
         return ap(buf, m * SLOT + b * BLK, m * SLOT + b * BLK + BLK)
@@ -176,23 +190,30 @@ def build_ops():
     def sele(k):
         return ap("EE", 15 - k, 143 - k)
 
-    def pieces(name, h):
-        t, out = HALF * h, []
-        for x in CUT[name]:
-            n = x[0] if name == "D" else x
-            out.append((t, t + n, x[1]) if name == "D" else (t, t + n))
+    def ct(j, n=HALF):
+        return ap("CT", 64 * j, 64 * j + n)
+
+    cuts = PARTS[0] + PARTS[1]
+    spans = parts()
+
+    def pieces(name, p):
+        t, out = spans[p][0], []
+        for x in cuts[p][name]:
+            n = x[0] if name in "DF" else x
+            out.append((t, t + n, x[1]) if name in "DF" else (t, t + n))
             t += n
         return out
 
     ID, NID, MH, BO = full("ID"), full("NID"), full("MH"), full("BO")
-    ONE, QC, MG, M15, M5, MT, C0 = [ap("CT", 64 * j, 64 * j + 64) for j in range(7)]
+    ONE, QC, MG, M15, M5, MT, C0, KT15 = range(8)
 
     for e, name, out in (("s", "z0", full("ZB")), ("a", "ka", ap("KAI", 0, 1)), ("s", "cb", ap("CBI", 0, 8)),
                          ("a", "le", ap("LEI", 0, 256)), ("s", "ad", ap("ADI", 0, 1024)), ("s", "vf", ap("W", 0, 2048)),
                          ("a", "th", ap("THI", 0, 1))):
-        add({e: ("load", (out, name))}, [], [out], "ld_" + name)
+        add({e: ("load", (out, name))}, [ap("queue" + e, 0, 1)], [out, ap("queue" + e, 0, 1)], "ld_" + name)
 
-    P, K, G16, K15, K16, WUC, VC, TH, MGN, W1, K2, C19, C4, MSC, MBI, B1, B2, B3 = [col(j) for j in range(18)]
+    P, K, G16, K15, K16, WUC, VC, TH, MGN, W1, K2, C19, C4, MSC, MBI, B1, B2, B3, G15, CMP, WKC = \
+        [col(j) for j in range(21)]
     iota(coli(0), [[0, 1]], 0, 1)
     iota(full("JG"), [[16, 8], [0, 16]], 0, 0)
     iota(ap("JJ", 0, 256), [[1, 256]], 0, 0)
@@ -207,36 +228,45 @@ def build_ops():
     copy(ap("COL", 0, 3), ap("COLI", 0, 3))
     ts(BO, full("JG"), G16, A.is_equal)
     ts(ID, ap("JJ", 0, 128), P, A.is_equal)
-    ts(ap("EE", 0, 144), ap("JJ", 0, 144), -15.0, A.add, G16, A.is_equal)
+    ts(G15, G16, 15.0, A.add)
+    ts(ap("EE", 0, 144), ap("JJ", 0, 144), G15, A.is_equal, 16.0, A.mult)
+    if "w" in [x[1] for c in cuts for x in c["D"]]:
+        ts(ap("EN", 0, 144), ap("JJ", 0, 144), G15, A.is_equal, -16.0, A.mult)
     ts(ap("MK", 0, 16), ap("JM", 0, 16), K, A.is_equal)
-    ts(full("M16"), full("JM"), K, A.is_equal, 16.0, A.mult)
+    ts(full("M1"), full("JM"), K, A.is_equal)
     ts(ap("BM", 0, 64), ap("JM", 0, 64), K, A.not_equal, BIG, A.mult)
     copy(ap("LC", 0, 8), ap("IOT", 0, 8))
     ts(ap("LB", 0, 8), ap("IOT", 0, 8), 16.0, A.mult, 15.0, A.add)
-    for c, mul, plus in ((WUC, 14.0, 1.0), (K15, -1.0, 4111.0), (K16, 1.0, 16.0)):
+    for c, mul, plus in ((WUC, 14.0, 1.0), (K15, -1.0, 15.0), (K16, 1.0, 16.0)):
         ts(c, K, mul, A.mult, plus, A.add)
+    ts(CMP, mk(15), 7.0, A.mult, -0.5, A.add)
+    ts(WKC, mk(15), -4111.0, A.mult, K, A.add)
     for t, val in ((ONE, 1.0), (QC, 0.25), (MG, MAGIC), (M15, MAGIC * 2 ** 15), (M5, MAGIC * 2 ** 5)):
-        memset(t, val)
-    lin(ap("CA", 0, 64), ONE, 16368.0)
+        memset(ct(t), val)
+    lin(ap("CA", 0, 64), ct(ONE), 16368.0)
     for name, mul in (("NID", -1.0), ("MH", -0.5), ("NEG", -4096.0), ("POS", 4096.0), ("DK", K16), ("D4", mk(4))):
         lin(full(name), ID, mul)
     tt(C19, mk(1), mk(9), A.add)
-    for name, mul in (("WK", K), ("B32", 1.0 / 32), ("SC", C19), ("WP", WUC)):
+    lin(ct(KT15), ct(ONE), K15)
+    ts(full("N15"), BO, mk(15), A.mult, -4096.0, A.mult)
+    ts(full("SQ4"), sele(4), mk(15), A.mult, 1.0 / 16, A.mult)
+    for name, mul in (("WK", WKC), ("B32", 1.0 / 32), ("SC", C19), ("WP", WUC)):
         lin(full(name), BO, mul)
-    ts(full("S32"), BO, mk(4), A.mult, -32.0, A.mult)
+    ts(full("S32"), BO, mk(4), A.mult, -512.0, A.mult)
     ts(full("SU"), BO, mk(2), A.mult, 1.0 / 2048, A.mult)
     ts(full("CE2"), ID, 2048.0, A.mult)
     for k in range(16):
         lin(ap("SELN", 128 * k, 128 * k + 128), full("CE2"), mk(k))
     asel(full("T01"), BO, A.is_gt, 0.0)
     asel(full("TR"), full("T01"), A.not_equal, -1.0)
+    lin(ap("TR", 15, 128, 16), ap("BO", 0, 128, 16))
     lin(ap("WP", 1, 128, 16), ap("BO", 0, 128, 16), 0.0)
     lin(full("WN"), full("WP"), -1.0)
-    ts(ap("CE", 0, 64), ONE, K, A.mult, 2.0, A.is_lt)
-    ts(C0, ap("CE", 0, 64), 2040.0, A.mult, 8.0, A.add)
+    ts(ap("CE", 0, 64), ct(ONE), K, A.mult, 2.0, A.is_lt)
+    ts(ct(C0), ap("CE", 0, 64), 2040.0, A.mult, 8.0, A.add)
     ts(ap("CE", 64, 128), ap("CE", 0, 64), MAGIC * 16 * 255, A.mult, MAGIC * 16, A.add)
     ts(C4, K, 4.0, A.is_lt)
-    lin(MT, ap("CE", 64, 128), C4)
+    lin(ct(MT), ap("CE", 64, 128), C4)
     ts(MSC, K, 2.0, A.is_ge, 1.0 / 16, A.max)
     ts(B1, K, 2.0, A.is_lt, 1279.53125, A.mult)
     ts(B2, K, 4.0, A.is_ge, -7.5, A.mult)
@@ -251,19 +281,24 @@ def build_ops():
     lin(ap("BT", 1, 128, 8), ap("BO", 0, 128, 8), -13152.0)
     for r, mul in ((2, K2), (3, 3232.0), (8, 25.0 / 2048)):
         lin(ap("BT", 128 + r, 256, 16), ap("BO", 0, 128, 16), mul)
-    for name, bank, sign in (("AP", "PA0", ID), ("AN", "PA1", NID)):
+    for name, bank, sign in (("AP", "P0", ID), ("AN", "P4", NID)):
         mm([(ap(bank, 128 + j, 256 + j), [(ap("BT", j, j + 128), sign)]) for j in (0, 128)])
         lin(ap(name, 0, 256), ap(bank, 128, 384))
-    copy(TH, ap("THI", 0, 1))
+    ts(TH, ap("THI", 0, 1), 16.0, A.mult, 4111.0, A.add)
     ts(ap("TB", 0, 192), ap("JJ", 0, 192), -128.0, A.add, 1.0 / 128, A.mult)
     ts(ap("BASE", 0, 144), ap("JJ", 0, 144), 16.0, A.mult, 2032.0, A.add)
-    wide = 16 * max(CUT["F"] + (4,))
+    merges = [x for p in range(len(spans)) for x in pieces("F", p)]
+    wide = 16 * max([t1 - t0 for t0, t1, e in merges if e != "r"] + [4])
     memset(ap("KEEP", 0, wide), 1.0)
     memset(ap("KEEP", 0, wide, 16), 0.0)
     memset(ap("RST", 0, wide), 0.0)
     memset(ap("RST", 0, wide, 16), 2 * BIG)
-    memset(ap("CMP", 0, 64), -0.5)
-    memset(ap("CMP", 64, 128), 6.5)
+    ts(full("ZC"), full("JM"), 256.0, A.mult, -2048.0, A.add)
+    for t0, t1, e in merges:
+        if e != "r":
+            memset(ap("ZC", t0, t1), 0.0)
+    ramp = max([t1 - t0 for t0, t1, e in merges if e == "r"] + [16]) // 16
+    iota(ap("RAMP", 0, 256 * ramp), [[0, ramp], [256, 16], [0, 16]], -2048, 0)
     ts(ap("RD", 0, 8 * SEG), ap("JP", 0, 8 * SEG), K, A.is_equal, -8.0, A.mult)
     ts(ap("RD", 0, 8 * SEG, SEG), ap("RD", 0, 8 * SEG, SEG), 3.0, A.add)
     ts(ap("RD", 64, 8 * SEG, SEG), ap("JP", 64, 8 * SEG, SEG), 0.0, A.mult, 8.0, A.add)
@@ -274,166 +309,225 @@ def build_ops():
     for j in range(0, 1024, 256):
         lin(ap("AD", j, j + 256), ap("ADI", j, j + 256), 1.0 / 2048)
 
-    def state(h, z, early, out):
-        reg = ap("PD%d" % h, 320, 384)
-        close = mm2(reg, [(ID, C0), (MH, ONE)] + early,
-                    [(full("WN"), z), (ID, MT), (NID, MT), (full("WP"), z)])
-        return lambda: (close(), lin(out, reg, MSC, MBI))
-
     copy(ap("CF", 0, 8), ap("CBI", 0, 8))
-    tt(full("CE"), ind(ap("CF", 0, 8), ap("LC", 0, 8)), full("M16"), A.mult)
-    for h in HALVES:
-        reg = ap("PD%d" % h, 320, 384)
-        mm([(reg, [(ID, C0), (MH, ONE), (full("WN"), hs("ZB", h)), (ID, MT), (NID, MT), (full("WP"), hs("ZB", h)),
-                   (sele(1), hs("CE", h))])])
-        lin(fld("ML", 0, h, 1), reg, MSC, MBI)
+    tt(full("CE"), ind(ap("CF", 0, 8), ap("LC", 0, 8)), full("M1"), A.mult)
+    for s, h in enumerate(HALVES):
+        reg, z = ap(PS[4 * s + 1], 256, 320), ap("ZB", 64 * h, 64 * h + 64)
+        mm([(reg, [(ID, ct(C0)), (MH, ct(ONE)), (full("WN"), z), (ID, ct(MT)), (NID, ct(MT)), (full("WP"), z),
+                   (sele(1), ap("CE", 64 * h, 64 * h + 64))])])
+        lin(fld("ML", 0, 64 * h, 64 * h + 64, 1), reg, MSC, MBI)
     ts(coli(5), coli(1), 15442.0, A.mult, 3151.0, A.add)
     ts(coli(6), coli(5), 4095, A.bitwise_and)
     ts(VC, coli(6), -2048.0, A.add)
     lin(ap("WP", 1, 128, 16), ap("BO", 0, 128, 16), VC)
     lin(ap("WN", 1, 128, 16), ap("WP", 1, 128, 16), -1.0)
 
-    for m in range(1, STEPS + 1):
+    VFW = ap("W", 0, 2048)
+
+    def chain(m, p, X, Y, spare):
         last = m == STEPS
-        VFW = ap("W", 0, 2048)
-        tails = []
-        seen.clear()
-        for s, h in enumerate(HALVES):
-            PA, PB, PC, PD = ["P%s%d" % (x, h) for x in "ABCD"]
-            cur[0] = "<>"[s]
-            vs = 2048 + 1024 * s - 1024 * h
-            if m > 1:
-                add({"n": ("recv", (m - 1, h))}, [ap("TOK", 2 * m + h - 2, 2 * m + h - 1)],
-                    [blk("ML", m - 1, b) for b in range(4 * h, 4 * h + 4) if (b + m - 1) % NR], "arr%d_%d" % (m - 1, h))
-            zh = hs("ZB", h) if m == 1 else fld("ML", m - 1, h, 0)
-            mh = fld("ML", m - 1, h, 1)
-            adr = ap(PA, 0, 64)
-            mm2(adr, [(ID, ap("CA", 0, 64))],
-                [(ap("AN", 0, 128), mh), (ap("AN", 128, 256), mh), (ID, M15), (NID, M15),
-                 (ap("AP", 0, 128), mh), (ap("AP", 128, 256), mh), (ID, M5), (NID, M5)])()
-            lin(hs("A16", h), adr, 1.0 / 32)
-            c16 = ap("C16", 4 * h, 4 * h + 4)
-            mm([(ap(PB, 64, 128), [(ID, ap("BM", 0, 64)), (full("SC"), mh)]), (ap(PB, 0, 64), [(full("SC"), mh)])])
-            scan(ap("AL", 128 * h, 128 * h + 64), ap("RST", 0, 64), ap(PB, 64, 128), A.max, A.min)
+        t0, t1 = spans[p]
+        n, h = t1 - t0, t0 // HALF
+        before = sum([b - a for a, b in spans[:p]])
+        vs = 2048 + 16 * (before - t0)
+        al = 128 * h - 64 * h
+
+        def my(name):
+            return ap(name, t0, t1)
+
+        def reg(bank, c):
+            return ap(bank, c, c + n)
+        if m > 1:
+            add({"n": ("recv", (m - 1, p))}, [ap("TOK", 4 * m + p - 4, 4 * m + p - 3)],
+                [blk("ML", m - 1, b) for b in range(t0 // 16, t1 // 16) if (b + m - 1) % NR], "arr%d_%d" % (m - 1, p))
+        zh = my("ZB") if m == 1 else fld("ML", m - 1, t0, t1, 0)
+        mh = fld("ML", m - 1, t0, t1, 1)
+        mm2(reg(X, 0), [(ID, ap("CA", 0, n))],
+            [(ap("AN", 0, 128), mh), (ap("AN", 128, 256), mh), (ID, ct(M15, n)), (NID, ct(M15, n)),
+             (ap("AP", 0, 128), mh), (ap("AP", 128, 256), mh), (ID, ct(M5, n)), (NID, ct(M5, n))])()
+        lin(my("A16"), reg(X, 0), 1.0 / 32)
+        c16 = ap("C16", t0 // 16, t1 // 16)
+        mm([(reg(Y, 0), [(ID, ap("BM", 0, n)), (full("SC"), mh)])])
+        scan(ap("AL", al + t0, al + t1), ap("RST", 0, n), reg(Y, 0), A.max, A.min)
+        if m == 1:
+            lin(c16, ap("CBI", t0 // 16, t1 // 16))
+            copy(my("SF"), ind(ap("LEI", 0, 256), c16))
+        else:
+            lin(c16, ap("AL", al + t0 + 15, al + t1, 16))
+            lin(my("SF"), ind(ap("LE", 0, 256), c16))
+        lin(my("S16"), my("SF"))
+        for a, b in pieces("G", p):
             if m == 1:
-                lin(c16, ap("CBI", 4 * h, 4 * h + 4))
-                copy(hs("SF", h), ind(ap("LEI", 0, 256), c16))
+                lin(ap("G", 16 * a, 16 * b), ind(ap("ADI", 0, 1024), ap("A16", a, b)), 1.0 / 2048)
             else:
-                lin(c16, ap("AL", 128 * h + 15, 128 * h + 64, 16))
-                lin(hs("SF", h), ind(ap("LE", 0, 256), c16))
-            lin(hs("S16", h), hs("SF", h))
-
-            def differ(key, row):
-                for b in range(4):
-                    o = SEG * (8 * h + 4 * key + b)
-                    out, x = ap("DD", o, o + 16 * b + 16), ap(PB, row, row + 16 * b + 16)
-                    own = ap("AL", 128 * h + 64 * key + 16 * b + 15, 128 * h + 64 * key + 16 * b + 16)
-                    add({"a": k_act(out, x, AF.Abs, own, -1.0), "v": k_ts(out, x, own, A.not_equal)}, [x, own], [out])
-            differ(0, 0)
-            for t0, t1 in pieces("G", h):
-                lin(ap("G", 16 * t0, 16 * t1), ind(ap("AD", 0, 1024), ap("A16", t0, t1)))
-            for t0, t1 in pieces("S", h):
-                lin(ap("W", vs + 16 * t0, vs + 16 * t1), ind(VFW, ap("S16", t0, t1)))
-            nn = ap(PA, 64, 128)
-            mm([(nn, [(ap("SELN", 128 * k, 128 * k + 128), ap("G", 1024 * h + k, 1024 * h + 1024, 16))
-                      for k in range(16)])])
-            lin(hs("N16", h), nn)
-            lin(hs("NF", h), nn)
-            side = 0
-            for t0, t1, e in pieces("D", h):
+                lin(ap("G", 16 * a, 16 * b), ind(ap("AD", 0, 1024), ap("A16", a, b)))
+        for a, b in pieces("S", p):
+            lin(ap("W", vs + 16 * a, vs + 16 * b), ind(VFW, ap("S16", a, b)))
+        lanes(reg(X, 64), [(ap("SELN", 128 * k, 128 * k + 128), ap("G", 16 * t0 + k, 16 * t1, 16)) for k in range(16)],
+              True)
+        lin(my("N16"), reg(X, 64))
+        lin(my("NF"), reg(X, 64))
+        side = 0
+        for a, b, e in pieces("D", p):
+            if e != "a":
+                tt(ap("D", 16 * a, 16 * b), ind(VFW, ap("N16", a, b)), ap("W", vs + 16 * a, vs + 16 * b), A.subtract)
                 if e == "v":
-                    tt(ap("D", 16 * t0, 16 * t1), ind(VFW, ap("N16", t0, t1)), ap("W", vs + 16 * t0, vs + 16 * t1),
-                       A.subtract)
-                    act(ap("DA", 16 * t0, 16 * t1), ap("D", 16 * t0, 16 * t1), AF.Abs)
-                    continue
-                act(ap("D", 16 * t0, 16 * t1), ind(VFW, ap("N16", t0, t1)), AF.Copy)
-                for c0 in range(16 * t0, 16 * t1, 256):
-                    c1 = min(c0 + 256, 16 * t1)
-                    pd = ap((PA, PC)[side], 128, 128 + c1 - c0)
-                    side ^= 1
-                    mm([(pd, [(NID, ap("W", vs + c0, vs + c1)), (ID, ap("D", c0, c1))])])
-                    act(ap("DA", c0, c1), pd, AF.Abs)
-            ee = ap(PC, 0, 64)
-            mm([(ee, ([(full("S32"), mh)] if m > 1 else []) +
-                 [(sele(k), ap("DA", 1024 * h + k, 1024 * h + 1024, 16)) for k in range(16)])])
-            r1, r2 = ap(PA, 384, 448), ap(PD, 128, 192)
-            okh = hs("OK", h)
-            fh, sq = ap("FL", 128 * h, 128 * h + 64), ap("FL", 128 * h + 64, 128 * h + 128)
-            close1 = mm2(r1, [(ID, ap("BASE", 64 * s + 1, 64 * s + 65))], [(full("WK"), fh), (full("NEG"), sq)])
-            ts(okh, ee, TH, A.is_le)
-            if not last:
-                lin(hs("KEY", h), ee, 16.0, K15)
-            closez = mm2(ap(PC, 64, 128), [(ID, zh), (ID, QC)],
-                         [(MH, ap("MX", 1024 * h + 15, 1024 * h + 1024, 16)),
-                          (MH, ap("MN", 1024 * h + 15, 1024 * h + 1024, 16)), (ID, MG)])
-            mm([(ap(PD, 0, 64), [(full("TR"), okh)]), (ap(PD, 64, 128), [(BO, okh)])])
-            close2 = mm2(r2, [(ID, ap("BASE", 64 * s, 64 * s + 64)), (full("DK"), okh)], [(full("NEG"), sq)])
-            tt(ap("FL", 128 * h, 128 * h + 128), ap(PD, 0, 128), full("CMP"), A.is_lt)
-            close2()
-            close1()
-            tt(hs("X1", h), r2, hs("NF", h), A.max)
-            tt(hs("X2", h), r1, hs("X1", h), A.max)
-            lin(hs("F16", h), hs("X2", h))
-            for t0, t1 in pieces("F", h):
-                n = 16 * (t1 - t0)
-                lin(ap("FV", 16 * t0, 16 * t1), ind(ap("W", 0, 3072 + 1024 * s), ap("F16", t0, t1)))
-                scan(ap("MX", 16 * t0, 16 * t1), ap("KEEP", 0, n), ap("FV", 16 * t0, 16 * t1), A.mult, A.max)
-                scan(ap("MN", 16 * t0, 16 * t1), ap("RST", 0, n), ap("FV", 16 * t0, 16 * t1), A.max, A.min)
-            mm([(ap(PD, 192, 256), [(ID, hs("SF", h)), (full("NEG"), ONE), (full("POS"), okh)]),
-                (ap(PD, 256, 320), [(ID, hs("NF", h)), (full("NEG"), okh)])])
-            lin(ap("LV", 128 * h, 128 * h + 128), ap(PD, 192, 320))
-            if not last:
-                transp(hs("KT", h), hs("KEY", h))
-                scan(hs("KS", h), ap("KEEP", 0, 64), hs("KT", h), A.mult, A.max)
-                tt(hs("IT", h), ind(hs("KS", h), ap("LB", 0, 4)), hs("KT", h), A.is_equal)
-                transp(hs("II", h), hs("IT", h))
-                tt(hs("IA", h), adr, hs("II", h), A.mult)
-                mm([(ap(PB, 192, 256), [(ID, ap("BM", 0, 64)), (full("B32"), hs("IA", h))]),
-                    (ap(PB, 128, 192), [(full("B32"), hs("IA", h))])])
-                scan(ap("AL", 128 * h + 64, 128 * h + 128), ap("RST", 0, 64), ap(PB, 192, 256), A.max, A.min)
-                differ(1, 128)
-            nk = 4 if last else 8
-            d0 = 8 * SEG * h
-            lin(ap("DD", d0 + 65, d0 + SEG * nk, SEG), ap("AL", 128 * h + 15, 128 * h + 16 * nk, 16), -1.0 / 2048)
-            scan(ap("RR", d0, d0 + SEG * nk), ap("RD", 0, SEG * nk), ap("DD", d0, d0 + SEG * nk), A.add, A.min)
-            lin(ap("O16", 8 * h, 8 * h + nk), ap("RR", d0 + 65, d0 + SEG * nk, SEG), -2048.0)
-            if not last:
-                tt(hs("T1", h), ind(ap("AD", 0, 1088), ap("O16", 8 * h + 4, 8 * h + 8)), hs("II", h), A.subtract)
-            zo = hs("Z16", h) if last else fld("MS", m - 1, h, 0)
-            early = [] if last else ([(full("D4"), mh)] if m > 1 else []) + [(full("D4"), sq)]
-            tails.append((closez, zo, state(h, zo, early, fld("MS", m - 1, h, 1))))
+                    act(ap("DA", 16 * a, 16 * b), ap("D", 16 * a, 16 * b), AF.Abs)
+                else:
+                    ts(ap("DA", 16 * a, 16 * b), ap("D", 16 * a, 16 * b), 0.0, A.max, 2.0, A.mult)
+                continue
+            act(ap("D", 16 * a, 16 * b), ind(VFW, ap("N16", a, b)), AF.Copy)
+            for c0 in range(16 * a, 16 * b, 256):
+                c1 = min(c0 + 256, 16 * b)
+                pd = ap((X, spare)[side], 128, 128 + c1 - c0)
+                side ^= 1
+                mm([(pd, [(NID, ap("W", vs + c0, vs + c1)), (ID, ap("D", c0, c1))])])
+                act(ap("DA", c0, c1), pd, AF.Abs)
+        mm([(reg(Y, 64), [(full("POS"), ct(ONE, n)), (ID, ct(KT15, n))] + ([(full("S32"), mh)] if m > 1 else []))],
+           True, False)
+        halved = [x for x in pieces("D", p) if x[2] == "w"]
+        if halved:
+            a, b = halved[0][0], halved[-1][1]
+            mm([(ap(Y, 64 + a - t0, 64 + b - t0),
+                 [(ap("EN", 15 - k, 143 - k), ap("D", 16 * a + k, 16 * b, 16)) for k in range(16)])], False, False)
+        lanes(reg(Y, 64), [(sele(k), ap("DA", 16 * t0 + k, 16 * t1, 16)) for k in range(16)], False)
+        r1, r2 = reg(X, 384), reg(Y, 192)
+        close1 = mm2(r1, [(ID, ap("BASE", before + 1, before + n + 1))], [(full("WK"), my("FL"))])
+        ts(my("OK"), reg(Y, 64), TH, A.is_le)
+        mm([(reg(Y, 128), [(full("TR"), my("OK"))])])
+        close2 = mm2(r2, [(ID, ap("BASE", before, before + n)), (full("DK"), my("OK"))], [(full("N15"), my("FL"))])
+        ts(my("FL"), reg(Y, 128), CMP, A.is_lt)
+        close2()
+        close1()
+        tt(my("X1"), r2, my("NF"), A.max)
+        tt(my("X2"), r1, my("X1"), A.max)
+        lin(my("F16"), my("X2"))
+        mn = t0 // 32 * 32
+        closez = mm2(reg(X, 448), [(ID, zh), (ID, ct(QC, n))] +
+                     [(ID, my("ZC"))] * ("r" in [x[2] for x in pieces("F", p)]),
+                     [(MH, ap("MX", 16 * t0 + 15, 16 * t1, 16)), (MH, ap("MN", mn + 16 * t0 + 15, mn + 16 * t1, 16)),
+                      (ID, ct(MG, n))])
+        zo = my("Z16") if last else fld("MS", m - 1, t0, t1, 0)
+        early = [] if last else ([(full("D4"), mh)] if m > 1 else []) + [(full("SQ4"), my("FL"))]
+        closem = mm2(reg(Y, 256), [(ID, ct(C0, n)), (MH, ct(ONE, n))] + early,
+                     [(full("WN"), zo), (ID, ct(MT, n)), (NID, ct(MT, n)), (full("WP"), zo)])
+        for a, b, e in pieces("F", p):
+            c0, c1 = 16 * a, 16 * b
+            src = ind(ap("W", 0, vs + 16 * t1), ap("F16", a, b))
+            if e == "r":
+                tt(ap("FV", c0, c1), src, ap("RAMP", 0, c1 - c0), A.add)
+                for c in range(c0, c1, 256):
+                    scan(ap("MX", c + 1, c + 256, 2), ap("FV", c, c + 256, 2), ap("FV", c + 1, c + 256, 2),
+                         A.max, A.max, -4096.0)
+                    scan(ap("MN", mn + c + 269, mn + c + 14, -2), ap("FV", c + 255, c, -2),
+                         ap("FV", c + 254, c - 1, -2), A.min, A.min, 4096.0)
+                continue
+            act(ap("FV", c0, c1), src, AF.Copy)
+            scan(ap("MX", c0, c1), ap("KEEP", 0, c1 - c0), ap("FV", c0, c1), A.mult, A.max)
+            scan(ap("MN", mn + c0, mn + c1), ap("RST", 0, c1 - c0), ap("FV", c0, c1), A.max, A.min)
+        closez()
+        act(zo, reg(X, 448), AF.Abs, MGN)
+        closem()
+        lin(fld("MS", m - 1, t0, t1, 1), reg(Y, 256), MSC, MBI)
+        if not last:
+            away = [blk("MS", m - 1, b) for b in range(t0 // 16, t1 // 16) if (b + m) % NR]
+            add({"g": ("send", (m, p))}, away, [ap("TOK", 4 * m + p, 4 * m + p + 1)], "none")
+            for b in range(t0 // 16, t1 // 16):
+                if (b + m) % NR == 0:
+                    lin(blk("ML", m, b), blk("MS", m - 1, b))
 
-        for s, h in enumerate(HALVES):
-            PB, PC = "PB%d" % h, "PC%d" % h
-            cur[0] = "<>"[s]
-            closez, zo, closem = tails[s]
-            mo = fld("MS", m - 1, h, 1)
-            closez()
-            act(zo, ap(PC, 64, 128), AF.Abs, MGN)
-            closem()
-            if not last:
-                away = []
-                for b in range(4 * h, 4 * h + 4):
-                    if (b + m) % NR:
-                        away.append(blk("MS", m - 1, b))
-                    else:
-                        lin(blk("ML", m, b), blk("MS", m - 1, b))
-                add({"g": ("send", (m, h))}, away, [ap("TOK", 2 * m + h, 2 * m + h + 1)], "none")
-            mm([(ap(PB, 320, 384), [(ID, ap("BM", 0, 64)), (ID, ap("TB", 128, 192)), (full("SU"), mo)])])
-            scan(hs("XS", h), ap("RST", 0, 64), ap(PB, 320, 384), A.max, A.min)
-            lin(ap("W16", 4 * h, 4 * h + 4), ap("XS", 64 * h + 15, 64 * h + 64, 16), 2048.0)
-            tt(ind(ap("LE", 0, 320), ap("O16", 8 * h, 8 * h + 4)), ap("LV", 128 * h, 128 * h + 64),
-               ap("LV", 128 * h + 64, 128 * h + 128), A.max)
-            if not last:
-                mm([(ap(PB, 256, 320), [(ID, hs("TB", h)), (full("SU"), mo)])])
-                tt(hs("T2", h), ap(PB, 256, 320), hs("II", h), A.add)
-                tt(ind(ap("AD", 0, 1088), ap("O16", 8 * h + 4, 8 * h + 8)), hs("T1", h), hs("T2", h), A.max)
-            copy(ind(ap("W", 1024 * h, 1024 * h + 1024), ap("W16", 4 * h, 4 * h + 4)), zo)
+    def aside(m, s, mine, places):
+        last, h = m == STEPS, HALVES[s]
+        crow, arow, amask, old, lv = places[:5]
+
+        def hs(name):
+            return ap(name, HALF * h, HALF * h + HALF)
+
+        def differ(key, row):
+            for b in range(4):
+                o = SEG * (8 * h + 4 * key + b)
+                out, x = ap("DD", o, o + 16 * b + 16), ap(row[0], row[1], row[1] + 16 * b + 16)
+                own = ap("AL", 128 * h + 64 * key + 16 * b + 15, 128 * h + 64 * key + 16 * b + 16)
+                add({"a": k_act(out, x, AF.Abs, own, -1.0), "v": k_ts(out, x, own, A.not_equal)}, [x, own], [out])
+        mm([(crow, [(full("SC"), fld("ML", m - 1, HALF * h, HALF * h + HALF, 1))])])
+        differ(0, crow)
+        mm([(ap(lv[0], lv[1], lv[1] + 64), [(ID, hs("SF")), (full("NEG"), ct(ONE)), (full("POS"), hs("OK"))]),
+            (ap(lv[0], lv[1] + 64, lv[2]), [(ID, hs("NF")), (full("NEG"), hs("OK"))])])
+        lin(ap("LV", 128 * h, 128 * h + 128), lv)
+        if not last:
+            for p, X, Y in mine:
+                transp(ap("KT", spans[p][0], spans[p][1]), ap(Y, 64, 64 + spans[p][1] - spans[p][0]))
+            scan(hs("KS"), ap("KEEP", 0, 64), hs("KT"), A.mult, A.max)
+            tt(hs("IT"), ind(hs("KS"), ap("LB", 0, 4)), hs("KT"), A.is_equal)
+            transp(hs("II"), hs("IT"))
+            for p, X, Y in mine:
+                a, b = spans[p]
+                tt(ap("IA", a, b), ap(X, 0, b - a), ap("II", a, b), A.mult)
+            mm([(amask, [(ID, ap("BM", 0, 64)), (full("B32"), hs("IA"))]), (arow, [(full("B32"), hs("IA"))])])
+            scan(ap("AL", 128 * h + 64, 128 * h + 128), ap("RST", 0, 64), amask, A.max, A.min)
+            differ(1, arow)
+        for k0, k1 in ((0, 4),) if last else ((0, 4), (4, 8)) if OPT["apart"][s] else ((0, 8),):
+            d0, d1 = SEG * (8 * h + k0), SEG * (8 * h + k1)
+            lin(ap("DD", d0 + 65, d1, SEG), ap("AL", 128 * h + 16 * k0 + 15, 128 * h + 16 * k1, 16), -1.0 / 2048)
+            scan(ap("RR", d0, d1), ap("RD", SEG * k0, SEG * k1), ap("DD", d0, d1), A.add, A.min)
+            lin(ap("O16", 8 * h + k0, 8 * h + k1), ap("RR", d0 + 65, d1, SEG), -2048.0)
+        if not last:
+            was = ind(ap("AD", 0, 1088), ap("O16", 8 * h + 4, 8 * h + 8))
+            if OPT["old"][s]:
+                act(hs("OG"), was, AF.Copy)
+                mm([(old, [(ID, hs("OG")), (NID, hs("II"))])])
+                act(hs("T1"), old, AF.Copy)
+            else:
+                tt(hs("T1"), was, hs("II"), A.subtract)
+
+    def writes(m, s, mine, places):
+        last, h = m == STEPS, HALVES[s]
+        name, masked = places[5:]
+        t0, t1 = HALF * h, HALF * h + HALF
+        tt(ind(ap("LE", 0, 320), ap("O16", 8 * h, 8 * h + 4)), ap("LV", 128 * h, 128 * h + 64),
+           ap("LV", 128 * h + 64, 128 * h + 128), A.max)
+        if not last:
+            mm([(name, [(ID, ap("TB", t0, t1)), (ID, ap("II", t0, t1)), (full("SU"), fld("MS", m - 1, t0, t1, 1))])])
+            lin(ap("T2", t0, t1), name)
+            tt(ind(ap("AD", 0, 1088), ap("O16", 8 * h + 4, 8 * h + 8)), ap("T1", t0, t1), ap("T2", t0, t1), A.max)
+        for j, (a, b) in enumerate([spans[p] for p, X, Y in mine] if last else [(t0, t1)]):
+            reg = ap(masked[0], masked[1] + a - t0, masked[1] + b - t0)
+            mm([(reg, [(ID, ap("BM", 0, b - a)), (ID, ap("TB", 128, 128 + b - a)),
+                       (full("SU"), fld("MS", m - 1, a, b, 1))])])
+            scan(ap("XS", a, b), ap("RST", 0, b - a), reg, A.max, A.min)
+            lin(ap("W16", a // 16, b // 16), ap("XS", a + 15, b, 16), 2048.0)
+            copy(ind(ap("W", 16 * a, 16 * b), ap("W16", a // 16, b // 16)),
+                 ap("Z16", a, b) if last else fld("MS", m - 1, a, b, 0))
+            if last:
+                add({"sa"[(s + j) % 2]: ("store", ("yv", (16 * a, 16 * b), ap("W", 16 * a, 16 * b)))},
+                    [ap("W", 16 * a, 16 * b)], [], "st_yv%d" % mine[j][0])
+
+    for m in range(1, STEPS + 1):
+        seen.clear()
+        todo = []
+        for s in range(2):
+            B = PS[4 * s:4 * s + 4]
+            p0 = s * len(PARTS[0])
+            if len(PARTS[s]) == 1:
+                mine, spare = [(p0, B[0], B[1])], B[3]
+                places = [ap(B[2], c, c + n) for c, n in ((128, 64), (192, 64), (256, 64), (320, 64), (384, 128),
+                                                          (0, 64), (64, 64))]
+            else:
+                mine, spare = [(p0, B[0], B[1]), (p0 + 1, B[2], B[3])], None
+                places = [ap(B[0], c, c + 64) for c in (128, 192, 256, 320)] + \
+                    [ap(B[1], 320, 448), ap(B[1], 448, 512), ap(B[1], 0, 64)]
+            for p, X, Y in mine:
+                cur[:] = ["abcd"[p], len(spans) - 1 - p, m]
+                chain(m, p, X, Y, spare or X)
+            cur[:] = ["<>"[s], 0, m]
+            aside(m, s, mine, places)
+            todo.append((m, s, mine, places))
+        for x in todo:
+            cur[0] = "<>"[x[1]]
+            writes(*x)
 
     add({"s": ("store", ("yl", None, ap("LE", 0, 256)))}, [ap("LE", 0, 256)], [], "st_yl")
     add({"s": ("store", ("yz", None, full("Z16")))}, [full("Z16")], [], "st_yz")
-    add({"s": ("store", ("yv", (1024, 2048), ap("W", 1024, 2048)))}, [ap("W", 1024, 2048)], [], "st_yv1")
-    add({"a": ("store", ("yv", (0, 1024), ap("W", 0, 1024)))}, [ap("W", 0, 1024)], [], "st_yv0")
     return ops
 
 
@@ -483,30 +577,41 @@ def cost(o, e, c):
             n *= 1 if [x for x in o["r"] if x[0] in PS] else 2
         elif all([x[0] in _S and _S[x[0]][0] in (BF, F16, U16) for x in o["r"] + o["w"] if cnt(x) > 1]):
             n /= 2
-    return max(64, n) * c["cy"]
+    return max(64, n) * c["cy"] + c["call" + e]
 
 
-def plan(ops, c):
-    deps = dependencies(ops)
-    n = len(ops)
-    costs = [{e: cost(o, e, c) for e in o["alt"]} for o in ops]
-    late = [0.0] * n
+def lags(ops, c):
+    late, ahead = [0.0] * len(ops), 0.0
     for i, o in enumerate(ops):
         k, a = list(o["alt"].values())[0]
         if k == "send":
             late[i] = c["way"]
         elif k in ("load", "store"):
             x = a[0] if k == "load" else a[2]
-            late[i] = c["dma"] + 128 * cnt(x) * (4 if _S[x[0]][0] in (F32, I32) else 2) / c["bw"]
+            t = 128 * cnt(x) * (4 if _S[x[0]][0] in (F32, I32) else 2) / c["bw"]
+            ahead = ahead + t if k == "load" else t
+            late[i] = c["dma"] + ahead
+    return late
+
+
+def waits_for(ops, deps, i, e, eng):
+    return [j for j in deps[i] if not (e == "p" and eng[j] == "p") and "load" != ops[i]["alt"][e][0]]
+
+
+def plan(ops, c):
+    deps = dependencies(ops)
+    n = len(ops)
+    costs = [{e: cost(o, e, c) for e in o["alt"]} for o in ops]
+    late = lags(ops, c)
     succ = [[] for _ in ops]
     for i in range(n):
         for j in deps[i]:
             succ[j].append(i)
     togo = [0.0] * n
     for i in range(n - 1, -1, -1):
-        togo[i] = min(costs[i].values()) + late[i] + max([togo[j] + c["hop"] for j in succ[i]] + [0.0])
-    rank = [togo[i] + (c["lead"] if "<" in o["tag"] and not o["tag"].startswith(ASIDE) else 0.0)
-            for i, o in enumerate(ops)]
+        togo[i] = min(costs[i].values()) + late[i] + max(
+            [togo[j] + c["same" if set(costs[i]) & set(costs[j]) else "hop"] for j in succ[i]] + [0.0])
+    rank = [togo[i] + c["lead"] * o["lead"] for i, o in enumerate(ops)]
     banks = [set([x[0] for x in o["r"] + o["w"] if x[0] in PS]) for o in ops]
     left = [len(d) for d in deps]
     ready = [i for i in range(n) if not left[i]]
@@ -516,9 +621,9 @@ def plan(ops, c):
         for i in ready:
             best = None
             for e, t in costs[i].items():
-                w = [j for j in deps[i] if not (e == "p" and eng[j] == "p")]
+                w = waits_for(ops, deps, i, e, eng)
                 w += [j for b in banks[i] for x, j in used.get(b, {}).items() if x != e]
-                at = max([free.get(e, 0.0)] + [fin[j] + c["hop"] for j in w])
+                at = max([free.get(e, 0.0)] + [fin[j] + c["same" if eng[j] == e else "hop"] for j in w])
                 end = at + t + (c["spare"] * t + c["plus"] if e == "v" else 0.0)
                 if best is None or end < best[4]:
                     best = (at, t, e, w, end)
@@ -539,20 +644,21 @@ def plan(ops, c):
     return order, eng, waits
 
 
-def routes(T, topo, m, h):
+def routes(T, topo, m, p):
     out = []
+    t0, t1 = parts()[p]
     for r in range(NR):
-        src, mine, used = T.cores[r], [], []
-        for b in range(4 * h, 4 * h + 4):
+        src, mine, turn = T.cores[r], [], p
+        for b in range(t0 // 16, t1 // 16):
             if (b + m) % NR == 0:
                 continue
             dst = T.cores[(r + b + m) % NR]
             via = None
             if not topo.may_write(src, dst):
-                able = [c for c in topo.cores_of(src) if c != src and T.rank_of(c) is None and topo.may_write(c, dst)]
-                able.sort(key=lambda c: (c in used, topo.die(c) != topo.die(src), c))
-                via = able[0]
-                used.append(via)
+                able = [c for c in topo.cores_of(src) if c != src and T.rank_of(c) is None and topo.may_write(c, dst)
+                        and topo.die(c) == topo.die(src)]
+                via = able[turn % len(able)]
+                turn += 1
             mine.append((b, dst, via))
         out.append(mine)
     return out
@@ -561,12 +667,12 @@ def routes(T, topo, m, h):
 def engine_masks(topo, src, mine):
     direct = [x for x in mine if x[2] is None]
     relay = [x for x in mine if x[2] is not None]
-    off = topo.engines(src, direct[0][1])
+    off = topo.engines(src, direct[0][1]) if direct else []
     on = [e for e in topo.engines(src, relay[0][2]) if e not in off]
     res = {}
     for group, eng in ((direct, off), (relay, on)):
-        k = len(eng) // len(group)
         for i, x in enumerate(group):
+            k = len(eng) // len(group)
             res[x[0]] = eng[i * k:(i + 1) * k]
     return res
 
@@ -575,9 +681,9 @@ def as_mask(eng):
     return sum([1 << e for e in eng])
 
 
-def arrivals(T, topo, m, h, core):
+def arrivals(T, topo, m, p, core):
     total = 0
-    for r, mine in enumerate(routes(T, topo, m, h)):
+    for r, mine in enumerate(routes(T, topo, m, p)):
         em = engine_masks(topo, T.cores[r], mine)
         for b, dst, via in mine:
             if dst == core:
@@ -588,11 +694,11 @@ def arrivals(T, topo, m, h, core):
 def relay_program(g, core, T, topo):
     sent = 0
     for m in range(1, STEPS):
-        for h in HALVES:
-            for r, mine in enumerate(routes(T, topo, m, h)):
+        for p in range(len(parts())):
+            for r, mine in enumerate(routes(T, topo, m, p)):
                 for b, dst, via in mine:
                     if via == core:
-                        sem = T.sem["arr%d_%d" % (m, h)]
+                        sem = T.sem["arr%d_%d" % (m, p)]
                         g.wait_ge(sem, len(engine_masks(topo, T.cores[r], mine)[b]))
                         blk = T["ML"][:, m * SLOT + b * BLK:m * SLOT + b * BLK + BLK]
                         rid, pid = topo.addr(dst, core)
@@ -623,7 +729,7 @@ def rank_program(g, core, T, topo):
             return T[x[0]][:, x[1]:x[2]].indirect(P(x[4]))
         if x[3] == 1:
             return T[x[0]][:, x[1]:x[2]]
-        return T[x[0]][:, x[1]:x[2]:x[3]]
+        return T[x[0]][:, x[1]:(x[2] if x[2] >= 0 else None):x[3]]
 
     count = {"v": 0, "a": 0, "p": 0, "g": 0}
     known = {"v": {}, "a": {}, "p": {}, "g": {}, "s": {}}
@@ -659,15 +765,15 @@ def rank_program(g, core, T, topo):
             own.append(o["sem"])
             continue
         if k == "send":
-            m, h = a
-            mine = routes(T, topo, m, h)[rank]
+            m, p = a
+            mine = routes(T, topo, m, p)[rank]
             em = engine_masks(topo, core, mine)
             trs = {True: [], False: []}
             for b, dst, via in mine:
                 rid, pid = topo.addr(dst if via is None else via, core)
                 trs[via is None].append(RemoteDMATransfer(
                     dst_ids=[DstId(rid=rid, pnc=pid)], dma_engine_mask=as_mask(em[b]),
-                    remote_sem=T.sem["arr%d_%d" % (m, h)],
+                    remote_sem=T.sem["arr%d_%d" % (m, p)],
                     src=T["MS"][:, (m - 1) * SLOT + b * BLK:(m - 1) * SLOT + b * BLK + BLK],
                     dst=T["ML"][:, m * SLOT + b * BLK:m * SLOT + b * BLK + BLK]))
                 sent += len(em[b])

from concourse.bass import DstId, RemoteDMATransfer
from concourse.mybir import AluOpType, ActivationFunctionType

F32, BF, F16, I32, U16 = "float32", "bfloat16", "float16", "int32", "uint16"
STEPS, NR, HALF = 5, 8, 64
BLK = 32
SLOT = 8 * BLK
SEG = 66
BIG = float(2 ** 25)
MAGIC = 1.5 * 2 ** 23
HALVES = (1, 0)

_S = {
    "W": (BF, 4096), "ADI": (I32, 1024), "LEI": (I32, 256), "AD": (F32, 1088), "LE": (F32, 320),
    "G": (F16, 2048), "D": (BF, 2048), "DA": (BF, 2048), "FV": (F16, 2048), "MX": (F16, 2048), "MN": (F16, 2176),
    "SELN": (BF, 2048), "EE": (BF, 144), "EN": (BF, 144), "ML": (F16, 5 * SLOT), "MS": (F16, 5 * SLOT),
    "CBI": (I32, 8), "KAI": (I32, 8), "THI": (I32, 8), "CF": (F32, 8), "COL": (F32, 32), "COLI": (I32, 16),
    "JJ": (BF, 256), "JM": (BF, 128), "JG": (BF, 128), "JP": (BF, 8 * SEG), "IOT": (I32, 8), "IOF": (F32, 8),
    "MK": (F32, 16), "CT": (BF, 512), "ZC": (BF, 128), "OG": (F16, 128), "RAMP": (BF, 512), "CA": (F16, 64),
    "WP": (F16, 128), "WN": (F16, 128), "BT": (F16, 256), "AP": (F16, 256), "AN": (F16, 256), "T01": (BF, 128),
    "BM": (BF, 64), "M1": (BF, 128), "CE": (BF, 128), "CE2": (BF, 128), "TB": (BF, 192), "BASE": (BF, 144),
    "KEEP": (BF, 512), "RST": (BF, 512),
    "RD": (F16, 8 * SEG), "DD": (F16, 16 * SEG), "RR": (F16, 16 * SEG),
    "LB": (U16, 8), "LC": (U16, 8), "C16": (U16, 8), "S16": (U16, 128), "A16": (U16, 128), "N16": (U16, 128),
    "F16": (U16, 128), "W16": (U16, 8), "O16": (U16, 16),
    "ZB": (BF, 128), "SF": (F16, 128), "NF": (F16, 128), "OK": (BF, 128), "FL": (BF, 128), "X1": (F32, 128),
    "X2": (F32, 128), "Z16": (BF, 128), "XS": (F32, 128), "LV": (F32, 256),
    "KT": (F32, 128), "KS": (F32, 128), "IT": (BF, 128), "II": (BF, 128), "IA": (F16, 128),
    "AL": (F32, 256), "T1": (F32, 128), "T2": (F32, 128),
}
for _n in ("ID", "NID", "MH", "BO", "TR", "WK", "DK", "NEG", "POS", "B32", "S32", "SC", "SU", "D4", "N15", "SQ4"):
    _S[_n] = (BF, 128)
PS = ["P%d" % b for b in range(8)]
SCRATCH = {}
for _n in _S:
    SCRATCH[_n] = ("sbuf", [128, _S[_n][1]], _S[_n][0])
for _n in PS:
    SCRATCH[_n] = ("psum", [128, 512], F32)

LOADS = ["z0", "cb", "ka", "le", "th", "ad", "vf"]
SEMAPHORES = ["cv", "ca", "cp", "cg", "sent", "st_yl", "st_yz"] + ["ld_" + x for x in LOADS] + \
    ["st_yv%d" % p for p in range(4)] + ["arr%d_%d" % (m, p) for m in range(1, STEPS) for p in range(4)]
CNT = {"v": "cv", "a": "ca", "p": "cp", "g": "cg"}

PARTS = [[{'G': (16, 48), 'S': (28, 36), 'D': ((16, 'a'), (24, 'v'), (24, 'v')), 'F': ((32, 'r'), (32, 'a'))}],
         [{'G': (16, 16, 16, 16), 'S': (40, 24), 'D': ((16, 'a'), (16, 'a'), (32, 'v')),
           'F': ((16, 'r'), (24, 'a'), (24, 'a'))}]]
OPT = {'apart': (0, 1), 'old': (1, 0), 'run': 16}
PIN = {'DD>9': 'a', 'Wa2': 'v', 'C16b1': 'a', 'DD>2': 'a', 'Gb3': 'a', 'SFb1': 'v', 'Wb1': 'a', 'F16b1': 'a', 'T2>1': 'v',
       'DD>5': 'a', 'N16a1': 'a', 'DD<2': 'a', 'Wa1': 'a', 'DD<7': 'a', 'Wb2': 'v', 'F16a1': 'v', 'DD>3': 'a',
       'DD<3': 'a', 'MLa2': 'a', 'Gb4': 'v', 'MSb1': 'v', 'DD<5': 'a', 'NFb1': 'a', 'LV<1': 'a', 'W16<1': 'a',
       'DD<10': 'a', 'Gb1': 'a', 'A16a1': 'a', 'DD<8': 'a', 'MLa1': 'a'}
PLAN = {"cy": 0.9, "pe": 0.58, "ga": 1.56, "sc": 3.8, "hop": 115.0, "same": 115.0, "callv": 62.0, "calla": 45.0,
        "send": 800.0, "way": 5400.0, "dma": 2000.0,
        "bw": 250.0, "look": 60.0, "spare": 0.15, "plus": 200.0, "slip": 30.0, "lead": 1500.0}


def parts():
    out = []
    for s, h in enumerate(HALVES):
        n = HALF // len(PARTS[s])
        out += [(HALF * h + HALF - n * (j + 1), HALF * h + HALF - n * j) for j in range(len(PARTS[s]))]
    return out


def ap(n, a, b, s=1):
    return (n, a, b, s, None)


def ind(win, off):
    return (win[0], win[1], win[2], 1, off)


def cnt(x):
    if x[4] is not None:
        return 16 * (x[4][2] - x[4][1])
    return len(range(x[1], x[2], x[3]))


def bits(x):
    r = range(x[1], x[2], x[3])
    s = abs(x[3])
    return (((1 << (len(r) * s)) - 1) // ((1 << s) - 1)) << min(r[0], r[-1])


def build_ops():
    ops = []
    cur, seen = ["-", 0, 0], {}
    A = AluOpType
    AF = ActivationFunctionType

    def add(alt, r, w, sem=None):
        rr = []
        for x in r:
            if isinstance(x, tuple):
                rr.append(x)
                if x[4] is not None:
                    rr.append(x[4])
        for x in w:
            if x[4] is not None:
                rr.append(x[4])
        tag = (w[0][0] if w else "out") + cur[0]
        seen[tag] = seen.get(tag, 0) + 1
        tag += str(seen[tag])
        if tag in PIN and len(alt) > 1:
            alt = {PIN[tag]: alt[PIN[tag]]}
        ops.append({"alt": alt, "r": rr, "w": w, "sem": sem, "tag": tag, "lead": cur[1], "step": cur[2]})

    def k_ts(out, x, s1, op0, s2=None, op1=None):
        return ("ts", (out, x, s1, s2, op0, op1))

    def k_act(out, x, func, bias=None, scale=None):
        return ("act", (out, x, func, bias, scale))

    def copy(out, x):
        add({"v": ("copy", (out, x))}, [x], [out])

    def lin(out, x, mul=None, plus=None):
        if mul is None and plus is None:
            v = ("copy", (out, x))
        elif plus is None:
            v = k_ts(out, x, mul, A.mult)
        elif mul is None:
            v = k_ts(out, x, plus, A.add)
        else:
            v = k_ts(out, x, mul, A.mult, plus, A.add)
        add({"v": v, "a": k_act(out, x, AF.Copy if plus is None else AF.Identity, plus, mul)}, [x, mul, plus], [out])

    def tt(out, x, y, op):
        add({"v": ("tt", (out, x, y, op))}, [x, y], [out])

    def ts(out, x, s1, op0, s2=None, op1=None):
        add({"v": k_ts(out, x, s1, op0, s2, op1)}, [x, s1, s2], [out])

    def scan(out, d0, d1, op0, op1, first=0.0):
        add({"v": ("scan", (out, d0, d1, first, op0, op1))}, [d0, d1], [out])

    def transp(out, x):
        add({"v": ("tr", (out, x))}, [x], [out])

    def memset(out, val):
        add({"v": ("memset", (out, val))}, [], [out])

    def act(out, x, func, bias=None, scale=None):
        add({"a": k_act(out, x, func, bias, scale)}, [x, bias, scale], [out])

    def mm(groups, first=True, final=True):
        lst, r, w = [], [], []
        for out, terms in groups:
            w.append(out)
            (r if first and final else w).append(ap("lock" + out[0], 0, 1))
            for i, (l, x) in enumerate(terms):
                lst.append((out, l, x, first and i == 0, final and i == len(terms) - 1))
                r += [l, x]
        add({"p": ("mm", lst)}, r, w)

    def mm2(out, early, late):
        mm([(out, early)], True, False)
        return lambda: mm([(out, late)], False, True)

    def lanes(out, terms, first):
        n = OPT["run"]
        for j in range(0, 16, n):
            mm([(out, terms[j:j + n])], first and j == 0, j + n >= 16)

    def iota(out, pattern, base, cm):
        add({"g": ("iota", (out, pattern, base, cm))}, [], [out])

    def asel(out, x, op, fill):
        add({"g": ("asel", (out, x, op, fill))}, [x], [out])

    def col(j):
        return ap("COL", j, j + 1)

    def coli(j):
        return ap("COLI", j, j + 1)

    def mk(j):
        return ap("MK", j, j + 1)

    def full(n):
        return ap(n, 0, 128)

    def fld(buf, m, t0, t1, f):
        return ap(buf, m * SLOT + 2 * t0 + f, m * SLOT + 2 * t1, 2)

    def blk(buf, m, b):
        return ap(buf, m * SLOT + b * BLK, m * SLOT + b * BLK + BLK)

    def sele(k):
        return ap("EE", 15 - k, 143 - k)

    def ct(j, n=HALF):
        return ap("CT", 64 * j, 64 * j + n)

    cuts = PARTS[0] + PARTS[1]
    spans = parts()

    def pieces(name, p):
        t, out = spans[p][0], []
        for x in cuts[p][name]:
            n = x[0] if name in "DF" else x
            out.append((t, t + n, x[1]) if name in "DF" else (t, t + n))
            t += n
        return out

    ID, NID, MH, BO = full("ID"), full("NID"), full("MH"), full("BO")
    ONE, QC, MG, M15, M5, MT, C0, KT15 = range(8)

    for e, name, out in (("s", "z0", full("ZB")), ("a", "ka", ap("KAI", 0, 1)), ("s", "cb", ap("CBI", 0, 8)),
                         ("a", "le", ap("LEI", 0, 256)), ("s", "ad", ap("ADI", 0, 1024)), ("s", "vf", ap("W", 0, 2048)),
                         ("a", "th", ap("THI", 0, 1))):
        add({e: ("load", (out, name))}, [ap("queue" + e, 0, 1)], [out, ap("queue" + e, 0, 1)], "ld_" + name)

    P, K, G16, K15, K16, WUC, VC, TH, MGN, W1, K2, C19, C4, MSC, MBI, B1, B2, B3, G15, CMP, WKC = \
        [col(j) for j in range(21)]
    iota(coli(0), [[0, 1]], 0, 1)
    iota(full("JG"), [[16, 8], [0, 16]], 0, 0)
    iota(ap("JJ", 0, 256), [[1, 256]], 0, 0)
    iota(full("JM"), [[0, 8], [1, 16]], 0, 0)
    iota(ap("IOT", 0, 8), [[1, 8]], 0, 0)
    iota(MGN, [[0, 1]], -int(MAGIC), 0)
    iota(ap("JP", 0, 8 * SEG), [[0, 2], [-16, 4], [1, SEG]], 0, 0)
    iota(ap("IOF", 0, 8), [[768, 2], [16, 4]], 256, 0)
    iota(ap("AD", 1024, 1088), [[0, 64]], 0, 0)
    ts(coli(1), coli(0), 15, A.bitwise_and)
    ts(coli(2), coli(0), 112, A.bitwise_and)
    copy(ap("COL", 0, 3), ap("COLI", 0, 3))
    ts(BO, full("JG"), G16, A.is_equal)
    ts(ID, ap("JJ", 0, 128), P, A.is_equal)
    ts(G15, G16, 15.0, A.add)
    ts(ap("EE", 0, 144), ap("JJ", 0, 144), G15, A.is_equal, 16.0, A.mult)
    if "w" in [x[1] for c in cuts for x in c["D"]]:
        ts(ap("EN", 0, 144), ap("JJ", 0, 144), G15, A.is_equal, -16.0, A.mult)
    ts(ap("MK", 0, 16), ap("JM", 0, 16), K, A.is_equal)
    ts(full("M1"), full("JM"), K, A.is_equal)
    ts(ap("BM", 0, 64), ap("JM", 0, 64), K, A.not_equal, BIG, A.mult)
    copy(ap("LC", 0, 8), ap("IOT", 0, 8))
    ts(ap("LB", 0, 8), ap("IOT", 0, 8), 16.0, A.mult, 15.0, A.add)
    for c, mul, plus in ((WUC, 14.0, 1.0), (K15, -1.0, 15.0), (K16, 1.0, 16.0)):
        ts(c, K, mul, A.mult, plus, A.add)
    ts(CMP, mk(15), 7.0, A.mult, -0.5, A.add)
    ts(WKC, mk(15), -4111.0, A.mult, K, A.add)
    for t, val in ((ONE, 1.0), (QC, 0.25), (MG, MAGIC), (M15, MAGIC * 2 ** 15), (M5, MAGIC * 2 ** 5)):
        memset(ct(t), val)
    lin(ap("CA", 0, 64), ct(ONE), 16368.0)
    for name, mul in (("NID", -1.0), ("MH", -0.5), ("NEG", -4096.0), ("POS", 4096.0), ("DK", K16), ("D4", mk(4))):
        lin(full(name), ID, mul)
    tt(C19, mk(1), mk(9), A.add)
    lin(ct(KT15), ct(ONE), K15)
    ts(full("N15"), BO, mk(15), A.mult, -4096.0, A.mult)
    ts(full("SQ4"), sele(4), mk(15), A.mult, 1.0 / 16, A.mult)
    for name, mul in (("WK", WKC), ("B32", 1.0 / 32), ("SC", C19), ("WP", WUC)):
        lin(full(name), BO, mul)
    ts(full("S32"), BO, mk(4), A.mult, -512.0, A.mult)
    ts(full("SU"), BO, mk(2), A.mult, 1.0 / 2048, A.mult)
    ts(full("CE2"), ID, 2048.0, A.mult)
    for k in range(16):
        lin(ap("SELN", 128 * k, 128 * k + 128), full("CE2"), mk(k))
    asel(full("T01"), BO, A.is_gt, 0.0)
    asel(full("TR"), full("T01"), A.not_equal, -1.0)
    lin(ap("TR", 15, 128, 16), ap("BO", 0, 128, 16))
    lin(ap("WP", 1, 128, 16), ap("BO", 0, 128, 16), 0.0)
    lin(full("WN"), full("WP"), -1.0)
    ts(ap("CE", 0, 64), ct(ONE), K, A.mult, 2.0, A.is_lt)
    ts(ct(C0), ap("CE", 0, 64), 2040.0, A.mult, 8.0, A.add)
    ts(ap("CE", 64, 128), ap("CE", 0, 64), MAGIC * 16 * 255, A.mult, MAGIC * 16, A.add)
    ts(C4, K, 4.0, A.is_lt)
    lin(ct(MT), ap("CE", 64, 128), C4)
    ts(MSC, K, 2.0, A.is_ge, 1.0 / 16, A.max)
    ts(B1, K, 2.0, A.is_lt, 1279.53125, A.mult)
    ts(B2, K, 4.0, A.is_ge, -7.5, A.mult)
    ts(B3, K, 8.0, A.is_ge, -1280.0, A.mult)
    ts(MBI, B1, B2, A.add, B3, A.add)
    ts(coli(3), ap("KAI", 0, 1), 2208.0, A.add)
    ts(coli(4), coli(3), 2047, A.bitwise_and)
    ts(W1, coli(4), -1024.0, A.add, 16.0, A.mult)
    ts(K2, ap("KAI", 0, 1), -2048.0, A.add)
    lin(ap("BT", 0, 256), ap("JJ", 0, 256), 0.0)
    lin(ap("BT", 0, 128, 8), ap("BO", 0, 128, 8), W1)
    lin(ap("BT", 1, 128, 8), ap("BO", 0, 128, 8), -13152.0)
    for r, mul in ((2, K2), (3, 3232.0), (8, 25.0 / 2048)):
        lin(ap("BT", 128 + r, 256, 16), ap("BO", 0, 128, 16), mul)
    for name, bank, sign in (("AP", "P0", ID), ("AN", "P4", NID)):
        mm([(ap(bank, 128 + j, 256 + j), [(ap("BT", j, j + 128), sign)]) for j in (0, 128)])
        lin(ap(name, 0, 256), ap(bank, 128, 384))
    ts(TH, ap("THI", 0, 1), 16.0, A.mult, 4111.0, A.add)
    ts(ap("TB", 0, 192), ap("JJ", 0, 192), -128.0, A.add, 1.0 / 128, A.mult)
    ts(ap("BASE", 0, 144), ap("JJ", 0, 144), 16.0, A.mult, 2032.0, A.add)
    merges = [x for p in range(len(spans)) for x in pieces("F", p)]
    wide = 16 * max([t1 - t0 for t0, t1, e in merges if e != "r"] + [4])
    memset(ap("KEEP", 0, wide), 1.0)
    memset(ap("KEEP", 0, wide, 16), 0.0)
    memset(ap("RST", 0, wide), 0.0)
    memset(ap("RST", 0, wide, 16), 2 * BIG)
    ts(full("ZC"), full("JM"), 256.0, A.mult, -2048.0, A.add)
    for t0, t1, e in merges:
        if e != "r":
            memset(ap("ZC", t0, t1), 0.0)
    ramp = max([t1 - t0 for t0, t1, e in merges if e == "r"] + [16]) // 16
    iota(ap("RAMP", 0, 256 * ramp), [[0, ramp], [256, 16], [0, 16]], -2048, 0)
    ts(ap("RD", 0, 8 * SEG), ap("JP", 0, 8 * SEG), K, A.is_equal, -8.0, A.mult)
    ts(ap("RD", 0, 8 * SEG, SEG), ap("RD", 0, 8 * SEG, SEG), 3.0, A.add)
    ts(ap("RD", 64, 8 * SEG, SEG), ap("JP", 64, 8 * SEG, SEG), 0.0, A.mult, 8.0, A.add)
    ts(ap("RD", 65, 8 * SEG, SEG), ap("IOF", 0, 8), K, A.add, -1.0 / 2048, A.mult)
    for h in range(2):
        ts(ap("DD", 8 * SEG * h, 8 * SEG * (h + 1)), ap("JP", 0, 8 * SEG), 0.0, A.mult, 4.0, A.add)
    lin(ap("LE", 0, 256), ap("LEI", 0, 256))
    for j in range(0, 1024, 256):
        lin(ap("AD", j, j + 256), ap("ADI", j, j + 256), 1.0 / 2048)

    copy(ap("CF", 0, 8), ap("CBI", 0, 8))
    tt(full("CE"), ind(ap("CF", 0, 8), ap("LC", 0, 8)), full("M1"), A.mult)
    for s, h in enumerate(HALVES):
        reg, z = ap(PS[4 * s + 1], 256, 320), ap("ZB", 64 * h, 64 * h + 64)
        mm([(reg, [(ID, ct(C0)), (MH, ct(ONE)), (full("WN"), z), (ID, ct(MT)), (NID, ct(MT)), (full("WP"), z),
                   (sele(1), ap("CE", 64 * h, 64 * h + 64))])])
        lin(fld("ML", 0, 64 * h, 64 * h + 64, 1), reg, MSC, MBI)
    ts(coli(5), coli(1), 15442.0, A.mult, 3151.0, A.add)
    ts(coli(6), coli(5), 4095, A.bitwise_and)
    ts(VC, coli(6), -2048.0, A.add)
    lin(ap("WP", 1, 128, 16), ap("BO", 0, 128, 16), VC)
    lin(ap("WN", 1, 128, 16), ap("WP", 1, 128, 16), -1.0)

    VFW = ap("W", 0, 2048)

    def chain(m, p, X, Y, spare):
        last = m == STEPS
        t0, t1 = spans[p]
        n, h = t1 - t0, t0 // HALF
        before = sum([b - a for a, b in spans[:p]])
        vs = 2048 + 16 * (before - t0)
        al = 128 * h - 64 * h

        def my(name):
            return ap(name, t0, t1)

        def reg(bank, c):
            return ap(bank, c, c + n)
        if m > 1:
            add({"n": ("recv", (m - 1, p))}, [ap("TOK", 4 * m + p - 4, 4 * m + p - 3)],
                [blk("ML", m - 1, b) for b in range(t0 // 16, t1 // 16) if (b + m - 1) % NR], "arr%d_%d" % (m - 1, p))
        zh = my("ZB") if m == 1 else fld("ML", m - 1, t0, t1, 0)
        mh = fld("ML", m - 1, t0, t1, 1)
        mm2(reg(X, 0), [(ID, ap("CA", 0, n))],
            [(ap("AN", 0, 128), mh), (ap("AN", 128, 256), mh), (ID, ct(M15, n)), (NID, ct(M15, n)),
             (ap("AP", 0, 128), mh), (ap("AP", 128, 256), mh), (ID, ct(M5, n)), (NID, ct(M5, n))])()
        lin(my("A16"), reg(X, 0), 1.0 / 32)
        c16 = ap("C16", t0 // 16, t1 // 16)
        mm([(reg(Y, 0), [(ID, ap("BM", 0, n)), (full("SC"), mh)])])
        scan(ap("AL", al + t0, al + t1), ap("RST", 0, n), reg(Y, 0), A.max, A.min)
        if m == 1:
            lin(c16, ap("CBI", t0 // 16, t1 // 16))
            copy(my("SF"), ind(ap("LEI", 0, 256), c16))
        else:
            lin(c16, ap("AL", al + t0 + 15, al + t1, 16))
            lin(my("SF"), ind(ap("LE", 0, 256), c16))
        lin(my("S16"), my("SF"))
        for a, b in pieces("G", p):
            if m == 1:
                lin(ap("G", 16 * a, 16 * b), ind(ap("ADI", 0, 1024), ap("A16", a, b)), 1.0 / 2048)
            else:
                lin(ap("G", 16 * a, 16 * b), ind(ap("AD", 0, 1024), ap("A16", a, b)))
        for a, b in pieces("S", p):
            lin(ap("W", vs + 16 * a, vs + 16 * b), ind(VFW, ap("S16", a, b)))
        lanes(reg(X, 64), [(ap("SELN", 128 * k, 128 * k + 128), ap("G", 16 * t0 + k, 16 * t1, 16)) for k in range(16)],
              True)
        lin(my("N16"), reg(X, 64))
        lin(my("NF"), reg(X, 64))
        side = 0
        for a, b, e in pieces("D", p):
            if e != "a":
                tt(ap("D", 16 * a, 16 * b), ind(VFW, ap("N16", a, b)), ap("W", vs + 16 * a, vs + 16 * b), A.subtract)
                if e == "v":
                    act(ap("DA", 16 * a, 16 * b), ap("D", 16 * a, 16 * b), AF.Abs)
                else:
                    ts(ap("DA", 16 * a, 16 * b), ap("D", 16 * a, 16 * b), 0.0, A.max, 2.0, A.mult)
                continue
            act(ap("D", 16 * a, 16 * b), ind(VFW, ap("N16", a, b)), AF.Copy)
            for c0 in range(16 * a, 16 * b, 256):
                c1 = min(c0 + 256, 16 * b)
                pd = ap((X, spare)[side], 128, 128 + c1 - c0)
                side ^= 1
                mm([(pd, [(NID, ap("W", vs + c0, vs + c1)), (ID, ap("D", c0, c1))])])
                act(ap("DA", c0, c1), pd, AF.Abs)
        mm([(reg(Y, 64), [(full("POS"), ct(ONE, n)), (ID, ct(KT15, n))] + ([(full("S32"), mh)] if m > 1 else []))],
           True, False)
        halved = [x for x in pieces("D", p) if x[2] == "w"]
        if halved:
            a, b = halved[0][0], halved[-1][1]
            mm([(ap(Y, 64 + a - t0, 64 + b - t0),
                 [(ap("EN", 15 - k, 143 - k), ap("D", 16 * a + k, 16 * b, 16)) for k in range(16)])], False, False)
        lanes(reg(Y, 64), [(sele(k), ap("DA", 16 * t0 + k, 16 * t1, 16)) for k in range(16)], False)
        r1, r2 = reg(X, 384), reg(Y, 192)
        close1 = mm2(r1, [(ID, ap("BASE", before + 1, before + n + 1))], [(full("WK"), my("FL"))])
        ts(my("OK"), reg(Y, 64), TH, A.is_le)
        mm([(reg(Y, 128), [(full("TR"), my("OK"))])])
        close2 = mm2(r2, [(ID, ap("BASE", before, before + n)), (full("DK"), my("OK"))], [(full("N15"), my("FL"))])
        ts(my("FL"), reg(Y, 128), CMP, A.is_lt)
        close2()
        close1()
        tt(my("X1"), r2, my("NF"), A.max)
        tt(my("X2"), r1, my("X1"), A.max)
        lin(my("F16"), my("X2"))
        mn = t0 // 32 * 32
        closez = mm2(reg(X, 448), [(ID, zh), (ID, ct(QC, n))] +
                     [(ID, my("ZC"))] * ("r" in [x[2] for x in pieces("F", p)]),
                     [(MH, ap("MX", 16 * t0 + 15, 16 * t1, 16)), (MH, ap("MN", mn + 16 * t0 + 15, mn + 16 * t1, 16)),
                      (ID, ct(MG, n))])
        zo = my("Z16") if last else fld("MS", m - 1, t0, t1, 0)
        early = [] if last else ([(full("D4"), mh)] if m > 1 else []) + [(full("SQ4"), my("FL"))]
        closem = mm2(reg(Y, 256), [(ID, ct(C0, n)), (MH, ct(ONE, n))] + early,
                     [(full("WN"), zo), (ID, ct(MT, n)), (NID, ct(MT, n)), (full("WP"), zo)])
        for a, b, e in pieces("F", p):
            c0, c1 = 16 * a, 16 * b
            src = ind(ap("W", 0, vs + 16 * t1), ap("F16", a, b))
            if e == "r":
                tt(ap("FV", c0, c1), src, ap("RAMP", 0, c1 - c0), A.add)
                for c in range(c0, c1, 256):
                    scan(ap("MX", c + 1, c + 256, 2), ap("FV", c, c + 256, 2), ap("FV", c + 1, c + 256, 2),
                         A.max, A.max, -4096.0)
                    scan(ap("MN", mn + c + 269, mn + c + 14, -2), ap("FV", c + 255, c, -2),
                         ap("FV", c + 254, c - 1, -2), A.min, A.min, 4096.0)
                continue
            act(ap("FV", c0, c1), src, AF.Copy)
            scan(ap("MX", c0, c1), ap("KEEP", 0, c1 - c0), ap("FV", c0, c1), A.mult, A.max)
            scan(ap("MN", mn + c0, mn + c1), ap("RST", 0, c1 - c0), ap("FV", c0, c1), A.max, A.min)
        closez()
        act(zo, reg(X, 448), AF.Abs, MGN)
        closem()
        lin(fld("MS", m - 1, t0, t1, 1), reg(Y, 256), MSC, MBI)
        if not last:
            away = [blk("MS", m - 1, b) for b in range(t0 // 16, t1 // 16) if (b + m) % NR]
            add({"g": ("send", (m, p))}, away, [ap("TOK", 4 * m + p, 4 * m + p + 1)], "none")
            for b in range(t0 // 16, t1 // 16):
                if (b + m) % NR == 0:
                    lin(blk("ML", m, b), blk("MS", m - 1, b))

    def aside(m, s, mine, places):
        last, h = m == STEPS, HALVES[s]
        crow, arow, amask, old, lv = places[:5]

        def hs(name):
            return ap(name, HALF * h, HALF * h + HALF)

        def differ(key, row):
            for b in range(4):
                o = SEG * (8 * h + 4 * key + b)
                out, x = ap("DD", o, o + 16 * b + 16), ap(row[0], row[1], row[1] + 16 * b + 16)
                own = ap("AL", 128 * h + 64 * key + 16 * b + 15, 128 * h + 64 * key + 16 * b + 16)
                add({"a": k_act(out, x, AF.Abs, own, -1.0), "v": k_ts(out, x, own, A.not_equal)}, [x, own], [out])
        mm([(crow, [(full("SC"), fld("ML", m - 1, HALF * h, HALF * h + HALF, 1))])])
        differ(0, crow)
        mm([(ap(lv[0], lv[1], lv[1] + 64), [(ID, hs("SF")), (full("NEG"), ct(ONE)), (full("POS"), hs("OK"))]),
            (ap(lv[0], lv[1] + 64, lv[2]), [(ID, hs("NF")), (full("NEG"), hs("OK"))])])
        lin(ap("LV", 128 * h, 128 * h + 128), lv)
        if not last:
            for p, X, Y in mine:
                transp(ap("KT", spans[p][0], spans[p][1]), ap(Y, 64, 64 + spans[p][1] - spans[p][0]))
            scan(hs("KS"), ap("KEEP", 0, 64), hs("KT"), A.mult, A.max)
            tt(hs("IT"), ind(hs("KS"), ap("LB", 0, 4)), hs("KT"), A.is_equal)
            transp(hs("II"), hs("IT"))
            for p, X, Y in mine:
                a, b = spans[p]
                tt(ap("IA", a, b), ap(X, 0, b - a), ap("II", a, b), A.mult)
            mm([(amask, [(ID, ap("BM", 0, 64)), (full("B32"), hs("IA"))]), (arow, [(full("B32"), hs("IA"))])])
            scan(ap("AL", 128 * h + 64, 128 * h + 128), ap("RST", 0, 64), amask, A.max, A.min)
            differ(1, arow)
        for k0, k1 in ((0, 4),) if last else ((0, 4), (4, 8)) if OPT["apart"][s] else ((0, 8),):
            d0, d1 = SEG * (8 * h + k0), SEG * (8 * h + k1)
            lin(ap("DD", d0 + 65, d1, SEG), ap("AL", 128 * h + 16 * k0 + 15, 128 * h + 16 * k1, 16), -1.0 / 2048)
            scan(ap("RR", d0, d1), ap("RD", SEG * k0, SEG * k1), ap("DD", d0, d1), A.add, A.min)
            lin(ap("O16", 8 * h + k0, 8 * h + k1), ap("RR", d0 + 65, d1, SEG), -2048.0)
        if not last:
            was = ind(ap("AD", 0, 1088), ap("O16", 8 * h + 4, 8 * h + 8))
            if OPT["old"][s]:
                act(hs("OG"), was, AF.Copy)
                mm([(old, [(ID, hs("OG")), (NID, hs("II"))])])
                act(hs("T1"), old, AF.Copy)
            else:
                tt(hs("T1"), was, hs("II"), A.subtract)

    def writes(m, s, mine, places):
        last, h = m == STEPS, HALVES[s]
        name, masked = places[5:]
        t0, t1 = HALF * h, HALF * h + HALF
        tt(ind(ap("LE", 0, 320), ap("O16", 8 * h, 8 * h + 4)), ap("LV", 128 * h, 128 * h + 64),
           ap("LV", 128 * h + 64, 128 * h + 128), A.max)
        if not last:
            mm([(name, [(ID, ap("TB", t0, t1)), (ID, ap("II", t0, t1)), (full("SU"), fld("MS", m - 1, t0, t1, 1))])])
            lin(ap("T2", t0, t1), name)
            tt(ind(ap("AD", 0, 1088), ap("O16", 8 * h + 4, 8 * h + 8)), ap("T1", t0, t1), ap("T2", t0, t1), A.max)
        for j, (a, b) in enumerate([spans[p] for p, X, Y in mine] if last else [(t0, t1)]):
            reg = ap(masked[0], masked[1] + a - t0, masked[1] + b - t0)
            mm([(reg, [(ID, ap("BM", 0, b - a)), (ID, ap("TB", 128, 128 + b - a)),
                       (full("SU"), fld("MS", m - 1, a, b, 1))])])
            scan(ap("XS", a, b), ap("RST", 0, b - a), reg, A.max, A.min)
            lin(ap("W16", a // 16, b // 16), ap("XS", a + 15, b, 16), 2048.0)
            copy(ind(ap("W", 16 * a, 16 * b), ap("W16", a // 16, b // 16)),
                 ap("Z16", a, b) if last else fld("MS", m - 1, a, b, 0))
            if last:
                add({"sa"[(s + j) % 2]: ("store", ("yv", (16 * a, 16 * b), ap("W", 16 * a, 16 * b)))},
                    [ap("W", 16 * a, 16 * b)], [], "st_yv%d" % mine[j][0])

    for m in range(1, STEPS + 1):
        seen.clear()
        todo = []
        for s in range(2):
            B = PS[4 * s:4 * s + 4]
            p0 = s * len(PARTS[0])
            if len(PARTS[s]) == 1:
                mine, spare = [(p0, B[0], B[1])], B[3]
                places = [ap(B[2], c, c + n) for c, n in ((128, 64), (192, 64), (256, 64), (320, 64), (384, 128),
                                                          (0, 64), (64, 64))]
            else:
                mine, spare = [(p0, B[0], B[1]), (p0 + 1, B[2], B[3])], None
                places = [ap(B[0], c, c + 64) for c in (128, 192, 256, 320)] + \
                    [ap(B[1], 320, 448), ap(B[1], 448, 512), ap(B[1], 0, 64)]
            for p, X, Y in mine:
                cur[:] = ["abcd"[p], len(spans) - 1 - p, m]
                chain(m, p, X, Y, spare or X)
            cur[:] = ["<>"[s], 0, m]
            aside(m, s, mine, places)
            todo.append((m, s, mine, places))
        for x in todo:
            cur[0] = "<>"[x[1]]
            writes(*x)

    add({"s": ("store", ("yl", None, ap("LE", 0, 256)))}, [ap("LE", 0, 256)], [], "st_yl")
    add({"s": ("store", ("yz", None, full("Z16")))}, [full("Z16")], [], "st_yz")
    return ops


def dependencies(ops):
    acc = {}
    deps = []
    for i, o in enumerate(ops):
        d = set()
        rd, wr = {}, {}
        for x in o["r"]:
            rd[x[0]] = rd.get(x[0], 0) | bits(x)
        for x in o["w"]:
            wr[x[0]] = wr.get(x[0], 0) | bits(x)
        for n in set(rd) | set(wr):
            r, w = rd.get(n, 0), wr.get(n, 0)
            keep = []
            for j, jr, jw in acc.get(n, []):
                if (jw & (r | w)) or (jr & w):
                    d.add(j)
                jr &= ~w
                jw &= ~w
                if jr or jw:
                    keep.append((j, jr, jw))
            keep.append((i, r, w))
            acc[n] = keep
        deps.append(sorted(d))
    return deps


def cost(o, e, c):
    k, a = o["alt"][e]
    if k == "send":
        return c["send"]
    if k in ("load", "store", "recv"):
        return 50.0
    if k == "mm":
        return sum([max(64, cnt(x[2])) for x in a]) * c["pe"]
    n = cnt(o["w"][0])
    if e == "g":
        return (170 + 2 * n) * c["cy"]
    if o["w"][0][4] is not None:
        return (60 + n * c["sc"]) * c["cy"]
    if [x for x in o["r"] if x[4] is not None]:
        return ((60 if e == "v" else 78) + n * c["ga"]) * c["cy"]
    if e == "v":
        if k == "tt":
            n *= 1 if [x for x in o["r"] if x[0] in PS] else 2
        elif all([x[0] in _S and _S[x[0]][0] in (BF, F16, U16) for x in o["r"] + o["w"] if cnt(x) > 1]):
            n /= 2
    return max(64, n) * c["cy"] + c["call" + e]


def lags(ops, c):
    late, ahead = [0.0] * len(ops), 0.0
    for i, o in enumerate(ops):
        k, a = list(o["alt"].values())[0]
        if k == "send":
            late[i] = c["way"]
        elif k in ("load", "store"):
            x = a[0] if k == "load" else a[2]
            t = 128 * cnt(x) * (4 if _S[x[0]][0] in (F32, I32) else 2) / c["bw"]
            ahead = ahead + t if k == "load" else t
            late[i] = c["dma"] + ahead
    return late


def waits_for(ops, deps, i, e, eng):
    return [j for j in deps[i] if not (e == "p" and eng[j] == "p") and "load" != ops[i]["alt"][e][0]]


def plan(ops, c):
    deps = dependencies(ops)
    n = len(ops)
    costs = [{e: cost(o, e, c) for e in o["alt"]} for o in ops]
    late = lags(ops, c)
    succ = [[] for _ in ops]
    for i in range(n):
        for j in deps[i]:
            succ[j].append(i)
    togo = [0.0] * n
    for i in range(n - 1, -1, -1):
        togo[i] = min(costs[i].values()) + late[i] + max(
            [togo[j] + c["same" if set(costs[i]) & set(costs[j]) else "hop"] for j in succ[i]] + [0.0])
    rank = [togo[i] + c["lead"] * o["lead"] for i, o in enumerate(ops)]
    banks = [set([x[0] for x in o["r"] + o["w"] if x[0] in PS]) for o in ops]
    left = [len(d) for d in deps]
    ready = [i for i in range(n) if not left[i]]
    free, fin, eng, used, order, waits = {}, [0.0] * n, [None] * n, {}, [], [None] * n
    while ready:
        cand = []
        for i in ready:
            best = None
            for e, t in costs[i].items():
                w = waits_for(ops, deps, i, e, eng)
                w += [j for b in banks[i] for x, j in used.get(b, {}).items() if x != e]
                at = max([free.get(e, 0.0)] + [fin[j] + c["same" if eng[j] == e else "hop"] for j in w])
                end = at + t + (c["spare"] * t + c["plus"] if e == "v" else 0.0)
                if best is None or end < best[4]:
                    best = (at, t, e, w, end)
            cand.append((i,) + best[:4])
        soon = min([x[1] for x in cand]) + c["look"]
        pick = max([x for x in cand if x[1] <= soon], key=lambda x: (rank[x[0]], -x[0]))
        fill = [x for x in cand if x[3] == pick[3] and x[1] + x[2] <= pick[1] + c["slip"] and x is not pick]
        i, at, t, e, w = max(fill, key=lambda x: (rank[x[0]], -x[0])) if fill else pick
        ready.remove(i)
        order.append(i)
        eng[i], waits[i], free[e], fin[i] = e, sorted(set(w)), at + t, at + t + late[i]
        for b in banks[i]:
            used.setdefault(b, {})[e] = i
        for j in succ[i]:
            left[j] -= 1
            if not left[j]:
                ready.append(j)
    return order, eng, waits


def routes(T, topo, m, p):
    out = []
    t0, t1 = parts()[p]
    for r in range(NR):
        src, mine, turn = T.cores[r], [], p
        for b in range(t0 // 16, t1 // 16):
            if (b + m) % NR == 0:
                continue
            dst = T.cores[(r + b + m) % NR]
            via = None
            if not topo.may_write(src, dst):
                able = [c for c in topo.cores_of(src) if c != src and T.rank_of(c) is None and topo.may_write(c, dst)
                        and topo.die(c) == topo.die(src)]
                via = able[turn % len(able)]
                turn += 1
            mine.append((b, dst, via))
        out.append(mine)
    return out


def engine_masks(topo, src, mine):
    direct = [x for x in mine if x[2] is None]
    relay = [x for x in mine if x[2] is not None]
    off = topo.engines(src, direct[0][1]) if direct else []
    on = [e for e in topo.engines(src, relay[0][2]) if e not in off]
    res = {}
    for group, eng in ((direct, off), (relay, on)):
        for i, x in enumerate(group):
            k = len(eng) // len(group)
            res[x[0]] = eng[i * k:(i + 1) * k]
    return res


def as_mask(eng):
    return sum([1 << e for e in eng])


def arrivals(T, topo, m, p, core):
    total = 0
    for r, mine in enumerate(routes(T, topo, m, p)):
        em = engine_masks(topo, T.cores[r], mine)
        for b, dst, via in mine:
            if dst == core:
                total += len(em[b]) if via is None else len(topo.engines(via, dst))
    return total


def relay_program(g, core, T, topo):
    sent = 0
    for m in range(1, STEPS):
        for p in range(len(parts())):
            for r, mine in enumerate(routes(T, topo, m, p)):
                for b, dst, via in mine:
                    if via == core:
                        sem = T.sem["arr%d_%d" % (m, p)]
                        g.wait_ge(sem, len(engine_masks(topo, T.cores[r], mine)[b]))
                        blk = T["ML"][:, m * SLOT + b * BLK:m * SLOT + b * BLK + BLK]
                        rid, pid = topo.addr(dst, core)
                        g.remote_dma(blk, blk, sem, T.sem["sent"], pid, rid, topo.mask(core, dst))
                        sent += len(topo.engines(core, dst))
    if sent:
        g.wait_ge(T.sem["sent"], sent)


_CACHE = {}


def rank_program(g, core, T, topo):
    rank = T.rank_of(core)
    if rank is None:
        relay_program(g, core, T, topo)
        return
    if "plan" not in _CACHE:
        ops = build_ops()
        _CACHE["plan"] = (ops,) + plan(ops, PLAN)
    ops, order, eng, deps = _CACHE["plan"]
    Q = {"v": g.vector, "a": g.scalar, "p": g.tensor, "g": g, "s": g.sync}

    def P(x):
        if not isinstance(x, tuple):
            return x
        if x[4] is not None:
            return T[x[0]][:, x[1]:x[2]].indirect(P(x[4]))
        if x[3] == 1:
            return T[x[0]][:, x[1]:x[2]]
        return T[x[0]][:, x[1]:(x[2] if x[2] >= 0 else None):x[3]]

    count = {"v": 0, "a": 0, "p": 0, "g": 0}
    known = {"v": {}, "a": {}, "p": {}, "g": {}, "s": {}}
    done = {}
    sent = 0
    own = []
    for i in order:
        o, e = ops[i], eng[i]
        k, a = o["alt"][e]
        if k == "recv":
            done[i] = (o["sem"], arrivals(T, topo, a[0], a[1], core), {})
            continue
        q, kn = Q[e], known[e]
        need = {}
        for j in deps[i]:
            if done[j][0] != "none":
                need[done[j][0]] = max(need.get(done[j][0], (0, 0)), (done[j][1], j))
        for s in sorted(need, key=lambda s: -need[s][1]):
            v, j = need[s]
            if kn.get(s, 0) < v:
                q.wait_ge(T.sem[s], v)
                kn[s] = v
                for s2, v2 in done[j][2].items():
                    if kn.get(s2, 0) < v2:
                        kn[s2] = v2
        if k == "load" or k == "store":
            if k == "load":
                ins = q.dma_start(P(a[0]), T[a[1]][:])
            else:
                ins = q.dma_start(T[a[0]][:] if a[1] is None else T[a[0]][:, a[1][0]:a[1][1]], P(a[2]))
            ins.then_inc(T.sem[o["sem"]], 16)
            done[i] = (o["sem"], 16, dict(kn))
            own.append(o["sem"])
            continue
        if k == "send":
            m, p = a
            mine = routes(T, topo, m, p)[rank]
            em = engine_masks(topo, core, mine)
            trs = {True: [], False: []}
            for b, dst, via in mine:
                rid, pid = topo.addr(dst if via is None else via, core)
                trs[via is None].append(RemoteDMATransfer(
                    dst_ids=[DstId(rid=rid, pnc=pid)], dma_engine_mask=as_mask(em[b]),
                    remote_sem=T.sem["arr%d_%d" % (m, p)],
                    src=T["MS"][:, (m - 1) * SLOT + b * BLK:(m - 1) * SLOT + b * BLK + BLK],
                    dst=T["ML"][:, m * SLOT + b * BLK:m * SLOT + b * BLK + BLK]))
                sent += len(em[b])
            g.remote_dma_fused(trs[False] + trs[True], local_sem=T.sem["sent"])
            done[i] = ("none", 0, {})
            continue
        if k == "mm":
            for x in a:
                q.matmul(P(x[0]), P(x[1]), P(x[2]), x[3], x[4]).then_inc(T.sem[CNT[e]], 1)
            count[e] += len(a)
            done[i] = (CNT[e], count[e], dict(kn))
            continue
        if k == "copy":
            ins = q.tensor_copy(P(a[0]), P(a[1]))
        elif k == "tt":
            ins = q.tensor_tensor(P(a[0]), P(a[1]), P(a[2]), a[3])
        elif k == "ts":
            if a[5] is None:
                ins = q.tensor_scalar(P(a[0]), P(a[1]), P(a[2]), None, a[4])
            else:
                ins = q.tensor_scalar(P(a[0]), P(a[1]), P(a[2]), P(a[3]), a[4], a[5])
        elif k == "scan":
            ins = q.tensor_tensor_scan(P(a[0]), P(a[1]), P(a[2]), a[3], a[4], a[5])
        elif k == "tr":
            ins = q.transpose(P(a[0]), P(a[1]))
        elif k == "memset":
            ins = q.memset(P(a[0]), a[1])
        elif k == "asel":
            ins = q.affine_select(P(a[0]), P(a[1]), [[1, 128]], a[2], a[3], 0, -1)
        elif k == "iota":
            if _S[a[0][0]][0] == I32:
                ins = q.iota(P(a[0]), a[1], a[2], a[3])
            else:
                ins = q.iota(P(a[0]), a[1], a[2], a[3], allow_small_or_imprecise_dtypes=True)
        else:
            kw = {}
            if a[3] is not None:
                kw["bias"] = P(a[3])
            if a[4] is not None:
                kw["scale"] = P(a[4])
            ins = q.activation(P(a[0]), P(a[1]), a[2], **kw)
        ins.then_inc(T.sem[CNT[e]], 1)
        count[e] += 1
        done[i] = (CNT[e], count[e], dict(kn))
    for e in count:
        g.wait_ge(T.sem[CNT[e]], count[e])
    g.wait_ge(T.sem["sent"], sent)
    for s in own:
        g.wait_ge(T.sem[s], 16)
